import numpy as np, ml_dtypes
CORES = [9,25,41,57]
N = 4
BF = ml_dtypes.bfloat16
def gentries(a):
    return np.ascontiguousarray(a.reshape(8, 16, -1).transpose(0, 2, 1)).reshape(8, -1)
def gtable(e):
    e = np.asarray(e); return np.ascontiguousarray(e.reshape(8, -1, 16).transpose(0, 2, 1)).reshape(128, -1).astype(np.int32)
L, LB, HB, J, CAP, M, S, RO = 1024, 10, 12, 3072, 896, 128, 64, 3
H, W, T, TOP = N * L, 2 * L, 2 ** (20 - HB), 2 ** 20 - 1
def shelf(rng, n, full):
    a = np.arange(H).reshape(N, 1, 1, L); b = np.roll(a, 1, axis=0); m = n.reshape(1, 8, 1, 1)
    e = rng.integers(0, T >> 4, (N, 8, 16, W)) + (T >> 4) * np.arange(16).reshape(1, 1, 16, 1)
    k = np.concatenate([a + H * np.where(a < m, e[..., :L] & -2, e[..., :L]), b + H * (e[..., L:] | 1)], axis=3)
    k = np.take_along_axis(k, np.argsort(rng.random(k.shape), axis=2), 2)
    c = np.where(rng.random((N, 8, 1, W)) < full, 16, rng.integers(0, 17, (N, 8, 1, W)))
    k = np.where(np.argsort(rng.random(k.shape), axis=2) < c, k, -1)
    k[..., L:] = np.where(b < m, k[..., L:], -1)
    return k
def lack(rng, k, t, c, n):
    c = np.asarray(c); lo = c < L; a = np.where(lo, t * L + c, ((t - 1) % N) * L + c - L)
    e = rng.integers(0, T, c.shape); e = np.where(lo, np.where(a < n, e & -2, e), e | 1)
    x = a[:, None] + H * ((e[:, None] + 2 * np.arange(17)) % T)
    ok = ~np.any(x[:, :, None] == k[:, c].T[:, None, :], axis=2)
    return x[np.arange(c.size), np.argmax(ok, axis=1)]
def stored(rng, k, shape):
    s = k[k >= 0]
    return s[rng.integers(0, s.size, shape)] if s.size else rng.integers(0, 2 ** 20, shape)
def lanes(rng, k, n, w, miss):
    key = np.zeros((N, 8, J), np.int64)
    for g in range(8):
        u = np.add.accumulate(w[:, g], axis=1)
        t = np.minimum(np.sum(rng.random((N, J, 1)) * u[:, None, -1:] >= u[:, None, :], axis=2), N - 1)
        for d in range(N):
            at = t == d; z = int(np.sum(at)); v = stored(rng, k[d, g], z); m = rng.random(z) < miss[g]
            c = rng.integers(0, L, z); c = np.where((rng.random(z) < 0.5) & (((d - 1) % N) * L + c < n[g]), c + L, c)
            v[m] = lack(rng, k[d, g], d, c[m], n[g]); key[:, g][at] = v
    return key
def draws(rng, k, n, w, miss):
    return np.stack([lanes(rng, k, n, w, miss) for _ in range(RO)], axis=2)
def pays(rng, k, miss):
    p = rng.integers(0, 2 ** 20, k.shape)
    for g in range(8):
        p[:, g] = np.where(rng.random(p[:, g].shape) < miss[g], p[:, g], stored(rng, k[:, g], p[:, g].shape))
    return p
def images(rng, n):
    m = n.reshape(1, 8, 1); z = rng.integers(0, 4, (N, 8, J))
    return np.where(z == 0, 0, np.where(z == 1, m, np.minimum((rng.random((N, 8, J)) * (m + 1)).astype(np.int64), m)))
def pack(k, p, n, key, img, dr):
    return {"tk": np.ascontiguousarray(k.reshape(N, 128, W)).astype(np.int32), "tp": np.ascontiguousarray(p.reshape(N, 128, W)).astype(np.int32),
            "pn": np.tile(np.repeat(n, 16).reshape(1, 128, 1), (N, 1, 1)).astype(np.int32), "lk": np.stack([gtable(a) for a in key]),
            "li": np.stack([gtable(a) for a in img]), "dk": np.stack([gtable(a.reshape(8, -1)) for a in dr])}
def setup_inputs(rng):
    n = rng.permutation(8) * (H >> 3) + rng.integers(1, H >> 3, 8)
    miss = rng.permutation(np.array([0.01, 0.01, 0.02, 0.04, 0.1, 0.2, 0.3, 0.4])); full = rng.choice(np.array([0.2, 0.4, 0.6]), (1, 8, 1, 1))
    k = shelf(rng, n, full); w = np.exp2(rng.integers(-1, 2, (N, 8, N)))
    return pack(k, pays(rng, k, miss), n, lanes(rng, k, n, w, miss), images(rng, n), draws(rng, k, n, w, miss))
def setup_inputs_spread(rng):
    n = np.minimum((H * rng.random(8) ** 2).astype(np.int64), H); k = shelf(rng, n, 0.4); b = (N, 8, 1, W)
    wild = rng.integers(0, 2 ** 16, k.shape) + 65536 * ((np.arange(16).reshape(1, 1, 16, 1) + rng.integers(0, 16, b)) % 16)
    wild = np.where(rng.random(k.shape) < rng.random(b) * 1.3, wild, -1)
    k = np.where(rng.random(b) < 0.4, wild, k); miss = rng.choice(np.array([0.01, 0.05, 0.2]), 8); w = np.exp2(rng.integers(-3, 4, (N, 8, N)))
    p = np.where(rng.random(k.shape) < 0.4, np.minimum(np.exp2(20 * rng.random(k.shape)).astype(np.int64), TOP), pays(rng, k, miss))
    key = np.where(rng.random((N, 8, J)) < 0.2, np.minimum(np.exp2(20 * rng.random((N, 8, J))).astype(np.int64), TOP), lanes(rng, k, n, w, miss))
    return pack(k, p, n, key, images(rng, n), draws(rng, k, n, w, miss))
def setup_inputs_ends(rng):
    n = np.concatenate([rng.permutation(np.array([0, 0, H, H, H, H - 1, H >> 1])), np.array([0])])
    k = shelf(rng, n, 1.0); b = (N, 8, 1, W); x = np.arange(16)
    one = rng.integers(0, 32, b) == x.reshape(1, 1, 16, 1)
    k = np.where(rng.random(b) < 0.68, np.where(one, TOP, -1), k)
    for g in range(8):
        k[0, g, :, 0] = H * (x + 1); k[N - 1, g, :, L - 1] = TOP - H * (x + 1); k[0, g, :, W - 1] = TOP - 2 * H * (x + 1)
        if g % 2 == 1: k[0, g, 15, 0] = 0; k[N - 1, g, 15, L - 1] = TOP; k[0, g, 15, W - 1] = TOP
    q = rng.random(b); p = TOP * np.where(q < 0.3, 1, np.where(q > 0.8, 0, rng.integers(0, 2, k.shape)))
    p[..., W - 1] = TOP; p[..., 2] = TOP; p[..., 5] = 0
    p[N - 1, 1::2, 15, L - 1] = TOP; p[N - 1, 1::2, 0, L - 1] = 0
    w = np.ones((N, 8, N)); miss = np.full(8, 0.7)
    def mix(v):
        z = rng.random(v.shape); return np.where(z < 0.34, 0, np.where(z < 0.68, TOP, v))
    img = np.where(rng.random((N, 8, J)) < 0.5, 0, n.reshape(1, 8, 1))
    return pack(k, p, n, mix(lanes(rng, k, n, w, miss)), img, mix(draws(rng, k, n, w, miss)))
def setup_inputs_corners(rng):
    n = rng.permutation(np.array([0, 1, L - 1, L, H - S, H - 1, H, (N - 1) * L - (S >> 1)])); k = shelf(rng, n, 0.5)
    miss = np.full(8, 0.04); w = np.exp2(rng.integers(-1, 2, (N, 8, N))); p = pays(rng, k, miss)
    key = lanes(rng, k, n, w, miss); img = images(rng, n); dr = draws(rng, k, n, w, miss)
    kind = rng.permutation(np.array([0, 0, 0, 1, 1, 1, 2, 2])); nth = [0, 0, 0]
    for g in range(8):
        i = nth[kind[g]]; nth[kind[g]] += 1
        if kind[g] == 0:
            for q in range(N):
                t = (q + 1) % N; x = int(rng.choice(np.array([0, 1, CAP - 1, CAP, CAP + 1, J])))
                if q == 0: x = (CAP, CAP + 1, CAP - 1)[i]
                to = rng.permutation(np.concatenate([np.full(x, t), (t + 1 + rng.integers(0, N - 1, J - x)) % N])); c = rng.integers(0, L, J)
                v = k[to, g, rng.integers(0, 16, J), c]; v = np.where(v < 0, to * L + c + H * rng.integers(0, T, J), v)
                key[q, g] = v; img[q, g] = np.where(((v >> HB) & 1) == 1, 0, img[q, g])
        elif kind[g] == 1:
            img[:, g] = n[g]; to = np.stack([rng.permutation(np.arange(J) % N) for _ in range(N)]); tot = S + i - 1
            for t in range(N):
                qi, ji = np.nonzero(to == t); v = stored(rng, k[t, g], qi.size); x = (M - 1, M, M + 1)[(t + i) % 3]
                f = rng.permutation(np.flatnonzero(np.all(k[t, g, :, :L] >= 0, axis=0))); c = rng.permutation(np.flatnonzero(np.any(k[t, g, :, :L] < 0, axis=0)))[:x]
                y = tot // N + (tot % N if t == N - 1 else 0); c[rng.permutation(M - 1)[:y]] = f[:y]
                if x > M: c[M] = f[y]
                v[np.sort(rng.permutation(qi.size)[:x])] = lack(rng, k[t, g], t, c, n[g]); key[qi, g, ji] = v
        else:
            a = key[:, g] & (H - 1); z = rng.integers(0, 5, a.shape); m = n[g]
            img[:, g] = np.where(z == 0, 0, np.where(z == 1, m, np.where(z == 2, np.minimum(a, m), np.where(z == 3, np.minimum(a + 1, m), max(int(m) - 1, 0)))))
    return pack(k, p, n, key, img, dr)
def setup_inputs_crowd(rng):
    kd = rng.permutation(8); n = np.concatenate([rng.integers(1, H, 4), np.array([0, 0, H, H >> 1])])[kd]
    k = shelf(rng, n, np.where(kd >= 4, 1.0, 0.5).reshape(1, 8, 1, 1)); miss = np.full(8, 0.1); w = np.ones((N, 8, N)); p = pays(rng, k, miss)
    key = lanes(rng, k, n, w, miss); img = images(rng, n); dr = draws(rng, k, n, w, miss); x = np.arange(16)
    for g in range(8):
        q1, j1 = int(rng.integers(0, N)), int(rng.integers(0, J)); keep = key[q1, g, j1]
        if kd[g] < 4:
            t, c = int(rng.integers(0, N)), int(rng.integers(0, L))
            if kd[g] == 3: t, c = N - 1, L - 1
            a = t * L + c; k[t, g, :, c] = rng.permutation(a + 2 * H * x); other = a + 2 * H * rng.integers(16, T >> 1, (N, J))
            if kd[g] == 0: key[:, g] = k[t, g, 15, c]; p[t, g, 15, c] = k[t, g, 3, c]; p[t, g, 3, c] = other[0, 0]
            elif kd[g] == 2: key[:, g] = other; dr[:, g, 0] = other[:, ::-1]
            else: k[t, g, 15, c] = -1; key[:, g] = a + 32 * H; dr[:, g, 0] = other
            if kd[g] == 3: key[q1, g, j1] = keep
        elif kd[g] < 6:
            if kd[g] == 4:
                for c in (0, S - 1, RO * S - 1): k[0, g, :, c] = c + H * (2 * rng.permutation(16) + 1)
            for t in range(N):
                cols = RO * S + rng.permutation(L - RO * S); sp = cols[-RO:]; cols = cols[:-RO]
                if kd[g] == 5: k[t, g, rng.integers(0, 16, RO), sp] = -1
                for rnd in range(RO + 1):
                    c = np.roll(cols, 7 * rnd)[np.arange(J // N) % cols.size]
                    if kd[g] == 5 and rnd < RO: c[5] = sp[rnd]
                    for q in range(N):
                        v = lack(rng, k[t, g], t, c, 0)
                        if rnd == 0: key[q, g, t::N] = v
                        else: dr[q, g, rnd - 1, t::N] = v
        else:
            t = 0 if kd[g] == 6 else 1; cols = L + rng.integers(0, L, 3)
            if kd[g] == 6: cols[0] = W - 1
            v = np.concatenate([stored(rng, k[t, g][:, cols], 4), lack(rng, k[t, g], t, cols, n[g])])
            img[:, g] = 0; key[:, g] = v[rng.integers(0, v.size, (N, J))]; dr[:, g, 0] = v[rng.integers(0, v.size, (N, J))]
            if kd[g] == 6: k[N - 1, g, 0, cols[2] - L] = v[-1]
            if kd[g] == 7:
                low = rng.random((N, J)) < 0.5
                key[:, g] = np.where(low, stored(rng, k[t, g][:, :L], (N, J)), key[:, g])
                key[q1, g, J - 1] = keep; img[q1, g, J - 1] = n[g]
                j = int(np.flatnonzero(~low[N - 1])[CAP - 1]); z, y = int(k[t, g, 15, cols[0]]), int(k[t, g, 0, cols[0]])
                key[N - 1, g, j] = z; dr[N - 1, g, 0, j] = y; p[t, g, 15, cols[0]] = z; p[t, g, 0, cols[0]] = y
    return pack(k, p, n, key, img, dr)
def setup_inputs_calm(rng):
    v = rng.permutation(np.array([0, 1, 2, 3, 0, 1, 2, 3])); n = np.where(rng.random(8) < 0.5, L * rng.integers(1, N, 8) - 2, rng.integers(16, H - 32, 8))
    few = np.concatenate([np.flatnonzero(v == 0), np.flatnonzero(v == 1)[:1]]); n[few] = np.array([0, 3, 0]); n[np.flatnonzero(v == 3)[0]] = L * int(rng.integers(1, N)) - 2
    k = shelf(rng, n, 0.5)
    for g in few:
        for x in range(3):
            if x < n[g]: k[1, g, :, L + x] = x + H * (2 * rng.permutation(16) + 1)
            else: k[0, g, :, x] = x + H * rng.permutation(16)
    none = np.zeros(8); w = np.ones((N, 8, N)); p = pays(rng, k, none); key = lanes(rng, k, n, w, none); dr = draws(rng, k, n, w, none)
    img = np.where(rng.random((N, 8, J)) < 0.5, np.maximum(n.reshape(1, 8, 1) - rng.integers(0, 4, (N, 8, J)), 0), images(rng, n))
    for g in range(8):
        s = k[:, g][k[:, g] >= 0]; s = s[np.abs((s & (H - 1)) - n[g] - 3) < 9]
        if s.size:
            for a in (p, key): a[:, g] = np.where(rng.random(a[:, g].shape) < 0.15, s[rng.integers(0, s.size, a[:, g].shape)], a[:, g])
        for i in range(int(v[g])):
            t = (i + 1) % N; f = np.flatnonzero(np.all(k[t, g, :, :L] >= 0, axis=0)); f = rng.permutation(f[np.abs(t * L + f - n[g] - 4) > 12])[:RO + 1]
            u = lack(rng, k[t, g], t, f, n[g]); key[i, g, 0] = u[0]; dr[i, g, :, 0] = u[1:]
    for g in few:
        for x in range(3):
            key[:, g, 2 + x] = x + H; p[:, g] = np.where(k[:, g] == x + H, x + H, p[:, g])
    return pack(k, p, n, key, img, dr)
def check_inputs(d):
    bad = []
    for a, lo, hi in (("tk", -1, TOP), ("tp", 0, TOP), ("pn", 0, H), ("lk", 0, TOP), ("li", 0, H), ("dk", 0, TOP)):
        if np.min(d[a]) < lo or np.max(d[a]) > hi: bad.append("range of " + a)
    s = np.sort(d["tk"].reshape(N, 8, 16, W), axis=2)
    if np.any((s[:, :, 1:] == s[:, :, :-1]) & (s[:, :, 1:] >= 0)): bad.append("tk: keys of one bucket differ")
    m = d["pn"].reshape(N, 8, 16)
    if np.any(m != m[:1, :, :1]): bad.append("pn: alike in a group and on all ranks")
    if np.any(d["li"].reshape(N, 8, -1) > m[:, :, :1]): bad.append("li: at most the pointer")
    return bad
def reference(tk, tp, pn, lk, li, dk):
    k = tk.astype(np.int64).reshape(N, 8, 16, W); p = tp.astype(np.int64).reshape(N, 8, 16, W); n = pn[0].astype(np.int64).reshape(8, 16)[:, 0]
    key = np.stack([gentries(a) for a in lk]).astype(np.int64); img = np.stack([gentries(a) for a in li]).astype(np.int64)
    dr = np.stack([gentries(a) for a in dk]).astype(np.int64).reshape(N, 8, RO, J)
    src = np.arange(N).reshape(N, 1, 1); grp = np.arange(8).reshape(1, 8, 1)
    for rnd in range(RO):
        home = key & (H - 1); bit = ((key >> HB) & 1) == 1
        old = bit & (home < img); new = bit & (home < n.reshape(1, 8, 1)); fwd = new & ~old
        to = ((home >> LB) + old) % N
        own = ((home >> LB) + new) % N; col = (home & (L - 1)) + L * new
        place = np.zeros_like(key)
        for d in range(N):
            m = (to == d).astype(np.int64); place = place + m * (np.add.accumulate(m, axis=2) - m)
        go = place < CAP
        eq = k[own, grp, :, col] == key[..., None]; hit = np.any(eq, axis=3)
        val = np.sum(np.where(eq, p[own, grp, :, col], 0), axis=3)
        order = fwd * (N * CAP) + src * CAP + place; miss = go & ~hit; over = np.zeros(8, np.int64)
        for t in range(N):
            for g in range(8):
                m = miss[:, g] & (own[:, g] == t)
                o = np.argsort(order[:, g][m])[:M]; ks = key[:, g][m][o]
                c, first = np.unique(col[:, g][m][o], return_index=True); ks = ks[first]
                e = k[t, g][:, c] == -1; room = np.any(e, axis=0); s = np.argmax(e, axis=0)
                over[g] += np.sum(~room)
                s, c, ks = s[room], c[room], ks[room]
                k[t, g, s, c] = ks; p[t, g, s, c] = (ks & 1023) * 1024 + (ks >> 10)
        key = np.where(go, np.where(hit, val, dr[:, :, rnd]), key); img = np.where(go & fwd, home + 1, img)
        nn = np.minimum(n + np.minimum(over, S), H)
        for g in range(8):
            x = np.arange(n[g], nn[g]); t = x >> LB; c = x & (L - 1); t2 = (t + 1) % N
            kl = k[t, g, :, c]; pl = p[t, g, :, c]; mv = (kl >= 0) & (((kl >> HB) & 1) == 1)
            k[t2, g, :, L + c] = np.where(mv, kl, -1); p[t2, g, :, L + c] = np.where(mv, pl, 0)
            k[t, g, :, c] = np.where(mv, -1, kl); p[t, g, :, c] = np.where(mv, 0, pl)
        n = nn
    return {"yk": k.reshape(N, 128, W).astype(np.float32), "ys": np.sum(p, axis=2).astype(np.float32), "yn": np.tile(np.repeat(n, 16).reshape(1, 128, 1), (N, 1, 1)).astype(np.float32),
            "yl": np.stack([gtable(a) for a in key]).astype(np.float32), "yi": np.stack([gtable(a) for a in img]).astype(np.float32)}

@@ -1,0 +1,826 @@
+from concourse.bass import DstId, RemoteDMATransfer
+from concourse.mybir import dt, AluOpType, AxisListType, ActivationFunctionType
+
+A = AluOpType
+AF = ActivationFunctionType
+N, J, CAP, RO = 4, 3072, 896, 3
+WT = 8704
+WM = 2176
+DH = 272
+WAKE = 0.08
+F, B, I, U, H = "float32", "bfloat16", "int32", "uint16", "float16"
+
+
+def sb(n, d=F):
+    return ("sbuf", [128, n], d)
+
+
+SCRATCH = {
+    "K": sb(WT), "P": sb(WT), "MK": sb(WM), "MS": sb(WM), "SI": sb(4096, I),
+    "VAL": sb(3072), "EQ": sb(3072), "KB": sb(3072), "KR": sb(1536),
+    "LS": sb(288, I), "DS": sb(432, I), "LK": sb(384, I), "DK": sb(576, I), "D1": sb(576),
+    "SBb": sb(2048, B), "SBh": sb(2048, H), "SRf": sb(2048), "SRb": sb(2048, B),
+    "IO": sb(128), "A16": sb(128), "B16": sb(128), "B32": sb(128), "UV": sb(384), "KP": sb(512), "PI": sb(16, I),
+    "C": sb(128), "ONb": sb(128, B), "ONf": sb(128), "UP": sb(128, B), "IDb": sb(128, B), "UA": sb(128, B),
+    "UB": sb(128, B), "FE": sb(128, B), "Rb": sb(512, B), "Rf": sb(512), "Ff": sb(128), "DG": sb(128),
+    "RS": sb(128), "THR": sb(128), "RG": sb(768, B), "TR": sb(24), "TL": sb(32), "JL": sb(8),
+    "TK": sb(128), "WCs": sb(128), "t1": sb(128), "t2": sb(128), "t3": sb(128),
+    "KEY": sb(192), "NN": sb(8), "k4": sb(192, I), "hb": sb(192, I), "home": sb(192, I),
+    "t0": sb(192, I), "cb0": sb(192), "tob": sb(192, B), "M": sb(1536, B), "S": sb(768, B), "WTb": sb(768, B),
+    "GO": sb(192), "G16": sb(192), "hi": sb(192, B), "lo": sb(192, H), "w1": sb(192), "w2": sb(192), "cbg": sb(192),
+    "pos": sb(192, U), "cat": sb(192, B), "S2": sb(1552, B), "cl": sb(32), "c2": sb(24), "ou": sb(24, U),
+    "AW": sb(648), "OG": sb(40, U), "G": sb(640, B), "MT": sb(512), "V": sb(512), "PK": sb(128),
+    "i1": sb(128, I), "i2": sb(128, I), "i3": sb(144, I), "cls": sb(128), "cu": sb(8, U),
+    "E": sb(1024, B), "inv": sb(128, B), "cd": sb(128), "KG": sb(128), "PG": sb(128), "Em": sb(128, B),
+    "w0": sb(128), "r0": sb(128), "pd": sb(128), "NP": sb(256),
+    "su": sb(32, U), "sf": sb(32), "og": sb(4, U), "so": sb(8, U), "SG": sb(128), "mk": sb(64),
+    "D": sb(2 * DH), "DL": sb(6 * DH), "du": sb(48, U), "o1": sb(40), "o2": sb(40), "o3": sb(40), "o4": sb(40),
+    "LD": ("dram", [4, 128, 96], I), "DD": ("dram", [4, 128, 144], I), "HL": ("dram", [4, 128, 256], F),
+    "XS": ("dram", [24, 128, 68], F), "XL": ("dram", [24, 128, 68], F),
+    "OS": ("dram", [4, 128, 96], F), "OD": ("dram", [4, 128, 96], F),
+}
+for _i in range(8):
+    SCRATCH["B%d" % _i] = ("psum", [128, 512], F)
+
+SEMAPHORES = (["qv", "qa", "qp", "qg", "ls", "lsA", "lsB", "aL", "aD", "aK", "aP", "aO", "fin", "fo", "fk", "fs"]
+              + ["aX%d" % i for i in range(6)] + ["h%d" % i for i in range(4)] + ["hr%d" % i for i in range(4)]
+              + ["d%d" % i for i in range(60)])
+
+
+def overlap(a, b):
+    return a[0] == b[0] and a[1] < b[2] and b[1] < a[2] and a[3] < b[4] and b[3] < a[4]
+
+
+def arrange(ops):
+    for o in ops:
+        o["left"] = len(o["dep"]) + len(o["soft"])
+        for x in o["dep"] + o["soft"]:
+            x["next"].append(o)
+    o_ = [o for o in ops if o["left"] == 0]
+    top, left = [], {o["i"]: o["left"] for o in ops}
+    while o_:
+        o = o_.pop()
+        top.append(o)
+        for x in o["next"]:
+            left[x["i"]] -= 1
+            if left[x["i"]] == 0:
+                o_.append(x)
+    for o in reversed(top):
+        o["pr"] = o["lat"] + o["up"] + WAKE + max([x["pr"] for x in o["next"]] + [0.0])
+    free = {q: 0.0 for q in "vapgsx"}
+    ready, out = [o for o in ops if o["left"] == 0], []
+    for o in ready:
+        o["at"] = o["t0"]
+    while ready:
+        first = min(ready, key=lambda o: max(o["at"], free[o["q"]]))
+        q = first["q"]
+        now = max(first["at"], free[q])
+        cand = [o for o in ready if o["q"] == q]
+        best = max([o for o in cand if o["at"] <= now + 0.02], key=lambda o: o["pr"])
+        for o in cand:
+            if o["pr"] > best["pr"] + best["c"] and o["at"] < now + 0.5 * best["c"] and q != "x":
+                best = o
+        ready.remove(best)
+        st = max(best["at"], free[q])
+        if q != "x":
+            free[q] = st + best["c"]
+        best["st"], best["end"] = st, st + best["lat"]
+        out.append(best)
+        for x in best["next"]:
+            x["left"] -= 1
+            if x["left"] == 0:
+                x["at"] = max([x["t0"]] + [y["end"] + WAKE for y in x["dep"]] + [y["st"] + y["c"] + x["gap"] for y in x["soft"]])
+                ready.append(x)
+    return out
+
+
+def emit(g, T, ops):
+    eng = {"v": g.vector, "a": g.scalar, "p": g.tensor, "g": g, "s": g.sync}
+    hist, known, cnt, total, group = {}, {q: {} for q in eng}, {}, {}, {}
+    for o in ops:
+        if o["sem"] is not None:
+            total[o["sem"]] = total.get(o["sem"], 0) + o["n"]
+            group.setdefault(o["sem"], []).append(o)
+    last = {}
+    for o in ops:
+        q = o["q"]
+        dep, soft = {}, {}
+        for kind, regs in (("r", o["r"]), ("w", o["w"])):
+            for r in regs:
+                ps = r[0][0] == "B" and len(r[0]) == 2
+                for (k2, r2, o2) in hist.get(r[0], []):
+                    if o2["q"] == "p" and q == "p" and ps:
+                        soft[o2["i"]] = o2
+                    elif o2["sem"] is not None and o2["sem"] == o["sem"]:
+                        continue
+                    elif (ps and o2["q"] != q) or ((kind == "w" or k2 == "w") and overlap(r, r2)):
+                        for o3 in (group[o2["sem"]] if o2["sem"] is not None else [o2]):
+                            dep[o3["i"]] = o3
+        if q in "gs" and q in last:
+            soft[last[q]["i"]] = last[q]
+        if q == "x":
+            soft[last["g"]["i"]] = last["g"]
+        last[q] = o
+        o["dep"], o["soft"], o["next"] = list(dep.values()), list(soft.values()), []
+        for r in o["r"]:
+            hist.setdefault(r[0], []).append(("r", r, o))
+        for r in o["w"]:
+            hist.setdefault(r[0], []).append(("w", r, o))
+    for o in arrange(ops):
+        q = o["q"]
+        need = {}
+        for o2 in o["dep"]:
+            s, v = o2["tok"]
+            if need.get(s, (0, None))[0] < v:
+                need[s] = (v, o2)
+        if q != "x":
+            kn = known[q]
+            for s, (v, o2) in sorted(need.items(), key=lambda e: -e[1][1]["end"]):
+                if kn.get(s, 0) < v:
+                    eng[q].wait_ge(T.sem[s], v)
+                    kn[s] = v
+                    for s3, v3 in o2["clock"].items():
+                        if kn.get(s3, 0) < v3:
+                            kn[s3] = v3
+            o["clock"] = dict(kn)
+            ins = o["f"](eng[q])
+            if o["sem"] is None:
+                s = "q" + q
+                cnt[s] = cnt.get(s, 0) + 1
+                ins.then_inc(T.sem[s], 1)
+                o["tok"] = (s, cnt[s])
+            else:
+                if o["dma"]:
+                    ins.then_inc(T.sem[o["sem"]], 16)
+                o["tok"] = (o["sem"], total[o["sem"]])
+        else:
+            o["clock"] = {}
+            o["tok"] = (o["sem"], total[o["sem"]])
+    for s, v in list(cnt.items()) + list(total.items()):
+        if known["s"].get(s, 0) < v:
+            g.sync.wait_ge(T.sem[s], v)
+
+
+def bits(es):
+    m = 0
+    for e in es:
+        m |= 1 << e
+    return m
+
+
+def dst(topo, c):
+    a = topo.addr(c)
+    return DstId(rid=a[0], pnc=a[1])
+
+
+def crew(T, topo, c):
+    rest = [x for x in topo.cores_of(c) if x not in T.cores]
+    return [x for x in rest if topo.die(x) == topo.die(c)], [x for x in rest if topo.die(x) != topo.die(c)]
+
+
+def piece_cols(t, h):
+    return 1024 * t if h == 0 else 4096 + 1024 * ((t - 1) % N)
+
+
+def helper(g, core, T, topo):
+    for r, c in enumerate(T.cores):
+        near, far = crew(T, topo, c)
+        n_off = len(topo.engines(c, T.cores[(r + 1) % N]))
+        n_on = len(topo.engines(c, far[0])) - n_off
+        if core in near[:N - 1] or core == far[N - 1]:
+            own = core == far[N - 1]
+            s = r if own else (r - 1 - near.index(core)) % N
+            n_in = n_on // 2 if own else n_off
+            es = topo.engines(core, c)
+            rid, pid = topo.addr(c)[0], topo.addr(c)[1]
+            for k in range(4):
+                tab = T.K if k < 2 else T.P
+                c0 = piece_cols(s, k % 2)
+                for x in range(4):
+                    q = g.sync if x % 2 == 0 else g.scalar
+                    if x < 2:
+                        q.wait_ge(T.sem["h%d" % k], n_in)
+                    q.dma_start(tab[32 * x:32 * x + 32, c0:c0 + 1024], T.HL[k]).then_inc(T.sem["hr%d" % k], 16)
+            for k in range(4):
+                tab = T.K if k < 2 else T.P
+                c0 = piece_cols(s, k % 2)
+                g.wait_ge(T.sem["hr%d" % k], 64)
+                g.remote_dma(tab[:, c0:c0 + 1024], tab[:, c0:c0 + 1024], T.sem["aK" if k < 2 else "aP"], T.sem.ls,
+                             pid, rid, bits(es))
+            g.wait_ge(T.sem.ls, 4 * len(es))
+        if core in far[:N - 1]:
+            j = far.index(core)
+            to = crew(T, topo, T.cores[(r + 1 + j) % N])[0][j]
+            es = topo.engines(core, to)
+            rid, pid = topo.addr(to)[0], topo.addr(to)[1]
+            for a in range(2):
+                k = 2 * a + 1
+                c0 = (4 * j + k) * 256
+                g.wait_ge(T.sem["h%d" % k], n_on)
+                g.remote_dma(T.HL[k], T.VAL[:, c0:c0 + 256], T.sem["h%d" % k], T.sem.ls, pid, rid, bits(es))
+            g.wait_ge(T.sem.ls, 2 * len(es))
+
+
+def rank_program(g, core, T, topo):
+    rank = T.rank_of(core)
+    if rank is None:
+        helper(g, core, T, topo)
+        return
+    ops, nd, up = [], [0], [0.0]
+    others = [(rank + 1 + j) % N for j in range(N - 1)]
+    off = topo.engines(core, T.cores[others[0]])
+    near, far = crew(T, topo, core)
+    on = [e for e in topo.engines(core, far[0]) if e not in off]
+
+    def v(name, c0=0, c1=None, st=1, p0=0, p1=128):
+        c1 = SCRATCH[name][1][1] if c1 is None else c1
+        return (T[name][p0:p1, c0:c1:st] if st > 1 else T[name][p0:p1, c0:c1], [(name, p0, p1, c0, c1)], [],
+                (c1 - c0 + st - 1) // st, "p" if SCRATCH[name][0] == "psum" else "2" if SCRATCH[name][2] in (B, H, U) else "4")
+
+    def blk(name, c0, c1, d):
+        return v(name, c0, c1, 1, 32 * d, 32 * d + 32)
+
+    def slot(name, k, c0=None, c1=None):
+        return (T[name][k] if c0 is None else T[name][k, :, c0:c1], [(name, k, k + 1, c0 or 0, c1 or 9999)], [], 64, "d")
+
+    def ind(name, o):
+        w = v(name)
+        return (w[0].indirect(o[0]), w[1], o[1], 16 * o[3], "i")
+
+    def op(q, f, outs, ins, sem=None, n=0, dma=False, t0=0.0, gap=0.0):
+        r, w = [], []
+        ins = [x for x in ins if isinstance(x, tuple)]
+        for x in ins:
+            r += x[1] + x[2]
+        for x in outs:
+            w += x[1]
+            r += x[2]
+        if q == "x":
+            c = lat = 0.0
+        elif dma:
+            c, lat = 0.1, 2.2 + max(outs[0][3], ins[0][3]) / 500.0
+        elif sem is not None:
+            c, lat = 1.0, 4.0
+        elif q == "p":
+            c = lat = max(64, ins[1][3]) * (4 if ins[1][4] == "4" else 1) * 0.00055
+        else:
+            big = [x for x in ins if x[3] > 1]
+            m = max([outs[0][3]] + [x[3] for x in big])
+            kinds = [x[4] for x in big]
+            per = (3.8 if outs[0][4] == "i" else 1.56 if "i" in kinds else 2.0 if q == "g" else
+                   0.5 if q == "v" and big and outs[0][4] == "2" and all(k == "2" for k in kinds) else
+                   2.0 if len(big) == 2 and "p" not in kinds and outs[0][3] > 1 else 1.0)
+            c = lat = max(64, m * per) * 0.00104 + 0.05
+        ops.append({"q": q, "f": f, "r": r, "w": w, "sem": sem, "n": n, "dma": dma, "i": len(ops), "c": c, "lat": lat,
+                    "t0": t0, "gap": gap, "up": up[0]})
+
+    def a_(x):
+        return x[0] if isinstance(x, tuple) else x
+
+    def ts(o, x, s1, op0, s2=None, op1=None):
+        if op1 is None:
+            op("v", lambda e: e.tensor_scalar(o[0], x[0], a_(s1), None, op0), [o], [x, s1])
+        else:
+            op("v", lambda e: e.tensor_scalar(o[0], x[0], a_(s1), a_(s2), op0, op1), [o], [x, s1, s2])
+
+    def tt(o, x, y, op0):
+        op("v", lambda e: e.tensor_tensor(o[0], x[0], y[0], op0), [o], [x, y])
+
+    def cp(o, x):
+        op("v", lambda e: e.tensor_copy(o[0], x[0]), [o], [x])
+
+    def scan(o, x, y, init, op0, op1):
+        op("v", lambda e: e.tensor_tensor_scan(o[0], x[0], y[0], init, op0, op1), [o], [x, y])
+
+    def ms(o, c):
+        op("v", lambda e: e.memset(o[0], c), [o], [])
+
+    def act(o, x, func=AF.Identity, bias=None, scale=1.0):
+        if bias is None:
+            op("a", lambda e: e.activation(o[0], x[0], func, scale=scale), [o], [x])
+        else:
+            op("a", lambda e: e.activation(o[0], x[0], func, bias=bias[0], scale=scale), [o], [x, bias])
+
+    def mm(o, l, r, start=True, stop=True):
+        op("p", lambda e: e.matmul(o[0], l[0], r[0], start, stop), [o], [l, r])
+
+    def iota(o, pat, base=0, cm=0, fl=True):
+        if fl:
+            op("g", lambda e: e.iota(o[0], pat, base, cm, allow_small_or_imprecise_dtypes=True), [o], [])
+        else:
+            op("g", lambda e: e.iota(o[0], pat, base, cm), [o], [])
+
+    def newsem():
+        nd[0] += 1
+        return "d%d" % (nd[0] - 1)
+
+    def dma(q, o, x, sem=None, after=None):
+        op(q, lambda e: e.dma_start(o[0], x[0]), [o] + ([after] if after else []), [x], sem or newsem(), 16, True)
+
+    def ext(ap_):
+        return (ap_, [], [], 64, "d")
+
+    def fused(trs, lsem="ls"):
+        lst = [RemoteDMATransfer(dst_ids=[dst(topo, c)], dma_engine_mask=bits(es), remote_sem=T.sem[rs], src=x[0], dst=d)
+               for (c, es, rs, x, d) in trs]
+        op("g", lambda e: e.remote_dma_fused(lst, local_sem=T.sem[lsem]), [], [t[3] for t in trs], lsem,
+           sum(len(t[1]) for t in trs))
+
+    def arrive(sem, n, outs, t0=0.0):
+        op("x", None, outs, [], sem, n, False, t0, 5.0)
+
+    third = [off[0:2], off[2:4], off[4:6]]
+    rows = slice(32 * rank, 32 * rank + 32)
+
+    def C(k):
+        return v("C", k, k + 1)
+
+    IM, X1, X2 = v("B5", 0, 192), v("B5", 192, 384), v("B5", 384, 512)
+    Y1, COL, Z1, Z2 = v("B4", 0, 128), v("B4", 128, 256), v("B4", 256, 384), v("B4", 384, 512)
+    VALP = v("B0", 0, 192)
+
+    sl = newsem()
+    for j, d in enumerate(others):
+        dma("s", v("LS", 96 * j, 96 * j + 48), ext(T.lk[32 * d:32 * d + 32, :]), sl)
+        dma("a", v("LS", 96 * j + 48, 96 * j + 96), ext(T.li[32 * d:32 * d + 32, :]), sl)
+    so_ = newsem()
+    for a, src in enumerate((T.tk, T.tp)):
+        for j, d in enumerate(others + [rank]):
+            sj = newsem()
+            for h in range(2):
+                c0 = (4 * j + 2 * a + h) * 256
+                dma("sa"[h], v("SI", c0, c0 + 256), ext(src[32 * d:32 * d + 32, 1024 * h:1024 * h + 1024]), sj)
+        if a == 0:
+            dma("s", blk("LK", 0, 192, rank), ext(T.lk[rows, :]), so_)
+            dma("a", blk("LK", 192, 384, rank), ext(T.li[rows, :]), so_)
+    for s in range(4):
+        dma("sa"[s % 2], blk("PI", 8, 9, s), ext(T.pn[rows, :]), so_)
+    sd, sdk = newsem(), newsem()
+    for j, d in enumerate(others):
+        dma("sa"[j % 2], v("DS", 144 * j, 144 * j + 144), ext(T.dk[32 * d:32 * d + 32, :]), sd)
+    dma("a", blk("DK", 0, 576, rank), ext(T.dk[rows, :]), sdk)
+    iota(v("PI", 0, 1), [[0, 1]], 0, 1, False)
+    iota(v("IO"), [[1, 128]])
+    iota(v("A16"), [[16, 8], [0, 16]])
+    iota(v("B16"), [[0, 8], [1, 16]])
+    iota(v("B32"), [[0, 4], [1, 32]])
+    fused([(T.cores[d], third[j], "aL", v("LS", 96 * j, 96 * j + 96), T.LD[rank]) for j, d in enumerate(others)])
+    hn = len(on) // 2
+    for a in range(2):
+        for j, d in enumerate(others):
+            c0 = (4 * j + 2 * a) * 256
+            ts(v("VAL", c0, c0 + 512), v("SI", c0, c0 + 512), float(a), A.add)
+            hp = crew(T, topo, T.cores[d])[0][j]
+            lo_, hi_ = v("VAL", c0, c0 + 256), v("VAL", c0 + 256, c0 + 512)
+            fused([(hp, off, "h%d" % (2 * a), lo_, T.HL[2 * a]), (far[j], on, "h%d" % (2 * a + 1), hi_, hi_[0])], "lsA")
+        c0 = 512 * a
+        ts(v("EQ", c0, c0 + 512), v("SI", 3072 + c0, 3584 + c0), float(a), A.add)
+        fused([(far[N - 1], on[hn * h:hn * h + hn], "h%d" % (2 * a + h), v("EQ", c0 + 256 * h, c0 + 256 * h + 256),
+                T.HL[2 * a + h]) for h in range(2)], "lsB")
+    fused([(T.cores[d], third[j], "aD", v("DS", 144 * j, 144 * j + 144), T.DD[rank]) for j, d in enumerate(others)])
+    iota(v("UV"), [[4, 24], [96, 16]])
+    iota(v("KP"), [[0, 4], [1, 128]], 256)
+    arrive("aL", 6, [slot("LD", d) for d in others])
+    for j, d in enumerate(others):
+        dma("s", blk("LK", 0, 192, d), slot("LD", d, 0, 48), so_)
+        dma("a", blk("LK", 192, 384, d), slot("LD", d, 48, 96), so_)
+
+    cp(C(0), v("PI", 0, 1))
+    ts(v("PI", 1, 2), v("PI", 0, 1), 112, A.bitwise_and)
+    ts(v("PI", 2, 3), v("PI", 0, 1), 15, A.bitwise_and)
+    ts(v("PI", 3, 4), v("PI", 0, 1), 31, A.bitwise_and)
+    ts(v("PI", 4, 5), v("PI", 0, 1), 5, A.arith_shift_right)
+    for k, x in ((8, -1.0), (9, -float(4096 + CAP)), (10, -16.0), (14, 2.0 ** 66), (15, 1.0), (52, 0.0625)):
+        ms(C(k), x)
+    ts(v("PI", 5, 6), v("PI", 4, 5), 3.0, A.add)
+    cp(v("C", 1, 5), v("PI", 1, 5))
+    ts(v("C", 32, 48), v("IO", 0, 16), -1.0, A.mult, C(0), A.add)
+    ts(v("C", 48, 52), v("IO", 0, 4), -32.0, A.mult, C(0), A.add)
+    ts(v("PI", 5, 6), v("PI", 5, 6), 3, A.bitwise_and)
+    ts(C(5), C(4), 1.0, A.add, 0.0625, A.mult)
+    ts(v("C", 16, 32), v("IO", 0, 16), C(1), A.add)
+    ts(C(6), v("PI", 5, 6), 5.0, A.add, 0.0625, A.mult)
+    ts(C(7), v("PI", 5, 6), 4.0, A.add)
+    ts(v("ONf"), v("A16"), C(1), A.is_equal)
+    ts(v("IDb"), v("IO"), C(0), A.is_equal)
+    ts(v("t1"), v("IO"), C(0), A.is_lt)
+    ts(v("t2"), v("IO"), C(0), A.is_gt)
+    ts(v("t3"), v("IO"), C(0), A.is_equal, 4096.0, A.mult)
+    act(v("ONb"), v("ONf"), AF.Copy)
+    tt(v("t1"), v("t1"), v("ONf"), A.mult)
+    tt(v("t2"), v("t2"), v("ONf"), A.mult)
+    cp(v("inv"), v("A16"))
+    tt(v("UP"), v("t3"), v("t1"), A.subtract)
+    ms(v("RG"), 1.0)
+    ms(v("RG", 0, 768, 192), 0.0)
+    for r in range(16):
+        ts(v("SBb", 128 * r, 128 * r + 128), v("inv"), C(32 + r), A.is_equal)
+    cp(v("SBh"), v("SBb"))
+    for s in range(4):
+        ts(v("Rf", 128 * s, 128 * s + 128), v("B32"), C(48 + s), A.is_equal)
+    act(v("Rb"), v("Rf"), AF.Copy)
+
+    def address1():
+        act(v("hi"), v("KEY"), AF.Copy)
+        ts(v("k4"), v("KEY"), 4095.0, A.add)
+        ts(v("hb"), v("k4"), 8191, A.bitwise_and)
+        ts(v("t0"), v("k4"), 10, A.arith_shift_right, 3, A.bitwise_and)
+        ts(v("home"), v("k4"), 4095, A.bitwise_and)
+        tt(X1, v("hb"), IM, A.is_le)
+
+    def address2():
+        up[0] = 8.0
+        tt(v("lo"), v("KEY"), v("hi"), A.subtract)
+        up[0] = 0.0
+        tt(v("k4"), v("t0"), X1, A.add)
+        act(X1, X1, AF.Identity, None, -4.0)
+        ts(v("t0"), v("k4"), 3, A.bitwise_and)
+        ts(v("tob"), v("t0"), 1.0, A.add)
+
+    def address3():
+        for d in range(4):
+            ts(v("M", 192 * d, 192 * d + 192), v("tob"), float(d + 1), A.is_equal)
+        tt(v("cb0"), v("tob"), X1, A.add)
+        up[0] = 11.0
+        scan(v("S"), v("RG"), v("M", 0, 768), 0.0, A.mult, A.add)
+        up[0] = 0.0
+
+    def places():
+        for h in range(2):
+            b = "B%d" % (6 + h)
+            mm(v(b, 0, 384), v("ONb"), v("S", 384 * h, 384 * h + 384), True, False)
+            mm(v(b, 0, 384), v("UP"), v("M", 384 * h, 384 * h + 384), False, True)
+            act(v("WTb", 384 * h, 384 * h + 384), v(b, 0, 384), AF.Relu, C(9))
+        for d in range(4):
+            mm(v("B6", 0, 192), v("IDb"), v("WTb", 192 * d, 192 * d + 192), d == 0, d == 3)
+        act(v("GO"), v("B6", 0, 192), AF.Relu, C(15), -1.0)
+        act(v("G16"), v("B6", 0, 192), AF.Relu, C(52), -1.0)
+
+    def spread(r0, r1):
+        for r in range(r0, r1):
+            b = "B%d" % (6 + r % 2)
+            mm(v(b, 0, 192), v("SBb", 128 * r, 128 * r + 128), v("hi"), True, False)
+            mm(v(b, 0, 192), v("SBh", 128 * r, 128 * r + 128), v("lo"), False, True)
+            act(v("KB", r, 3072, 16), v(b, 0, 192), AF.Identity, C(8))
+
+    def repeat_keys():
+        for h in range(2):
+            b = "B%d" % (6 + h)
+            for s in range(2):
+                mm(v(b, 192 * s, 192 * s + 192), v("Rf", 128 * (2 * h + s), 128 * (2 * h + s) + 128), v("KEY"))
+            act(v("KR", 384 * h, 384 * h + 384), v(b, 0, 384), AF.Copy)
+            act(v("KR", 768 + 384 * h, 768 + 384 * h + 384), v(b, 0, 384), AF.Copy)
+
+    def columns():
+        ts(X1, v("hb"), v("NN", 0, 1), A.is_lt, 4096.0, A.mult)
+        tt(v("w2"), v("home"), X1, A.add)
+        cp(v("pos"), v("w2"))
+        act(X1, X1, AF.Identity, None, 1.0 / 1024)
+
+    def classes():
+        tt(X1, v("cb0"), X1, A.add)
+        tt(v("cbg"), v("G16"), X1, A.mult)
+
+    def images():
+        ts(v("w2"), v("cbg"), 0.28, A.is_le, -8192.0, A.mult)
+        tt(v("w2"), v("home"), v("w2"), A.add)
+        tt(IM, v("w2"), IM, A.max)
+
+    def look_eq(c):
+        tt(v("EQ", 1024 * c, 1024 * c + 1024), ind("K", v("pos", 64 * c, 64 * c + 64)), v("KB", 1024 * c, 1024 * c + 1024), A.is_equal)
+
+    def look_val(c):
+        tt(v("VAL", 1024 * c, 1024 * c + 1024), ind("P", v("pos", 64 * c, 64 * c + 64)), v("EQ", 1024 * c, 1024 * c + 1024), A.mult)
+        for r in range(16):
+            mm(v("B0", 64 * c, 64 * c + 64), v("SRf", 128 * r, 128 * r + 128), v("VAL", 1024 * c + r, 1024 * c + 1024, 16), r == 0, r == 15)
+
+    def new_keys(t):
+        tt(v("w1"), v("D1", 192 * t, 192 * t + 192), X1, A.mult)
+        tt(X1, v("w1"), VALP, A.add)
+        tt(X1, X1, v("KEY"), A.subtract)
+        tt(X1, X1, v("GO"), A.mult)
+        tt(v("KEY"), X1, v("KEY"), A.add)
+
+    def tolist(o, x):
+        tt(v("t1"), x, v("DG"), A.mult)
+        scan(o, v("RS"), v("t1"), 0.0, A.mult, A.add)
+
+    def early(last):
+        ms(v("AW", 0, 128), 0.0)
+        ts(v("og"), v("JL", 0, 4), v("NN", 0, 1), A.add, 4095.0, A.min)
+        ts(v("NN", 4, 5), v("NN", 0, 1), -8192.0, A.add)
+        ts(v("NN", 5, 6), v("NN", 0, 1), -4160.0, A.add)
+        if last:
+            ts(v("i1", 0, 64), v("IO", 0, 64), v("NN", 0, 1), A.add, 4095.0, A.min)
+            ts(v("i1", 0, 64), v("i1", 0, 64), 10, A.arith_shift_right)
+            ts(v("mk"), v("i1", 0, 64), C(4), A.is_equal)
+
+    def send_lanes():
+        act(v("w2"), v("KEY"), AF.Identity, C(8))
+        act(v("cb0"), IM, AF.Identity, C(15))
+        s1 = newsem()
+        for d in others:
+            dma("s", slot("OS", d, 0, 48), blk("w2", 0, 192, d), s1)
+            dma("s", slot("OS", d, 48, 96), blk("cb0", 0, 192, d), s1)
+        dma("s", ext(T.yl[rows, :]), blk("w2", 0, 192, rank), "fo")
+        dma("s", ext(T.yi[rows, :]), blk("cb0", 0, 192, rank), "fo")
+        fused([(T.cores[d], third[j], "aO", slot("OS", d), T.OD[rank]) for j, d in enumerate(others)])
+        arrive("aO", 6, [slot("OD", d) for d in others])
+
+    def store_lanes():
+        for d in others:
+            dma("s", ext(T.yl[32 * d:32 * d + 32, :]), slot("OD", d, 0, 48), "fin")
+            dma("s", ext(T.yi[32 * d:32 * d + 32, :]), slot("OD", d, 48, 96), "fin")
+
+    landing = {}
+
+    def send_changes(k, q="s"):
+        c0 = DH * (k % 2)
+        s1 = newsem()
+        landing[k] = newsem()
+        for j, d in enumerate(others):
+            dma(q[j % len(q)], slot("XS", 4 * k + d), blk("D", c0, c0 + DH, d), s1)
+        dma("s", blk("DL", DH * k, DH * k + DH, rank), blk("D", c0, c0 + DH, rank), landing[k])
+        fused([(T.cores[d], third[j], "aX%d" % k, slot("XS", 4 * k + d), T.XL[4 * k + rank]) for j, d in enumerate(others)])
+        arrive("aX%d" % k, 6, [slot("XL", 4 * k + d) for d in others])
+
+    def take_changes(k, q="s"):
+        for j, d in enumerate(others):
+            dma(q[j % len(q)], blk("DL", DH * k, DH * k + DH, d), slot("XL", 4 * k + d), landing[k])
+
+    def own_columns(o, n, ta, tb):
+        ts(v("i3", 48, 48 + n), v("i3", 0, n), 10, A.arith_shift_right)
+        ts(v("i3", 96, 96 + n), v("i3", 0, n), 1023, A.bitwise_and)
+        ts(v("o1", 0, n), v("i3", 48, 48 + n), ta, A.is_equal)
+        ts(v("o2", 0, n), v("i3", 48, 48 + n), tb, A.is_equal)
+        ts(v("o4", 0, n), v("i3", 48, 48 + n), tb, A.is_equal, 1024.0, A.mult)
+        tt(v("o3", 0, n), v("i3", 96, 96 + n), v("C", 64, 64 + n), A.subtract)
+        tt(v("o1", 0, n), v("o1", 0, n), v("o2", 0, n), A.add)
+        tt(v("o4", 0, n), v("o4", 0, n), v("C", 64, 64 + n), A.add)
+        tt(v("o3", 0, n), v("o3", 0, n), v("o1", 0, n), A.mult)
+        tt(o, v("o3", 0, n), v("o4", 0, n), A.add)
+
+    def patch(k0, k1):
+        for k in range(k0, k1):
+            cp(v("i3", 8 * (k - k0), 8 * (k - k0) + 8), v("DL", DH * k + 256, DH * k + 264))
+        n = 8 * (k1 - k0)
+        own_columns(v("o2", 0, n), n, float(rank), float(4 + (rank - 1) % N))
+        cp(v("du", 8 * k0, 8 * k1), v("o2", 0, n))
+        for k in range(k0, k1):
+            cp(ind("MK", v("du", 8 * k, 8 * k + 8)), v("DL", DH * k, DH * k + 128))
+            cp(ind("MS", v("du", 8 * k, 8 * k + 8)), v("DL", DH * k + 128, DH * k + 256))
+
+    def finish():
+        k = 2 * RO - 1
+        patch(0, k - 1)
+        patch(k - 1, k)
+        cp(v("du", 8 * k, 8 * k + 8), v("DL", DH * k + 256, DH * k + 264))
+        cp(ind("MK", v("du", 8 * k, 8 * k + 8)), v("DL", DH * k, DH * k + 128))
+        dma("s", ext(T.yk[:, 0:1024]), v("MK", 0, 1024), "fk")
+        dma("a", ext(T.yk[:, 1024:2048]), v("MK", 1024, 2048), "fk")
+        dma("a", ext(T.yn[:, :]), v("DL", DH * k + 264, DH * k + 265), "fk")
+        cp(ind("MS", v("du", 8 * k, 8 * k + 8)), v("DL", DH * k + 128, DH * k + 256))
+        for x in range(8):
+            dma("sa"[x % 2], ext(T.ys[x:x + 1, :]), v("MS", 0, 2048, 1, 16 * x, 16 * x + 1), "fs")
+
+    def round_(t):
+        last = t == RO - 1
+        nn = v("D", DH + 264, DH + 265)
+        tt(v("cat"), v("cbg"), VALP, A.subtract)
+        for s in range(4):
+            mm(v("B%d" % (1 + s // 2), 192 * (s % 2), 192 * (s % 2) + 192), v("Rb", 128 * s, 128 * s + 128), v("cat"))
+        act(v("WTb", 0, 384), v("B1", 0, 384), AF.Copy)
+        act(v("WTb", 384, 768), v("B2", 0, 384), AF.Copy)
+        act(X1, VALP, AF.Relu, C(15), -1.0)
+        for h in range(2):
+            for k in range(2):
+                ts(v("M", 768 * k + 384 * h, 768 * k + 384 * h + 384), v("WTb", 384 * h, 384 * h + 384), C(5 + k), A.is_equal)
+        scan(v("S2", 1, 1537), v("M"), v("M"), 0.0, A.add, A.max)
+        for r in range(16):
+            mm(v("B3", 0, 25), v("SRb", 128 * r, 128 * r + 128), v("S2", 96 * r, 96 * r + 97, 4), r == 0, r == 15)
+        new_keys(t)
+        if last:
+            send_lanes()
+        ts(v("cl", 0, 25), v("B3", 0, 25), 128.0, A.min)
+        tt(v("c2"), v("cl", 1, 25), v("cl", 0, 24), A.is_equal)
+        tt(v("c2"), v("c2"), v("TR"), A.mult)
+        tt(v("c2"), v("c2"), v("cl", 0, 24), A.add)
+        cp(v("ou"), v("c2"))
+        cp(ind("AW", v("ou")), v("UV"))
+        scan(Y1, v("AW", 0, 128), v("AW", 0, 128), 0.0, A.max, A.max)
+        tolist(v("t3"), Y1)
+        for i in range(5):
+            ts(v("OG", 8 * i, 8 * i + 8), v("t3", 15, 128, 16), float(i), A.add)
+        act(v("G"), ind("S2", v("OG")))
+        mm(v("B1"), v("UA"), v("G", 0, 512), True, False)
+        mm(v("B1"), v("UB"), v("G", 128, 640), False, True)
+        if not last:
+            address1()
+        tt(v("MT"), v("B1"), v("KP"), A.is_equal)
+        tt(v("V"), ind("KR", v("OG", 0, 32)), v("MT"), A.mult)
+        pk = v("B2", 0, 128)
+        for i in range(4):
+            mm(pk, v("ONf"), v("V", 128 * i, 128 * i + 128), i == 0, i == 3)
+        if not last:
+            address2()
+        ts(v("i1"), pk, 4095.0, A.add)
+        act(v("PK"), pk, AF.Copy)
+        act(v("inv"), v("PK"), AF.Relu, C(14), -2.0 ** 66)
+        ts(v("i2"), v("i1"), 8191, A.bitwise_and)
+        ts(v("i3", 0, 128), v("i1"), 4095, A.bitwise_and)
+        ts(Y1, v("i2"), v("NN", 0, 1), A.is_lt, 4096.0, A.mult)
+        tt(COL, v("i3", 0, 128), Y1, A.add)
+        tolist(v("cls"), COL)
+        cp(v("cu"), v("cls", 15, 128, 16))
+        act(v("Em"), ind("K", v("cu")), AF.Relu, None, -1.0)
+        act(v("KG"), ind("K", v("cu")))
+        act(v("PG"), ind("P", v("cu")))
+        mm(v("B3", 0, 128), v("IDb"), v("inv"), True, False)
+        for c in range(8):
+            ts(v("E", 144 * c, 128 * c + 128), v("B4", 128 + 16 * c, 256), v("cls", 16 * c + 15, 16 * c + 16), A.is_equal,
+               v("WCs", 16 * c + 15, 16 * c + 16), A.mult)
+            mm(v("B3", 16 * c, 128), v("ONb"), v("E", 144 * c, 128 * c + 128), False, c == 7)
+        mm(v("B1", 0, 128), v("FE"), v("Em"))
+        mm(v("B1", 128, 256), v("ONb"), v("Em"))
+        act(v("w0"), v("B1", 0, 128), AF.Relu)
+        act(v("r0"), v("B1", 128, 256), AF.Relu, C(15), -1.0)
+        tt(v("cd"), COL, v("TK"), A.subtract)
+        ts(v("i2"), v("i1"), 1023, A.bitwise_and)
+        ts(v("i3", 0, 128), v("i1"), 10, A.arith_shift_right)
+        tt(Y1, v("THR"), v("B3", 0, 128), A.is_gt)
+        tt(Z1, v("w0"), Y1, A.mult)
+        tt(Z2, v("PK"), Z1, A.mult)
+        tt(v("D", 0, 128), v("KG"), Z2, A.add)
+        if not last:
+            for s in range(4):
+                mm(v("B2", 128 * s, 128 * s + 128), v("Rf", 128 * s, 128 * s + 128), v("D", 0, 128))
+            for h in range(2):
+                act(v("MT", 256 * h, 256 * h + 256), v("B2", 256 * h, 256 * h + 256), AF.Copy)
+        tt(Z2, v("cd"), Y1, A.mult)
+        tolist(v("t3"), Z2)
+        if not last:
+            for s in range(4):
+                mm(v("B3", 128 + 8 * s, 136 + 8 * s), v("Rf", 128 * s, 128 * s + 128), v("t3", 15, 128, 16))
+        ts(X2, v("i2"), 1024.0, A.mult, -3.0, A.add)
+        tt(X2, v("i3", 0, 128), X2, A.add)
+        tt(v("pd"), X2, v("PG"), A.subtract)
+        tt(X2, v("pd"), Z1, A.mult)
+        tt(v("NP", 0, 128), v("PG"), X2, A.add)
+        if not last:
+            tt(v("sf"), v("B3", 128, 160), v("TL"), A.add)
+            for s in range(4):
+                mm(v("B3", 128 * s, 128 * s + 128), v("Rf", 128 * s, 128 * s + 128), v("NP", 0, 128))
+            act(v("V"), v("B3"), AF.Copy)
+            cp(v("su"), v("sf"))
+        tt(v("r0"), v("r0"), Y1, A.mult)
+        op("v", lambda e: e.tensor_reduce(T.NN[:, 1:2], T.r0[:, :], AxisListType.X, A.add), [v("NN", 1, 2)], [v("r0")])
+        mm(v("B1", 256, 257), v("Ff"), v("NN", 1, 2))
+        mm(v("B1", 0, 128), v("ONf"), v("NP", 0, 128))
+        tt(v("D", 256, 264), v("t3", 15, 128, 16), v("C", 56, 64), A.add)
+        if not last:
+            cp(ind("K", v("su")), v("MT"))
+        else:
+            cp(v("su", 0, 8), v("D", 256, 264))
+            cp(ind("K", v("su", 0, 8)), v("D", 0, 128))
+        act(v("SG", 0, 64), ind("K", v("og")))
+        act(v("t1", 0, 64), v("SG", 0, 64), AF.Identity, C(15)) if not last else None
+        ts(v("NN", 2, 3), v("B1", 256, 257), 64.0, A.min, v("NN", 0, 1), A.add)
+        act(v("D", 128, 256), v("B1", 0, 128), AF.Identity, C(10))
+        send_changes(2 * t)
+        ts(nn, v("NN", 2, 3), 4096.0, A.min)
+        tt(v("NN", 3, 4), nn, v("NN", 0, 1), A.subtract)
+        if not last:
+            spread(0, 16)
+            address3()
+            places()
+            repeat_keys()
+            cp(ind("P", v("su")), v("V"))
+        else:
+            cp(ind("P", v("su", 0, 8)), v("NP", 0, 128))
+        act(v("SG", 64, 128), ind("P", v("og")))
+        ts(v("o1", 0, 4), v("JL", 0, 4), v("NN", 3, 4), A.is_lt, v("NN", 4, 5), A.mult)
+        ts(v("o1", 4, 8), v("JL", 0, 4), v("NN", 3, 4), A.is_lt, v("NN", 5, 6), A.mult)
+        cp(v("NN", 0, 1), nn)
+        if last:
+            tt(v("i3", 0, 8), v("o1", 0, 8), v("C", 112, 120), A.add)
+            tt(v("t2", 0, 64), v("SG", 0, 64), v("mk"), A.mult)
+            tt(v("t2", 64, 128), v("SG", 64, 128), v("mk"), A.mult)
+            mm(v("B2", 0, 128), v("Ff"), v("t2"))
+            own_columns(v("D", DH + 256, DH + 264), 8, C(4), C(7))
+            cp(v("SG"), v("B2", 0, 128))
+            act(v("t1", 0, 64), v("SG", 0, 64), AF.Identity, C(15))
+        else:
+            tt(v("D", DH + 256, DH + 264), v("o1", 0, 8), v("C", 112, 120), A.add)
+            cp(v("so"), v("D", DH + 256, DH + 264))
+        act(v("t1", 64, 128), v("SG", 64, 128), AF.Identity, C(8))
+        ts(v("i1", 0, 64), v("SG", 0, 64), 0.0, A.max)
+        ts(v("i2", 0, 64), v("i1", 0, 64), 12, A.arith_shift_right, 1, A.bitwise_and)
+        tt(v("t3", 0, 64), v("t1", 0, 64), v("i2", 0, 64), A.mult)
+        tt(v("D", DH, DH + 64), v("SG", 0, 64), v("t3", 0, 64), A.subtract)
+        ts(v("D", DH + 64, DH + 128), v("t3", 0, 64), -1.0, A.add)
+        if not last:
+            cp(ind("K", v("so")), v("D", DH, DH + 128))
+        tt(v("t3", 64, 128), v("t1", 64, 128), v("i2", 0, 64), A.mult)
+        tt(v("NP", 128, 192), v("SG", 64, 128), v("t3", 64, 128), A.subtract)
+        ts(v("NP", 192, 256), v("t3", 64, 128), 1.0, A.add)
+        mm(v("B1", 0, 128), v("ONf"), v("NP", 128, 256))
+        act(v("D", DH + 128, DH + 256), v("B1", 0, 128), AF.Identity, C(10))
+        if not last:
+            cp(ind("P", v("so")), v("NP", 128, 256))
+            columns()
+        send_changes(2 * t + 1, "sa" if last else "s")
+        if last:
+            take_changes(2 * t)
+            store_lanes()
+            take_changes(2 * t + 1, "sa")
+        else:
+            take_changes(2 * t)
+            take_changes(2 * t + 1)
+
+    cp(v("inv"), v("IO"))
+    for r in range(16):
+        ts(v("SRb", 128 * r, 128 * r + 128), v("inv"), C(16 + r), A.is_equal)
+    ts(v("t3"), v("IO"), C(0), A.is_equal, -255.0, A.mult)
+    ts(v("cd"), v("IO"), C(0), A.is_equal, 256.0, A.mult)
+    tt(v("FE"), v("IDb"), v("t2"), A.subtract)
+    tt(v("UA"), v("t3"), v("t1"), A.add)
+    tt(v("UB"), v("cd"), v("t2"), A.add)
+    ts(v("Ff"), v("B32"), C(3), A.is_equal)
+    ts(v("DG"), v("B16"), C(2), A.is_equal)
+    ts(v("RS"), v("B16"), 0.5, A.is_gt)
+    ts(v("KEY"), v("LK", 0, 192), 1.0, A.add)
+    ts(IM, v("LK", 192, 384), -1.0, A.add)
+    cp(v("NN", 0, 1), v("PI", 8, 9))
+    address1()
+    address2()
+    address3()
+    places()
+    spread(0, 16)
+    act(v("SRf"), v("SRb"), AF.Copy)
+    repeat_keys()
+    columns()
+    sn, sm = newsem(), newsem()
+    for a, m in enumerate(("MK", "MS")):
+        for h in range(2):
+            c0 = 512 * a + 256 * h
+            dma("s", blk(m, 1024 * h, 1024 * h + 1024, rank), v("EQ", c0, c0 + 256), sn)
+    for a, m in enumerate(("MS", "MK")):
+        for j, d in enumerate(others):
+            for h in range(2):
+                c0 = (4 * j + 2 * (1 - a) + h) * 256
+                dma("s", blk(m, 1024 * h, 1024 * h + 1024, d), v("VAL", c0, c0 + 256), sm, v("VAL", 0, 1) if a + j + h == 0 else None)
+    arrive("aD", 6, [slot("DD", d) for d in others], 46.0)
+    for d in others:
+        dma("s", blk("DK", 0, 576, d), slot("DD", d), sdk)
+    ms(v("t2"), 0.5)
+    ms(v("t3"), 0.0)
+    scan(v("THR"), v("t2"), v("t3"), 2.0 ** 64, A.mult, A.add)
+    tolist(v("WCs"), v("THR"))
+    ts(v("THR"), v("THR"), 2.5, A.mult)
+    ts(C(11), C(2), 24.0, A.mult, 129.0, A.add)
+    ts(C(12), C(4), 128.0, A.mult, 8192.0, A.add)
+    ts(C(13), C(2), 8192.0, A.add)
+    ts(v("JL", 0, 8), v("IO", 0, 8), 16.0, A.mult, C(2), A.add)
+    ts(v("TR"), v("IO", 0, 24), C(11), A.add)
+    ts(v("TK"), v("IO"), C(12), A.add)
+    ts(v("TL"), v("IO", 0, 32), 16.0, A.mult, C(13), A.add)
+    ts(v("C", 112, 120), v("JL"), 8192.0, A.add)
+    ts(v("C", 56, 64), v("JL"), C(12), A.add)
+    for x in range(5):
+        ts(v("C", 64 + 8 * x, 72 + 8 * x), v("JL"), 2048.0, A.add)
+    ms(v("K", 8192, WT), 0.0)
+    ms(v("P", 8192, WT), 0.0)
+    ms(v("MK", 2048, WM), 0.0)
+    ms(v("MS", 2048, WM), 0.0)
+    ms(v("AW"), 0.0)
+    ms(v("S2", 0, 1), 0.0)
+    ms(v("S2", 1537, 1552), 0.0)
+    ms(v("D", 264, DH), 0.0)
+    ms(v("D", DH + 264, 2 * DH), 0.0)
+    classes()
+    images()
+    early(False)
+    ts(v("D1"), v("DK"), 1.0, A.add)
+    for x in range(4):
+        b = "B%d" % (6 + x % 2)
+        mm(v(b), v("ONf"), v("MS", 512 * x, 512 * x + 512))
+        act(v("MS", 512 * x, 512 * x + 512), v(b), AF.Identity, C(10))
+    ne = len(topo.engines(near[0], core))
+    arrive("aK", 8 * ne, [v("K", 0, 8192)], 33.0)
+    arrive("aP", 8 * ne, [v("P", 0, 8192)], 40.0)
+    for t in range(RO):
+        if t == 0:
+            for c in range(3):
+                look_eq(c)
+            for c in range(3):
+                look_val(c)
+        else:
+            for c in range(3):
+                look_eq(c)
+                look_val(c)
+            classes()
+            images()
+            early(t == RO - 1)
+        round_(t)
+    finish()
+    emit(g, T, ops)

@@ -8,6 +8,9 @@ WT = 8704
 WM = 2176
 DH = 272
 WAKE = 0.08
+UP = [0.0, 0.0, 5.0, 5.0]
+PASSES = 3
+SHAKE = [0, 0.0]
 F, B, I, U, H = "float32", "bfloat16", "int32", "uint16", "float16"
 
 
@@ -17,11 +20,11 @@ def sb(n, d=F):
 
 SCRATCH = {
     "K": sb(WT), "P": sb(WT), "MK": sb(WM), "MS": sb(WM), "SI": sb(4096, I),
-    "VAL": sb(3072), "EQ": sb(3072), "KB": sb(3072), "KR": sb(1536),
+    "VAL": sb(3072), "EQ": sb(1024), "EQb": sb(3072, B), "OI": sb(40, B), "KB": sb(3072), "KR": sb(1536),
     "LS": sb(288, I), "DS": sb(432, I), "LK": sb(384, I), "DK": sb(576, I), "D1": sb(576),
     "SBb": sb(2048, B), "SBh": sb(2048, H), "SRf": sb(2048), "SRb": sb(2048, B),
     "IO": sb(128), "A16": sb(128), "B16": sb(128), "B32": sb(128), "UV": sb(384), "KP": sb(512), "PI": sb(16, I),
-    "C": sb(128), "ONb": sb(128, B), "ONf": sb(128), "UP": sb(128, B), "IDb": sb(128, B), "UA": sb(128, B),
+    "C": sb(128), "ONb": sb(128, B), "ONf": sb(128), "UP": sb(128, B), "IDb": sb(128, B), "IDf": sb(128), "UA": sb(128, B),
     "UB": sb(128, B), "FE": sb(128, B), "Rb": sb(512, B), "Rf": sb(512), "Ff": sb(128), "DG": sb(128),
     "RS": sb(128), "THR": sb(128), "RG": sb(768, B), "TR": sb(24), "TL": sb(32), "JL": sb(8),
     "TK": sb(128), "WCs": sb(128), "t1": sb(128), "t2": sb(128), "t3": sb(128),
@@ -67,6 +70,8 @@ def arrange(ops):
                 o_.append(x)
     for o in reversed(top):
         o["pr"] = o["lat"] + o["up"] + WAKE + max([x["pr"] for x in o["next"]] + [0.0])
+    for o in ops:
+        o["pr"] += SHAKE[1] * ((o["i"] * 7919 + SHAKE[0] * 104729) * 48271 % 65537) / 65537.0
     free = {q: 0.0 for q in "vapgsx"}
     ready, out = [o for o in ops if o["left"] == 0], []
     for o in ready:
@@ -91,7 +96,41 @@ def arrange(ops):
             if x["left"] == 0:
                 x["at"] = max([x["t0"]] + [y["end"] + WAKE for y in x["dep"]] + [y["st"] + y["c"] + x["gap"] for y in x["soft"]])
                 ready.append(x)
-    return out
+    for o in ops:
+        o["dn"], o["sn"] = [], []
+    for o in ops:
+        for y in o["dep"]:
+            y["dn"].append(o)
+        for y in o["soft"]:
+            y["sn"].append(o)
+
+    def place(line, at, c):
+        k = 0
+        while k < len(line) and line[k][1] <= at:
+            k += 1
+        while k < len(line) and line[k][0] < at + c - 1e-9:
+            at = max(at, line[k][1])
+            k += 1
+        line.insert(k, (at, at + c))
+        return at
+
+    best, span = [o["st"] for o in ops], max(o["end"] for o in ops)
+    for _ in range(PASSES):
+        lines = {q: [] for q in free}
+        for o in sorted(ops, key=lambda o: (-o["st"] - o["c"], -o["st"])):
+            at = max([o["lat"] - o["c"]] + [x["rs"] + x["c"] + o["lat"] - o["c"] + WAKE for x in o["dn"]]
+                     + [x["rs"] + x["c"] + x["gap"] for x in o["sn"]])
+            o["rs"] = at if o["q"] == "x" else place(lines[o["q"]], at, o["c"])
+        lines = {q: [] for q in free}
+        for o in sorted(ops, key=lambda o: (-o["rs"] - o["c"], -o["rs"])):
+            at = max([o["t0"]] + [y["end"] + WAKE for y in o["dep"]] + [y["st"] + y["c"] + o["gap"] for y in o["soft"]])
+            o["st"] = at if o["q"] == "x" else place(lines[o["q"]], at, o["c"])
+            o["end"] = o["st"] + o["lat"]
+        if max(o["end"] for o in ops) < span:
+            best, span = [o["st"] for o in ops], max(o["end"] for o in ops)
+    for o, s in zip(ops, best):
+        o["st"], o["end"] = s, s + o["lat"]
+    return sorted(ops, key=lambda o: o["st"])
 
 
 def emit(g, T, ops):
@@ -118,6 +157,10 @@ def emit(g, T, ops):
                             dep[o3["i"]] = o3
         if q in "gs" and q in last:
             soft[last[q]["i"]] = last[q]
+        if q == "a" and o["dma"]:
+            if "ad" in last:
+                soft[last["ad"]["i"]] = last["ad"]
+            last["ad"] = o
         if q == "x":
             soft[last["g"]["i"]] = last["g"]
         last[q] = o
@@ -260,7 +303,7 @@ def rank_program(g, core, T, topo):
         elif dma:
             c, lat = 0.1, 2.2 + max(outs[0][3], ins[0][3]) / 500.0
         elif sem is not None:
-            c, lat = 1.0, 4.0
+            c, lat = 1.0, (12.0 if sem == "lsA" else 4.0)
         elif q == "p":
             c = lat = max(64, ins[1][3]) * (4 if ins[1][4] == "4" else 1) * 0.00055
         else:
@@ -365,6 +408,7 @@ def rank_program(g, core, T, topo):
     iota(v("B16"), [[0, 8], [1, 16]])
     iota(v("B32"), [[0, 4], [1, 32]])
     fused([(T.cores[d], third[j], "aL", v("LS", 96 * j, 96 * j + 96), T.LD[rank]) for j, d in enumerate(others)])
+    arrive("aL", 6, [slot("LD", d) for d in others], 12.0)
     hn = len(on) // 2
     for a in range(2):
         for j, d in enumerate(others):
@@ -380,7 +424,6 @@ def rank_program(g, core, T, topo):
     fused([(T.cores[d], third[j], "aD", v("DS", 144 * j, 144 * j + 144), T.DD[rank]) for j, d in enumerate(others)])
     iota(v("UV"), [[4, 24], [96, 16]])
     iota(v("KP"), [[0, 4], [1, 128]], 256)
-    arrive("aL", 6, [slot("LD", d) for d in others])
     for j, d in enumerate(others):
         dma("s", blk("LK", 0, 192, d), slot("LD", d, 0, 48), so_)
         dma("a", blk("LK", 192, 384, d), slot("LD", d, 48, 96), so_)
@@ -390,7 +433,8 @@ def rank_program(g, core, T, topo):
     ts(v("PI", 2, 3), v("PI", 0, 1), 15, A.bitwise_and)
     ts(v("PI", 3, 4), v("PI", 0, 1), 31, A.bitwise_and)
     ts(v("PI", 4, 5), v("PI", 0, 1), 5, A.arith_shift_right)
-    for k, x in ((8, -1.0), (9, -float(4096 + CAP)), (10, -16.0), (14, 2.0 ** 66), (15, 1.0), (52, 0.0625)):
+    for k, x in ((8, -1.0), (9, -float(4096 + CAP)), (10, -16.0), (14, 2.0 ** 66), (15, 1.0), (52, 0.0625),
+                 (53, -8192.0), (54, -4160.0), (55, 40960.0)):
         ms(C(k), x)
     ts(v("PI", 5, 6), v("PI", 4, 5), 3.0, A.add)
     cp(v("C", 1, 5), v("PI", 1, 5))
@@ -429,7 +473,7 @@ def rank_program(g, core, T, topo):
         tt(X1, v("hb"), IM, A.is_le)
 
     def address2():
-        up[0] = 8.0
+        up[0] = UP[0]
         tt(v("lo"), v("KEY"), v("hi"), A.subtract)
         up[0] = 0.0
         tt(v("k4"), v("t0"), X1, A.add)
@@ -441,7 +485,7 @@ def rank_program(g, core, T, topo):
         for d in range(4):
             ts(v("M", 192 * d, 192 * d + 192), v("tob"), float(d + 1), A.is_equal)
         tt(v("cb0"), v("tob"), X1, A.add)
-        up[0] = 11.0
+        up[0] = UP[1]
         scan(v("S"), v("RG"), v("M", 0, 768), 0.0, A.mult, A.add)
         up[0] = 0.0
 
@@ -482,15 +526,18 @@ def rank_program(g, core, T, topo):
         tt(v("cbg"), v("G16"), X1, A.mult)
 
     def images():
-        ts(v("w2"), v("cbg"), 0.28, A.is_le, -8192.0, A.mult)
-        tt(v("w2"), v("home"), v("w2"), A.add)
+        act(v("w2"), v("cbg"), AF.Relu, C(55), -131072.0)
+        tt(v("w2"), v("home"), v("w2"), A.subtract)
         tt(IM, v("w2"), IM, A.max)
 
     def look_eq(c):
-        tt(v("EQ", 1024 * c, 1024 * c + 1024), ind("K", v("pos", 64 * c, 64 * c + 64)), v("KB", 1024 * c, 1024 * c + 1024), A.is_equal)
+        tt(v("EQb", 1024 * c, 1024 * c + 1024), ind("K", v("pos", 64 * c, 64 * c + 64)), v("KB", 1024 * c, 1024 * c + 1024), A.is_equal)
+        for r in range(16):
+            mm(v("B3", 64 * c, 64 * c + 64), v("SRb", 128 * r, 128 * r + 128), v("EQb", 1024 * c + r, 1024 * c + 1024, 16), r == 0, r == 15)
 
     def look_val(c):
-        tt(v("VAL", 1024 * c, 1024 * c + 1024), ind("P", v("pos", 64 * c, 64 * c + 64)), v("EQ", 1024 * c, 1024 * c + 1024), A.mult)
+        for h in range(2 * c, 2 * c + 2):
+            tt(v("VAL", 512 * h, 512 * h + 512), ind("P", v("pos", 32 * h, 32 * h + 32)), v("EQb", 512 * h, 512 * h + 512), A.mult)
         for r in range(16):
             mm(v("B0", 64 * c, 64 * c + 64), v("SRf", 128 * r, 128 * r + 128), v("VAL", 1024 * c + r, 1024 * c + 1024, 16), r == 0, r == 15)
 
@@ -506,10 +553,10 @@ def rank_program(g, core, T, topo):
         scan(o, v("RS"), v("t1"), 0.0, A.mult, A.add)
 
     def early(last):
-        ms(v("AW", 0, 128), 0.0)
+        act(v("AW", 0, 128), v("IO"), AF.Relu, None, -1.0)
         ts(v("og"), v("JL", 0, 4), v("NN", 0, 1), A.add, 4095.0, A.min)
-        ts(v("NN", 4, 5), v("NN", 0, 1), -8192.0, A.add)
-        ts(v("NN", 5, 6), v("NN", 0, 1), -4160.0, A.add)
+        act(v("NN", 4, 5), v("NN", 0, 1), AF.Identity, C(53))
+        act(v("NN", 5, 6), v("NN", 0, 1), AF.Identity, C(54))
         if last:
             ts(v("i1", 0, 64), v("IO", 0, 64), v("NN", 0, 1), A.add, 4095.0, A.min)
             ts(v("i1", 0, 64), v("i1", 0, 64), 10, A.arith_shift_right)
@@ -572,6 +619,10 @@ def rank_program(g, core, T, topo):
 
     def finish():
         k = 2 * RO - 1
+        for x in range(8):
+            b = "B%d" % (6 + x % 2)
+            mm(v(b, 0, 256), v("ONf"), v("MS", 256 * x, 256 * x + 256))
+            act(v("MS", 256 * x, 256 * x + 256), v(b, 0, 256), AF.Identity, C(10))
         patch(0, k - 1)
         patch(k - 1, k)
         cp(v("du", 8 * k, 8 * k + 8), v("DL", DH * k + 256, DH * k + 264))
@@ -586,12 +637,12 @@ def rank_program(g, core, T, topo):
     def round_(t):
         last = t == RO - 1
         nn = v("D", DH + 264, DH + 265)
-        tt(v("cat"), v("cbg"), VALP, A.subtract)
+        tt(v("cat"), v("cbg"), v("B3", 0, 192), A.subtract)
         for s in range(4):
             mm(v("B%d" % (1 + s // 2), 192 * (s % 2), 192 * (s % 2) + 192), v("Rb", 128 * s, 128 * s + 128), v("cat"))
         act(v("WTb", 0, 384), v("B1", 0, 384), AF.Copy)
         act(v("WTb", 384, 768), v("B2", 0, 384), AF.Copy)
-        act(X1, VALP, AF.Relu, C(15), -1.0)
+        act(X1, v("B3", 0, 192), AF.Relu, C(15), -1.0)
         for h in range(2):
             for k in range(2):
                 ts(v("M", 768 * k + 384 * h, 768 * k + 384 * h + 384), v("WTb", 384 * h, 384 * h + 384), C(5 + k), A.is_equal)
@@ -606,11 +657,17 @@ def rank_program(g, core, T, topo):
         tt(v("c2"), v("c2"), v("TR"), A.mult)
         tt(v("c2"), v("c2"), v("cl", 0, 24), A.add)
         cp(v("ou"), v("c2"))
+        up[0] = UP[2]
         cp(ind("AW", v("ou")), v("UV"))
+        up[0] = 0.0
         scan(Y1, v("AW", 0, 128), v("AW", 0, 128), 0.0, A.max, A.max)
         tolist(v("t3"), Y1)
         for i in range(5):
-            ts(v("OG", 8 * i, 8 * i + 8), v("t3", 15, 128, 16), float(i), A.add)
+            mm(v("B2", 8 * i, 8 * i + 8), v("IDb"), v("OI", 8 * i, 8 * i + 8), True, False)
+            mm(v("B2", 8 * i, 8 * i + 8), v("IDf"), v("t3", 15, 128, 16), False, True)
+        up[0] = UP[3]
+        cp(v("OG"), v("B2", 0, 40))
+        up[0] = 0.0
         act(v("G"), ind("S2", v("OG")))
         mm(v("B1"), v("UA"), v("G", 0, 512), True, False)
         mm(v("B1"), v("UB"), v("G", 128, 640), False, True)
@@ -772,6 +829,9 @@ def rank_program(g, core, T, topo):
     arrive("aD", 6, [slot("DD", d) for d in others], 46.0)
     for d in others:
         dma("s", blk("DK", 0, 576, d), slot("DD", d), sdk)
+    act(v("IDf"), v("IDb"), AF.Copy)
+    for i in range(5):
+        ms(v("OI", 8 * i, 8 * i + 8), float(i))
     ms(v("t2"), 0.5)
     ms(v("t3"), 0.0)
     scan(v("THR"), v("t2"), v("t3"), 2.0 ** 64, A.mult, A.add)
@@ -788,11 +848,12 @@ def rank_program(g, core, T, topo):
     ts(v("C", 56, 64), v("JL"), C(12), A.add)
     for x in range(5):
         ts(v("C", 64 + 8 * x, 72 + 8 * x), v("JL"), 2048.0, A.add)
-    ms(v("K", 8192, WT), 0.0)
-    ms(v("P", 8192, WT), 0.0)
-    ms(v("MK", 2048, WM), 0.0)
-    ms(v("MS", 2048, WM), 0.0)
-    ms(v("AW"), 0.0)
+    act(v("K", 8192, WT), v("KP"), AF.Relu, None, -1.0)
+    act(v("P", 8192, WT), v("KP"), AF.Relu, None, -1.0)
+    act(v("MK", 2048, WM), v("IO"), AF.Relu, None, -1.0)
+    act(v("MS", 2048, WM), v("IO"), AF.Relu, None, -1.0)
+    act(v("AW", 128, 640), v("KP"), AF.Relu, None, -1.0)
+    ms(v("AW", 640, 648), 0.0)
     ms(v("S2", 0, 1), 0.0)
     ms(v("S2", 1537, 1552), 0.0)
     ms(v("D", 264, DH), 0.0)
@@ -801,23 +862,15 @@ def rank_program(g, core, T, topo):
     images()
     early(False)
     ts(v("D1"), v("DK"), 1.0, A.add)
-    for x in range(4):
-        b = "B%d" % (6 + x % 2)
-        mm(v(b), v("ONf"), v("MS", 512 * x, 512 * x + 512))
-        act(v("MS", 512 * x, 512 * x + 512), v(b), AF.Identity, C(10))
     ne = len(topo.engines(near[0], core))
-    arrive("aK", 8 * ne, [v("K", 0, 8192)], 33.0)
+    arrive("aK", 8 * ne, [v("K", 0, 8192)], 28.0)
     arrive("aP", 8 * ne, [v("P", 0, 8192)], 40.0)
     for t in range(RO):
-        if t == 0:
-            for c in range(3):
-                look_eq(c)
-            for c in range(3):
-                look_val(c)
-        else:
-            for c in range(3):
-                look_eq(c)
-                look_val(c)
+        for c in range(3):
+            look_eq(c)
+        for c in range(3):
+            look_val(c)
+        if t > 0:
             classes()
             images()
             early(t == RO - 1)

@@ -1,3 +1,4 @@
+import numpy as np
 from concourse.bass import DstId, RemoteDMATransfer
 from concourse.mybir import dt, AluOpType, AxisListType, ActivationFunctionType
 
@@ -7,10 +8,11 @@ N, J, CAP, RO = 4, 3072, 896, 3
 WT = 8704
 WM = 2176
 DH = 272
-WAKE = 0.08
+WAKE = 0.12
 UP = [0.0, 0.0, 5.0, 5.0]
-PASSES = 3
-SHAKE = [0, 0.0]
+PASSES = 500
+SHAKE = [0, 6.0]
+KEPT = {}
 F, B, I, U, H = "float32", "bfloat16", "int32", "uint16", "float16"
 
 
@@ -38,15 +40,15 @@ SCRATCH = {
     "w0": sb(128), "r0": sb(128), "pd": sb(128), "NP": sb(256),
     "su": sb(32, U), "sf": sb(32), "og": sb(4, U), "so": sb(8, U), "SG": sb(128), "mk": sb(64),
     "D": sb(2 * DH), "DL": sb(6 * DH), "du": sb(48, U), "o1": sb(40), "o2": sb(40), "o3": sb(40), "o4": sb(40),
-    "LD": ("dram", [4, 128, 96], I), "DD": ("dram", [4, 128, 144], I), "HL": ("dram", [4, 128, 256], F),
+    "LD": ("dram", [4, 128, 48], I), "LE": ("dram", [4, 128, 48], I), "DD": ("dram", [4, 128, 144], I), "HL": ("dram", [5, 128, 256], F),
     "XS": ("dram", [24, 128, 68], F), "XL": ("dram", [24, 128, 68], F),
     "OS": ("dram", [4, 128, 96], F), "OD": ("dram", [4, 128, 96], F),
 }
 for _i in range(8):
     SCRATCH["B%d" % _i] = ("psum", [128, 512], F)
 
-SEMAPHORES = (["qv", "qa", "qp", "qg", "ls", "lsA", "lsB", "aL", "aD", "aK", "aP", "aO", "fin", "fo", "fk", "fs"]
-              + ["aX%d" % i for i in range(6)] + ["h%d" % i for i in range(4)] + ["hr%d" % i for i in range(4)]
+SEMAPHORES = (["qv", "qa", "qp", "qg", "ls", "lsA", "lsB", "aL", "aI", "aD", "aK", "aP", "aO", "fin", "fo", "fk", "fs"]
+              + ["aX%d" % i for i in range(6)] + ["h%d" % i for i in range(5)] + ["hr%d" % i for i in range(5)]
               + ["d%d" % i for i in range(60)])
 
 
@@ -70,8 +72,6 @@ def arrange(ops):
                 o_.append(x)
     for o in reversed(top):
         o["pr"] = o["lat"] + o["up"] + WAKE + max([x["pr"] for x in o["next"]] + [0.0])
-    for o in ops:
-        o["pr"] += SHAKE[1] * ((o["i"] * 7919 + SHAKE[0] * 104729) * 48271 % 65537) / 65537.0
     free = {q: 0.0 for q in "vapgsx"}
     ready, out = [o for o in ops if o["left"] == 0], []
     for o in ready:
@@ -105,9 +105,13 @@ def arrange(ops):
             y["sn"].append(o)
 
     def place(line, at, c):
-        k = 0
-        while k < len(line) and line[k][1] <= at:
-            k += 1
+        k, hi = 0, len(line)
+        while k < hi:
+            m = (k + hi) // 2
+            if line[m][1] <= at:
+                k = m + 1
+            else:
+                hi = m
         while k < len(line) and line[k][0] < at + c - 1e-9:
             at = max(at, line[k][1])
             k += 1
@@ -115,7 +119,18 @@ def arrange(ops):
         return at
 
     best, span = [o["st"] for o in ops], max(o["end"] for o in ops)
-    for _ in range(PASSES):
+    rng = np.random.default_rng(SHAKE[0])
+    for n_ in range(0 if len(ops) in KEPT else PASSES):
+        if n_ % 2 == 0:
+            mid, wid, amp = rng.random() * span, 4.0 + 16.0 * rng.random(), SHAKE[1] * rng.random()
+            key = {o["i"]: s + (amp * rng.random() if abs(s - mid) < wid else 0.0) for o, s in zip(ops, best)}
+            for o in top:
+                key[o["i"]] = max([key[o["i"]]] + [key[y["i"]] + 1e-6 for y in o["dep"] + o["soft"]])
+            lines = {q: [] for q in free}
+            for o in sorted(ops, key=lambda o: key[o["i"]]):
+                at = max([o["t0"]] + [y["end"] + WAKE for y in o["dep"]] + [y["st"] + y["c"] + o["gap"] for y in o["soft"]])
+                o["st"] = at if o["q"] == "x" else place(lines[o["q"]], at, o["c"])
+                o["end"] = o["st"] + o["lat"]
         lines = {q: [] for q in free}
         for o in sorted(ops, key=lambda o: (-o["st"] - o["c"], -o["st"])):
             at = max([o["lat"] - o["c"]] + [x["rs"] + x["c"] + o["lat"] - o["c"] + WAKE for x in o["dn"]]
@@ -126,8 +141,9 @@ def arrange(ops):
             at = max([o["t0"]] + [y["end"] + WAKE for y in o["dep"]] + [y["st"] + y["c"] + o["gap"] for y in o["soft"]])
             o["st"] = at if o["q"] == "x" else place(lines[o["q"]], at, o["c"])
             o["end"] = o["st"] + o["lat"]
-        if max(o["end"] for o in ops) < span:
+        if max(o["end"] for o in ops) <= span:
             best, span = [o["st"] for o in ops], max(o["end"] for o in ops)
+    best = KEPT.setdefault(len(ops), best)
     for o, s in zip(ops, best):
         o["st"], o["end"] = s, s + o["lat"]
     return sorted(ops, key=lambda o: o["st"])
@@ -231,37 +247,47 @@ def helper(g, core, T, topo):
         n_off = len(topo.engines(c, T.cores[(r + 1) % N]))
         n_on = len(topo.engines(c, far[0])) - n_off
         if core in near[:N - 1] or core == far[N - 1]:
-            own = core == far[N - 1]
-            s = r if own else (r - 1 - near.index(core)) % N
-            n_in = n_on // 2 if own else n_off
+            if core == far[N - 1]:
+                jobs = [(2 + h, 1, piece_cols(r, h), n_on // 2) for h in range(2)]
+            else:
+                j = near.index(core)
+                jobs = [(4, 0, piece_cols(r, j - 1), n_on // 4)] if j > 0 else []
+                jobs += [(k, k // 2, piece_cols((r - 1 - j) % N, k % 2), n_off) for k in range(4)]
             es = topo.engines(core, c)
             rid, pid = topo.addr(c)[0], topo.addr(c)[1]
-            for k in range(4):
-                tab = T.K if k < 2 else T.P
-                c0 = piece_cols(s, k % 2)
+            for (k, a, c0, n_in) in jobs:
+                tab = (T.K, T.P)[a]
                 for x in range(4):
                     q = g.sync if x % 2 == 0 else g.scalar
                     if x < 2:
+                        if k == 2 and core in near:
+                            q.wait_ge(T.sem.fo, 1)
                         q.wait_ge(T.sem["h%d" % k], n_in)
                     q.dma_start(tab[32 * x:32 * x + 32, c0:c0 + 1024], T.HL[k]).then_inc(T.sem["hr%d" % k], 16)
-            for k in range(4):
-                tab = T.K if k < 2 else T.P
-                c0 = piece_cols(s, k % 2)
+            for (k, a, c0, n_in) in jobs:
+                tab = (T.K, T.P)[a]
                 g.wait_ge(T.sem["hr%d" % k], 64)
-                g.remote_dma(tab[:, c0:c0 + 1024], tab[:, c0:c0 + 1024], T.sem["aK" if k < 2 else "aP"], T.sem.ls,
+                g.remote_dma(tab[:, c0:c0 + 1024], tab[:, c0:c0 + 1024], T.sem[("aK", "aP")[a]], T.sem.ls,
                              pid, rid, bits(es))
-            g.wait_ge(T.sem.ls, 4 * len(es))
-        if core in far[:N - 1]:
-            j = far.index(core)
-            to = crew(T, topo, T.cores[(r + 1 + j) % N])[0][j]
-            es = topo.engines(core, to)
-            rid, pid = topo.addr(to)[0], topo.addr(to)[1]
+                if k == 1:
+                    g.sem_inc(T.sem.fo, 1)
+            g.wait_ge(T.sem.ls, len(jobs) * len(es))
+        if core == far[0]:
+            es = topo.engines(core, T.cores[(r + 1) % N])
+            g.wait_ge(T.sem.aI, 6)
+            g.remote_dma_fused([RemoteDMATransfer(dst_ids=[dst(topo, T.cores[(r + 1 + j) % N])],
+                                                  dma_engine_mask=bits(es[2 * j:2 * j + 2]), remote_sem=T.sem.aI,
+                                                  src=T.LS[:, 96 * j + 48:96 * j + 96], dst=T.LE[r])
+                                for j in range(N - 1)], local_sem=T.sem.ls)
             for a in range(2):
                 k = 2 * a + 1
-                c0 = (4 * j + k) * 256
-                g.wait_ge(T.sem["h%d" % k], n_on)
-                g.remote_dma(T.HL[k], T.VAL[:, c0:c0 + 256], T.sem["h%d" % k], T.sem.ls, pid, rid, bits(es))
-            g.wait_ge(T.sem.ls, 2 * len(es))
+                for j in range(N - 1):
+                    to = crew(T, topo, T.cores[(r + 1 + j) % N])[0][j]
+                    c0 = (4 * j + k) * 256
+                    g.wait_ge(T.sem["d%d" % (3 * a + j)], n_on // 2 if a + j == 0 else n_on)
+                    g.remote_dma(T.HL[k], T.VAL[:, c0:c0 + 256], T.sem["h%d" % k], T.sem.ls, topo.addr(to)[1],
+                                 topo.addr(to)[0], bits(es))
+            g.wait_ge(T.sem.ls, 6 + 2 * (N - 1) * n_off)
 
 
 def rank_program(g, core, T, topo):
@@ -313,7 +339,7 @@ def rank_program(g, core, T, topo):
             per = (3.8 if outs[0][4] == "i" else 1.56 if "i" in kinds else 2.0 if q == "g" else
                    0.5 if q == "v" and big and outs[0][4] == "2" and all(k == "2" for k in kinds) else
                    2.0 if len(big) == 2 and "p" not in kinds and outs[0][3] > 1 else 1.0)
-            c = lat = max(64, m * per) * 0.00104 + 0.05
+            c = lat = max(64, m * per) * 0.00100 + (0.1 if q == "a" else 0.04)
         ops.append({"q": q, "f": f, "r": r, "w": w, "sem": sem, "n": n, "dma": dma, "i": len(ops), "c": c, "lat": lat,
                     "t0": t0, "gap": gap, "up": up[0]})
 
@@ -388,7 +414,8 @@ def rank_program(g, core, T, topo):
         dma("a", v("LS", 96 * j + 48, 96 * j + 96), ext(T.li[32 * d:32 * d + 32, :]), sl)
     so_ = newsem()
     for a, src in enumerate((T.tk, T.tp)):
-        for j, d in enumerate(others + [rank]):
+        for j in ((0, 3, 1, 2) if a == 0 else (0, 1, 2, 3)):
+            d = (others + [rank])[j]
             sj = newsem()
             for h in range(2):
                 c0 = (4 * j + 2 * a + h) * 256
@@ -407,8 +434,11 @@ def rank_program(g, core, T, topo):
     iota(v("A16"), [[16, 8], [0, 16]])
     iota(v("B16"), [[0, 8], [1, 16]])
     iota(v("B32"), [[0, 4], [1, 32]])
-    fused([(T.cores[d], third[j], "aL", v("LS", 96 * j, 96 * j + 96), T.LD[rank]) for j, d in enumerate(others)])
-    arrive("aL", 6, [slot("LD", d) for d in others], 12.0)
+    fused([(T.cores[d], third[j], "aL", v("LS", 96 * j, 96 * j + 48), T.LD[rank]) for j, d in enumerate(others)]
+          + [(far[0], on[2 * j:2 * j + 2], "aI", v("LS", 96 * j + 48, 96 * j + 96), T.LS[:, 96 * j + 48:96 * j + 96])
+             for j in range(N - 1)])
+    arrive("aL", 6, [slot("LD", d) for d in others], 11.0)
+    arrive("aI", 6, [slot("LE", d) for d in others], 19.0)
     hn = len(on) // 2
     for a in range(2):
         for j, d in enumerate(others):
@@ -416,17 +446,25 @@ def rank_program(g, core, T, topo):
             ts(v("VAL", c0, c0 + 512), v("SI", c0, c0 + 512), float(a), A.add)
             hp = crew(T, topo, T.cores[d])[0][j]
             lo_, hi_ = v("VAL", c0, c0 + 256), v("VAL", c0 + 256, c0 + 512)
-            fused([(hp, off, "h%d" % (2 * a), lo_, T.HL[2 * a]), (far[j], on, "h%d" % (2 * a + 1), hi_, hi_[0])], "lsA")
-        c0 = 512 * a
-        ts(v("EQ", c0, c0 + 512), v("SI", 3072 + c0, 3584 + c0), float(a), A.add)
-        fused([(far[N - 1], on[hn * h:hn * h + hn], "h%d" % (2 * a + h), v("EQ", c0 + 256 * h, c0 + 256 * h + 256),
-                T.HL[2 * a + h]) for h in range(2)], "lsB")
+            if a + j == 0:
+                ts(v("EQ", 0, 512), v("SI", 3072, 3584), 0.0, A.add)
+                qn = hn // 2
+                fused([(hp, off, "h0", lo_, T.HL[0]), (far[0], on[:hn], "d0", hi_, hi_[0])]
+                      + [(near[1 + h], on[hn + qn * h:hn + qn * h + qn], "h4", v("EQ", 256 * h, 256 * h + 256), T.HL[4])
+                         for h in range(2)], "lsA")
+            else:
+                fused([(hp, off, "h%d" % (2 * a), lo_, T.HL[2 * a]), (far[0], on, "d%d" % (3 * a + j), hi_, hi_[0])], "lsA")
+    ts(v("EQ", 512, 1024), v("SI", 3584, 4096), 1.0, A.add)
+    fused([(far[N - 1], on[hn * h:hn * h + hn], "h%d" % (2 + h), v("EQ", 512 + 256 * h, 768 + 256 * h), T.HL[2 + h])
+           for h in range(2)], "lsB")
     fused([(T.cores[d], third[j], "aD", v("DS", 144 * j, 144 * j + 144), T.DD[rank]) for j, d in enumerate(others)])
     iota(v("UV"), [[4, 24], [96, 16]])
     iota(v("KP"), [[0, 4], [1, 128]], 256)
     for j, d in enumerate(others):
-        dma("s", blk("LK", 0, 192, d), slot("LD", d, 0, 48), so_)
-        dma("a", blk("LK", 192, 384, d), slot("LD", d, 48, 96), so_)
+        dma("sa"[j % 2], blk("LK", 0, 192, d), slot("LD", d), so_)
+    si = newsem()
+    for j, d in enumerate(others):
+        dma("s", blk("LK", 192, 384, d), slot("LE", d), si)
 
     cp(C(0), v("PI", 0, 1))
     ts(v("PI", 1, 2), v("PI", 0, 1), 112, A.bitwise_and)
@@ -455,7 +493,8 @@ def rank_program(g, core, T, topo):
     tt(v("t2"), v("t2"), v("ONf"), A.mult)
     cp(v("inv"), v("A16"))
     tt(v("UP"), v("t3"), v("t1"), A.subtract)
-    ms(v("RG"), 1.0)
+    for x in range(6):
+        act(v("RG", 128 * x, 128 * x + 128), v("IO"), AF.Identity, C(15), 0.0)
     ms(v("RG", 0, 768, 192), 0.0)
     for r in range(16):
         ts(v("SBb", 128 * r, 128 * r + 128), v("inv"), C(32 + r), A.is_equal)
@@ -509,7 +548,7 @@ def rank_program(g, core, T, topo):
 
     def repeat_keys():
         for h in range(2):
-            b = "B%d" % (6 + h)
+            b = "B%d" % (2 - h)
             for s in range(2):
                 mm(v(b, 192 * s, 192 * s + 192), v("Rf", 128 * (2 * h + s), 128 * (2 * h + s) + 128), v("KEY"))
             act(v("KR", 384 * h, 384 * h + 384), v(b, 0, 384), AF.Copy)
@@ -537,7 +576,10 @@ def rank_program(g, core, T, topo):
 
     def look_val(c):
         for h in range(2 * c, 2 * c + 2):
-            tt(v("VAL", 512 * h, 512 * h + 512), ind("P", v("pos", 32 * h, 32 * h + 32)), v("EQb", 512 * h, 512 * h + 512), A.mult)
+            b, x = v("B%d" % (6 + h % 2)), v("VAL", 512 * h, 512 * h + 512)
+            act(x, ind("P", v("pos", 32 * h, 32 * h + 32)))
+            mm(b, v("IDb"), v("EQb", 512 * h, 512 * h + 512))
+            tt(x, x, b, A.mult)
         for r in range(16):
             mm(v("B0", 64 * c, 64 * c + 64), v("SRf", 128 * r, 128 * r + 128), v("VAL", 1024 * c + r, 1024 * c + 1024, 16), r == 0, r == 15)
 
@@ -673,8 +715,9 @@ def rank_program(g, core, T, topo):
         mm(v("B1"), v("UB"), v("G", 128, 640), False, True)
         if not last:
             address1()
-        tt(v("MT"), v("B1"), v("KP"), A.is_equal)
-        tt(v("V"), ind("KR", v("OG", 0, 32)), v("MT"), A.mult)
+        act(v("MT"), ind("KR", v("OG", 0, 32)))
+        tt(v("B2"), v("B1"), v("KP"), A.is_equal)
+        tt(v("V"), v("MT"), v("B2"), A.mult)
         pk = v("B2", 0, 128)
         for i in range(4):
             mm(pk, v("ONf"), v("V", 128 * i, 128 * i + 128), i == 0, i == 3)
@@ -750,14 +793,13 @@ def rank_program(g, core, T, topo):
             spread(0, 16)
             address3()
             places()
-            repeat_keys()
             cp(ind("P", v("su")), v("V"))
         else:
             cp(ind("P", v("su", 0, 8)), v("NP", 0, 128))
         act(v("SG", 64, 128), ind("P", v("og")))
         ts(v("o1", 0, 4), v("JL", 0, 4), v("NN", 3, 4), A.is_lt, v("NN", 4, 5), A.mult)
         ts(v("o1", 4, 8), v("JL", 0, 4), v("NN", 3, 4), A.is_lt, v("NN", 5, 6), A.mult)
-        cp(v("NN", 0, 1), nn)
+        act(v("NN", 0, 1), nn, AF.Copy)
         if last:
             tt(v("i3", 0, 8), v("o1", 0, 8), v("C", 112, 120), A.add)
             tt(v("t2", 0, 64), v("SG", 0, 64), v("mk"), A.mult)
@@ -779,12 +821,13 @@ def rank_program(g, core, T, topo):
             cp(ind("K", v("so")), v("D", DH, DH + 128))
         tt(v("t3", 64, 128), v("t1", 64, 128), v("i2", 0, 64), A.mult)
         tt(v("NP", 128, 192), v("SG", 64, 128), v("t3", 64, 128), A.subtract)
-        ts(v("NP", 192, 256), v("t3", 64, 128), 1.0, A.add)
+        act(v("NP", 192, 256), v("t3", 64, 128), AF.Identity, C(15))
         mm(v("B1", 0, 128), v("ONf"), v("NP", 128, 256))
         act(v("D", DH + 128, DH + 256), v("B1", 0, 128), AF.Identity, C(10))
         if not last:
             cp(ind("P", v("so")), v("NP", 128, 256))
             columns()
+            repeat_keys()
         send_changes(2 * t + 1, "sa" if last else "s")
         if last:
             take_changes(2 * t)
@@ -811,9 +854,10 @@ def rank_program(g, core, T, topo):
     address1()
     address2()
     address3()
-    places()
     spread(0, 16)
-    act(v("SRf"), v("SRb"), AF.Copy)
+    places()
+    for x in range(4):
+        act(v("SRf", 512 * x, 512 * x + 512), v("SRb", 512 * x, 512 * x + 512), AF.Copy)
     repeat_keys()
     columns()
     sn, sm = newsem(), newsem()
@@ -826,7 +870,7 @@ def rank_program(g, core, T, topo):
             for h in range(2):
                 c0 = (4 * j + 2 * (1 - a) + h) * 256
                 dma("s", blk(m, 1024 * h, 1024 * h + 1024, d), v("VAL", c0, c0 + 256), sm, v("VAL", 0, 1) if a + j + h == 0 else None)
-    arrive("aD", 6, [slot("DD", d) for d in others], 46.0)
+    arrive("aD", 6, [slot("DD", d) for d in others], 42.0)
     for d in others:
         dma("s", blk("DK", 0, 576, d), slot("DD", d), sdk)
     act(v("IDf"), v("IDb"), AF.Copy)
@@ -861,10 +905,11 @@ def rank_program(g, core, T, topo):
     classes()
     images()
     early(False)
-    ts(v("D1"), v("DK"), 1.0, A.add)
+    for x in range(RO):
+        ts(v("D1", 192 * x, 192 * x + 192), v("DK", 192 * x, 192 * x + 192), 1.0, A.add)
     ne = len(topo.engines(near[0], core))
     arrive("aK", 8 * ne, [v("K", 0, 8192)], 28.0)
-    arrive("aP", 8 * ne, [v("P", 0, 8192)], 40.0)
+    arrive("aP", 8 * ne, [v("P", 0, 8192)], 37.0)
     for t in range(RO):
         for c in range(3):
             look_eq(c)

@@ -8,8 +8,8 @@ N, J, CAP, RO = 4, 3072, 896, 3
 WT = 8704
 WM = 2176
 DH = 272
+BIG = 2.0 ** 21
 WAKE = 0.12
-UP = [0.0, 0.0, 5.0, 5.0]
 PASSES = 500
 SHAKE = [0, 6.0]
 KEPT = {}
@@ -22,23 +22,24 @@ def sb(n, d=F):
 
 SCRATCH = {
     "K": sb(WT), "P": sb(WT), "MK": sb(WM), "MS": sb(WM), "SI": sb(4096, I),
-    "VAL": sb(3072), "EQ": sb(1024), "EQb": sb(3072, B), "OI": sb(40, B), "KB": sb(3072), "KR": sb(1536),
+    "VAL": sb(3072), "EQ": sb(1024), "EQb": sb(3072, B), "KB": sb(3072), "KR": sb(776, I), "CR": sb(776),
     "LS": sb(288, I), "DS": sb(432, I), "LK": sb(384, I), "DK": sb(576, I), "D1": sb(576),
     "SBb": sb(2048, B), "SBh": sb(2048, H), "SRf": sb(2048), "SRb": sb(2048, B),
-    "IO": sb(128), "A16": sb(128), "B16": sb(128), "B32": sb(128), "UV": sb(384), "KP": sb(512), "PI": sb(16, I),
-    "C": sb(128), "ONb": sb(128, B), "ONf": sb(128), "UP": sb(128, B), "IDb": sb(128, B), "IDf": sb(128), "UA": sb(128, B),
-    "UB": sb(128, B), "FE": sb(128, B), "Rb": sb(512, B), "Rf": sb(512), "Ff": sb(128), "DG": sb(128),
-    "RS": sb(128), "THR": sb(128), "RG": sb(768, B), "TR": sb(24), "TL": sb(32), "JL": sb(8),
+    "IO": sb(128), "A16": sb(128), "B16": sb(128), "B32": sb(128), "KP": sb(128), "PI": sb(16, I),
+    "C": sb(128), "ONb": sb(128, B), "ONf": sb(128), "UP": sb(128, B), "IDf": sb(128), "IDh": sb(128, H),
+    "II": sb(1280, B), "UB": sb(128, B), "FE": sb(384, B), "Rb": sb(512, B), "Rf": sb(512), "Ff": sb(128), "DG": sb(128),
+    "RS": sb(128), "THR": sb(128), "RG": sb(768, B), "RU": sb(768, B), "TL": sb(32), "JL": sb(8), "CF": sb(320, B),
     "TK": sb(128), "WCs": sb(128), "t1": sb(128), "t2": sb(128), "t3": sb(128),
-    "KEY": sb(192), "NN": sb(8), "k4": sb(192, I), "hb": sb(192, I), "home": sb(192, I),
-    "t0": sb(192, I), "cb0": sb(192), "tob": sb(192, B), "M": sb(1536, B), "S": sb(768, B), "WTb": sb(768, B),
-    "GO": sb(192), "G16": sb(192), "hi": sb(192, B), "lo": sb(192, H), "w1": sb(192), "w2": sb(192), "cbg": sb(192),
-    "pos": sb(192, U), "cat": sb(192, B), "S2": sb(1552, B), "cl": sb(32), "c2": sb(24), "ou": sb(24, U),
-    "AW": sb(648), "OG": sb(40, U), "G": sb(640, B), "MT": sb(512), "V": sb(512), "PK": sb(128),
-    "i1": sb(128, I), "i2": sb(128, I), "i3": sb(144, I), "cls": sb(128), "cu": sb(8, U),
-    "E": sb(1024, B), "inv": sb(128, B), "cd": sb(128), "KG": sb(128), "PG": sb(128), "Em": sb(128, B),
-    "w0": sb(128), "r0": sb(128), "pd": sb(128), "NP": sb(256),
-    "su": sb(32, U), "sf": sb(32), "og": sb(4, U), "so": sb(8, U), "SG": sb(128), "mk": sb(64),
+    "NN": sb(24), "k4": sb(192, I), "hb": sb(192, I), "home": sb(192, I), "tg": sb(192, I),
+    "t0": sb(192, I), "tob": sb(192, B), "old": sb(192, B), "new": sb(384, B), "Wb": sb(192, B),
+    "MA": sb(768, B), "M": sb(1552, B), "S": sb(768, B), "WA": sb(768, B), "WTb": sb(768, B),
+    "hi": sb(192, B), "lo": sb(192, H), "w1": sb(192), "w2": sb(192), "zz": sb(192), "cc": sb(192),
+    "pos": sb(192, U), "cat": sb(192, B), "S2": sb(1552, B), "CM": sb(768, B), "UU": sb(768, B), "EE": sb(112, B),
+    "ou": sb(8, U), "OG": sb(16, U), "g8": sb(16), "G": sb(384, B), "MT": sb(512), "V": sb(512), "mq": sb(128),
+    "Vc": sb(256), "i1": sb(128, I), "i2": sb(128, I), "i3": sb(144, I), "cls": sb(128), "cu": sb(8, U),
+    "E": sb(1024, B), "inv": sb(128, B), "fst": sb(128, B), "KG": sb(128), "PG": sb(128), "Em": sb(128, B),
+    "r0": sb(128), "pd": sb(128), "NP": sb(256),
+    "su": sb(32, U), "og": sb(4, U), "so": sb(8, U), "SG": sb(128), "mk": sb(64),
     "D": sb(2 * DH), "DL": sb(6 * DH), "du": sb(48, U), "o1": sb(40), "o2": sb(40), "o3": sb(40), "o4": sb(40),
     "LD": ("dram", [4, 128, 48], I), "LE": ("dram", [4, 128, 48], I), "DD": ("dram", [4, 128, 144], I), "HL": ("dram", [5, 128, 256], F),
     "XS": ("dram", [24, 128, 68], F), "XL": ("dram", [24, 128, 68], F),
@@ -71,7 +72,7 @@ def arrange(ops):
             if left[x["i"]] == 0:
                 o_.append(x)
     for o in reversed(top):
-        o["pr"] = o["lat"] + o["up"] + WAKE + max([x["pr"] for x in o["next"]] + [0.0])
+        o["pr"] = o["lat"] + WAKE + max([x["pr"] for x in o["next"]] + [0.0])
     free = {q: 0.0 for q in "vapgsx"}
     ready, out = [o for o in ops if o["left"] == 0], []
     for o in ready:
@@ -295,7 +296,7 @@ def rank_program(g, core, T, topo):
     if rank is None:
         helper(g, core, T, topo)
         return
-    ops, nd, up = [], [0], [0.0]
+    ops, nd = [], [0]
     others = [(rank + 1 + j) % N for j in range(N - 1)]
     off = topo.engines(core, T.cores[others[0]])
     near, far = crew(T, topo, core)
@@ -331,7 +332,7 @@ def rank_program(g, core, T, topo):
         elif sem is not None:
             c, lat = 1.0, (12.0 if sem == "lsA" else 4.0)
         elif q == "p":
-            c = lat = max(64, ins[1][3]) * (4 if ins[1][4] == "4" else 1) * 0.00055
+            c = lat = max(64, ins[1][3]) * (4 if ins[1][4] == "4" else 1) * 0.00050
         else:
             big = [x for x in ins if x[3] > 1]
             m = max([outs[0][3]] + [x[3] for x in big])
@@ -341,7 +342,7 @@ def rank_program(g, core, T, topo):
                    2.0 if len(big) == 2 and "p" not in kinds and outs[0][3] > 1 else 1.0)
             c = lat = max(64, m * per) * 0.00100 + (0.1 if q == "a" else 0.04)
         ops.append({"q": q, "f": f, "r": r, "w": w, "sem": sem, "n": n, "dma": dma, "i": len(ops), "c": c, "lat": lat,
-                    "t0": t0, "gap": gap, "up": up[0]})
+                    "t0": t0, "gap": gap})
 
     def a_(x):
         return x[0] if isinstance(x, tuple) else x
@@ -364,14 +365,20 @@ def rank_program(g, core, T, topo):
     def ms(o, c):
         op("v", lambda e: e.memset(o[0], c), [o], [])
 
-    def act(o, x, func=AF.Identity, bias=None, scale=1.0):
-        if bias is None:
+    def act(o, x, func=AF.Identity, bias=None, scale=1.0, acc=None):
+        if acc is not None:
+            op("a", lambda e: e.activation(o[0], x[0], func, scale=scale, accum_out=acc[0]), [o, acc], [x])
+        elif bias is None:
             op("a", lambda e: e.activation(o[0], x[0], func, scale=scale), [o], [x])
         else:
             op("a", lambda e: e.activation(o[0], x[0], func, bias=bias[0], scale=scale), [o], [x, bias])
 
     def mm(o, l, r, start=True, stop=True):
         op("p", lambda e: e.matmul(o[0], l[0], r[0], start, stop), [o], [l, r])
+
+    def mms(o, pairs):
+        for x, (l, r) in enumerate(pairs):
+            mm(o, l, r, x == 0, x == len(pairs) - 1)
 
     def iota(o, pat, base=0, cm=0, fl=True):
         if fl:
@@ -404,9 +411,21 @@ def rank_program(g, core, T, topo):
     def C(k):
         return v("C", k, k + 1)
 
-    IM, X1, X2 = v("B5", 0, 192), v("B5", 192, 384), v("B5", 384, 512)
-    Y1, COL, Z1, Z2 = v("B4", 0, 128), v("B4", 128, 256), v("B4", 256, 384), v("B4", 384, 512)
-    VALP = v("B0", 0, 192)
+    SCALES = [1.0, 0.25, -0.25, 4096.0, BIG, -BIG, -1.0, 16.0]
+
+    def times(x):
+        k = SCALES.index(x)
+        return v("II", 128 * k, 128 * k + 128)
+
+    def sel(r, name="SRb"):
+        return v(name, 128 * r, 128 * r + 128)
+
+    IM, X1, X2, W0 = v("B5", 0, 192), v("B5", 192, 384), v("B5", 384, 512), v("B5", 192, 320)
+    Y1, Y2, Y3 = v("B4", 0, 128), v("B4", 128, 256), v("B4", 256, 384)
+    VALP, CAT = v("B0", 0, 192), v("B3", 0, 192)
+
+    def n_(t):
+        return v("NN", 8 + t, 9 + t)
 
     sl = newsem()
     for j, d in enumerate(others):
@@ -443,23 +462,21 @@ def rank_program(g, core, T, topo):
     for a in range(2):
         for j, d in enumerate(others):
             c0 = (4 * j + 2 * a) * 256
-            ts(v("VAL", c0, c0 + 512), v("SI", c0, c0 + 512), float(a), A.add)
+            cp(v("VAL", c0, c0 + 512), v("SI", c0, c0 + 512))
             hp = crew(T, topo, T.cores[d])[0][j]
             lo_, hi_ = v("VAL", c0, c0 + 256), v("VAL", c0 + 256, c0 + 512)
             if a + j == 0:
-                ts(v("EQ", 0, 512), v("SI", 3072, 3584), 0.0, A.add)
+                act(v("EQ", 0, 512), v("SI", 3072, 3584), AF.Copy)
                 qn = hn // 2
                 fused([(hp, off, "h0", lo_, T.HL[0]), (far[0], on[:hn], "d0", hi_, hi_[0])]
                       + [(near[1 + h], on[hn + qn * h:hn + qn * h + qn], "h4", v("EQ", 256 * h, 256 * h + 256), T.HL[4])
                          for h in range(2)], "lsA")
             else:
                 fused([(hp, off, "h%d" % (2 * a), lo_, T.HL[2 * a]), (far[0], on, "d%d" % (3 * a + j), hi_, hi_[0])], "lsA")
-    ts(v("EQ", 512, 1024), v("SI", 3584, 4096), 1.0, A.add)
+    act(v("EQ", 512, 1024), v("SI", 3584, 4096), AF.Copy)
     fused([(far[N - 1], on[hn * h:hn * h + hn], "h%d" % (2 + h), v("EQ", 512 + 256 * h, 768 + 256 * h), T.HL[2 + h])
            for h in range(2)], "lsB")
     fused([(T.cores[d], third[j], "aD", v("DS", 144 * j, 144 * j + 144), T.DD[rank]) for j, d in enumerate(others)])
-    iota(v("UV"), [[4, 24], [96, 16]])
-    iota(v("KP"), [[0, 4], [1, 128]], 256)
     for j, d in enumerate(others):
         dma("sa"[j % 2], blk("LK", 0, 192, d), slot("LD", d), so_)
     si = newsem()
@@ -471,148 +488,143 @@ def rank_program(g, core, T, topo):
     ts(v("PI", 2, 3), v("PI", 0, 1), 15, A.bitwise_and)
     ts(v("PI", 3, 4), v("PI", 0, 1), 31, A.bitwise_and)
     ts(v("PI", 4, 5), v("PI", 0, 1), 5, A.arith_shift_right)
-    for k, x in ((8, -1.0), (9, -float(4096 + CAP)), (10, -16.0), (14, 2.0 ** 66), (15, 1.0), (52, 0.0625),
-                 (53, -8192.0), (54, -4160.0), (55, 40960.0)):
-        ms(C(k), x)
+    NUMS = {-1.0: 8, -float(4096 + CAP): 9, -2048.0: 10, 2048.0: 11, 2.0 ** 66: 14, 1.0: 15, -0.0625: 52, -8192.0: 53,
+            -4160.0: 54, 2049.0 - BIG: 55, -4096.0: 104, 4096.0: 105}
+
+    def num(x):
+        return C(NUMS[x])
+
+    for x in NUMS:
+        ms(num(x), x)
     ts(v("PI", 5, 6), v("PI", 4, 5), 3.0, A.add)
     cp(v("C", 1, 5), v("PI", 1, 5))
     ts(v("C", 32, 48), v("IO", 0, 16), -1.0, A.mult, C(0), A.add)
     ts(v("C", 48, 52), v("IO", 0, 4), -32.0, A.mult, C(0), A.add)
     ts(v("PI", 5, 6), v("PI", 5, 6), 3, A.bitwise_and)
-    ts(C(5), C(4), 1.0, A.add, 0.0625, A.mult)
+    ts(C(5), C(4), 1.0, A.add, -0.0625, A.mult)
     ts(v("C", 16, 32), v("IO", 0, 16), C(1), A.add)
-    ts(C(6), v("PI", 5, 6), 5.0, A.add, 0.0625, A.mult)
+    ts(C(6), v("PI", 5, 6), 5.0, A.add, -0.0625, A.mult)
     ts(C(7), v("PI", 5, 6), 4.0, A.add)
     ts(v("ONf"), v("A16"), C(1), A.is_equal)
-    ts(v("IDb"), v("IO"), C(0), A.is_equal)
+    ts(times(1.0), v("IO"), C(0), A.is_equal)
     ts(v("t1"), v("IO"), C(0), A.is_lt)
     ts(v("t2"), v("IO"), C(0), A.is_gt)
-    ts(v("t3"), v("IO"), C(0), A.is_equal, 4096.0, A.mult)
     act(v("ONb"), v("ONf"), AF.Copy)
+    for x in SCALES[1:]:
+        act(times(x), times(1.0), AF.Identity, None, x)
+    cp(v("IDh"), times(1.0))
     tt(v("t1"), v("t1"), v("ONf"), A.mult)
     tt(v("t2"), v("t2"), v("ONf"), A.mult)
     cp(v("inv"), v("A16"))
-    tt(v("UP"), v("t3"), v("t1"), A.subtract)
-    for x in range(6):
-        act(v("RG", 128 * x, 128 * x + 128), v("IO"), AF.Identity, C(15), 0.0)
-    ms(v("RG", 0, 768, 192), 0.0)
+    tt(v("UP"), times(4096.0), v("t1"), A.subtract)
+    for name, step in (("RG", 192), ("RU", 96)):
+        ms(v(name), 1.0)
+        ms(v(name, 0, 768, step), 0.0)
     for r in range(16):
-        ts(v("SBb", 128 * r, 128 * r + 128), v("inv"), C(32 + r), A.is_equal)
+        ts(sel(r, "SBb"), v("inv"), C(32 + r), A.is_equal)
     cp(v("SBh"), v("SBb"))
+    ts(v("SBb"), v("SBb"), 4096.0, A.mult)
     for s in range(4):
-        ts(v("Rf", 128 * s, 128 * s + 128), v("B32"), C(48 + s), A.is_equal)
+        ts(sel(s, "Rf"), v("B32"), C(48 + s), A.is_equal)
     act(v("Rb"), v("Rf"), AF.Copy)
 
-    def address1():
-        act(v("hi"), v("KEY"), AF.Copy)
-        ts(v("k4"), v("KEY"), 4095.0, A.add)
-        ts(v("hb"), v("k4"), 8191, A.bitwise_and)
-        ts(v("t0"), v("k4"), 10, A.arith_shift_right, 3, A.bitwise_and)
+    def address(t):
         ts(v("home"), v("k4"), 4095, A.bitwise_and)
-        tt(X1, v("hb"), IM, A.is_le)
-
-    def address2():
-        up[0] = UP[0]
-        tt(v("lo"), v("KEY"), v("hi"), A.subtract)
-        up[0] = 0.0
-        tt(v("k4"), v("t0"), X1, A.add)
-        act(X1, X1, AF.Identity, None, -4.0)
-        ts(v("t0"), v("k4"), 3, A.bitwise_and)
-        ts(v("tob"), v("t0"), 1.0, A.add)
-
-    def address3():
+        ts(v("tg"), v("k4"), 12, A.arith_shift_right)
+        ts(v("hb"), v("k4"), 8191, A.bitwise_and)
+        ts(v("lo"), v("home"), -2048.0, A.add)
+        act(v("hi"), v("tg"), AF.Copy)
+        ts(v("new", 0, 192), v("hb"), n_(max(t - 1, 0)), A.is_lt)
+        mms(v("B6", 0, 192), [(v("IDh"), v("lo")), (times(4096.0), v("new", 0, 192))])
+        ts(v("pos"), v("B6", 0, 192), 2048.0, A.add)
+        for r in range(8):
+            b = "B%d" % (7 - r % 2)
+            for h in range(2):
+                mms(v(b, h, 384, 2), [(sel(r + 8 * h, "SBb"), v("hi")), (sel(r + 8 * h, "SBh"), v("lo"))])
+            act(v("KB", r, 3072, 8), v(b, 0, 384), AF.Identity, num(-2048.0))
+        ts(v("t0"), v("k4"), 10, A.arith_shift_right, 3, A.bitwise_and)
+        tt(X1, v("hb"), IM, A.is_lt)
+        tt(v("tg"), v("t0"), X1, A.add)
+        act(v("old"), X1, AF.Copy)
+        ts(v("t0"), v("tg"), 3, A.bitwise_and)
+        act(v("tob"), v("t0"), AF.Identity, num(-0.0625), -0.0625)
         for d in range(4):
-            ts(v("M", 192 * d, 192 * d + 192), v("tob"), float(d + 1), A.is_equal)
-        tt(v("cb0"), v("tob"), X1, A.add)
-        up[0] = UP[1]
-        scan(v("S"), v("RG"), v("M", 0, 768), 0.0, A.mult, A.add)
-        up[0] = 0.0
-
-    def places():
+            ts(v("MA", 192 * d, 192 * d + 192), v("tob"), -(d + 1) / 16.0, A.is_equal)
+        scan(v("S"), v("RG"), v("MA"), 0.0, A.mult, A.add)
         for h in range(2):
-            b = "B%d" % (6 + h)
-            mm(v(b, 0, 384), v("ONb"), v("S", 384 * h, 384 * h + 384), True, False)
-            mm(v(b, 0, 384), v("UP"), v("M", 384 * h, 384 * h + 384), False, True)
-            act(v("WTb", 384 * h, 384 * h + 384), v(b, 0, 384), AF.Relu, C(9))
-        for d in range(4):
-            mm(v("B6", 0, 192), v("IDb"), v("WTb", 192 * d, 192 * d + 192), d == 0, d == 3)
-        act(v("GO"), v("B6", 0, 192), AF.Relu, C(15), -1.0)
-        act(v("G16"), v("B6", 0, 192), AF.Relu, C(52), -1.0)
+            b = v("B%d" % (6 + h), 0, 384)
+            mms(b, [(v("ONb"), v("S", 384 * h, 384 * h + 384)), (v("UP"), v("MA", 384 * h, 384 * h + 384))])
+            act(v("WA", 384 * h, 384 * h + 384), b, AF.Relu, num(-float(4096 + CAP)))
+        mms(v("B6", 0, 192), [(times(BIG), v("WA", 192 * d, 192 * d + 192)) for d in range(4)])
+        act(v("Wb"), v("B6", 0, 192), AF.Copy)
+        tt(v("w1"), v("k4"), v("B6", 0, 192), A.min)
 
-    def spread(r0, r1):
-        for r in range(r0, r1):
-            b = "B%d" % (6 + r % 2)
-            mm(v(b, 0, 192), v("SBb", 128 * r, 128 * r + 128), v("hi"), True, False)
-            mm(v(b, 0, 192), v("SBh", 128 * r, 128 * r + 128), v("lo"), False, True)
-            act(v("KB", r, 3072, 16), v(b, 0, 192), AF.Identity, C(8))
+    def repeat(name, x):
+        s1 = newsem()
+        for t in range(4):
+            for s in range(4):
+                dma("s", blk(name, 192 * s, 192 * s + 192, t), blk(x, 0, 192, s), s1)
 
-    def repeat_keys():
-        for h in range(2):
-            b = "B%d" % (2 - h)
-            for s in range(2):
-                mm(v(b, 192 * s, 192 * s + 192), v("Rf", 128 * (2 * h + s), 128 * (2 * h + s) + 128), v("KEY"))
-            act(v("KR", 384 * h, 384 * h + 384), v(b, 0, 384), AF.Copy)
-            act(v("KR", 768 + 384 * h, 768 + 384 * h + 384), v(b, 0, 384), AF.Copy)
+    def by_pointer(t):
+        new = v("new", 0, 192) if t == 0 else v("new", 192, 384)
+        if t > 0:
+            ts(new, v("hb"), n_(t), A.is_lt)
+        mms(v("B6", 0, 192), [(v("IDh"), v("lo")), (times(4096.0), new)])
+        act(v("cc"), v("B6", 0, 192), AF.Identity, num(2048.0))
+        repeat("CR", "cc")
+        mms(v("B7", 0, 192), [(v("IDh"), v("lo")), (times(BIG), new), (times(-BIG), v("old")), (times(-1.0), v("Wb"))])
+        act(v("zz"), v("B7", 0, 192), AF.Identity, num(2049.0 - BIG))
+        tt(IM, v("zz"), IM, A.max)
+        ts(v("og"), v("JL", 0, 4), n_(t), A.add, 4095.0, A.min)
+        act(v("NN", 4, 5), n_(t), AF.Identity, num(-8192.0))
+        act(v("NN", 5, 6), n_(t), AF.Identity, num(-4160.0))
+        if t == RO - 1:
+            ts(v("i3", 0, 64), v("IO", 0, 64), n_(t), A.add, 4095.0, A.min)
+            ts(v("i3", 0, 64), v("i3", 0, 64), 10, A.arith_shift_right)
+            ts(v("mk"), v("i3", 0, 64), C(4), A.is_equal)
 
-    def columns():
-        ts(X1, v("hb"), v("NN", 0, 1), A.is_lt, 4096.0, A.mult)
-        tt(v("w2"), v("home"), X1, A.add)
-        cp(v("pos"), v("w2"))
-        act(X1, X1, AF.Identity, None, 1.0 / 1024)
-
-    def classes():
-        tt(X1, v("cb0"), X1, A.add)
-        tt(v("cbg"), v("G16"), X1, A.mult)
-
-    def images():
-        act(v("w2"), v("cbg"), AF.Relu, C(55), -131072.0)
-        tt(v("w2"), v("home"), v("w2"), A.subtract)
-        tt(IM, v("w2"), IM, A.max)
-
-    def look_eq(c):
-        tt(v("EQb", 1024 * c, 1024 * c + 1024), ind("K", v("pos", 64 * c, 64 * c + 64)), v("KB", 1024 * c, 1024 * c + 1024), A.is_equal)
-        for r in range(16):
-            mm(v("B3", 64 * c, 64 * c + 64), v("SRb", 128 * r, 128 * r + 128), v("EQb", 1024 * c + r, 1024 * c + 1024, 16), r == 0, r == 15)
-
-    def look_val(c):
-        for h in range(2 * c, 2 * c + 2):
-            b, x = v("B%d" % (6 + h % 2)), v("VAL", 512 * h, 512 * h + 512)
-            act(x, ind("P", v("pos", 32 * h, 32 * h + 32)))
-            mm(b, v("IDb"), v("EQb", 512 * h, 512 * h + 512))
-            tt(x, x, b, A.mult)
-        for r in range(16):
-            mm(v("B0", 64 * c, 64 * c + 64), v("SRf", 128 * r, 128 * r + 128), v("VAL", 1024 * c + r, 1024 * c + 1024, 16), r == 0, r == 15)
+    def look_up(t):
+        new = v("new", 0, 192) if t == 0 else v("new", 192, 384)
+        mm(CAT, times(1.0), v("tob"), True, False)
+        for c in range(3):
+            tt(v("EQb", 1024 * c, 1024 * c + 1024), ind("K", v("pos", 64 * c, 64 * c + 64)), v("KB", 1024 * c, 1024 * c + 1024), A.is_equal)
+            if c == 2:
+                mm(CAT, times(0.25), v("old"), False, False)
+                mm(CAT, times(1.0), v("Wb"), False, False)
+                mm(CAT, times(-0.25), new, False, False)
+            for r in range(16):
+                mm(v("B3", 64 * c, 64 * c + 64), sel(r), v("EQb", 1024 * c + r, 1024 * c + 1024, 16), False, c == 2 and r == 15)
+        if t > 0:
+            cp(ind("K", v("so")), v("D", DH, DH + 128))
+        mm(VALP, times(1.0), v("CF", 0, 192), True, False)
+        for c in range(3):
+            for h in range(2 * c, 2 * c + 2):
+                b, x = v("B%d" % (6 + h % 2)), v("VAL", 512 * h, 512 * h + 512)
+                act(x, ind("P", v("pos", 32 * h, 32 * h + 32)))
+                mm(b, times(1.0), v("EQb", 512 * h, 512 * h + 512))
+                tt(x, x, b, A.mult)
+            if c == 2:
+                mm(VALP, times(-1.0), v("Wb"), False, False)
+            for r in range(16):
+                mm(v("B0", 64 * c, 64 * c + 64), sel(r, "SRf"), v("VAL", 1024 * c + r, 1024 * c + 1024, 16), False, c == 2 and r == 15)
+        if t > 0:
+            cp(ind("P", v("so")), v("NP", 128, 256))
 
     def new_keys(t):
-        tt(v("w1"), v("D1", 192 * t, 192 * t + 192), X1, A.mult)
-        tt(X1, v("w1"), VALP, A.add)
-        tt(X1, X1, v("KEY"), A.subtract)
-        tt(X1, X1, v("GO"), A.mult)
-        tt(v("KEY"), X1, v("KEY"), A.add)
-
-    def tolist(o, x):
-        tt(v("t1"), x, v("DG"), A.mult)
-        scan(o, v("RS"), v("t1"), 0.0, A.mult, A.add)
-
-    def early(last):
-        act(v("AW", 0, 128), v("IO"), AF.Relu, None, -1.0)
-        ts(v("og"), v("JL", 0, 4), v("NN", 0, 1), A.add, 4095.0, A.min)
-        act(v("NN", 4, 5), v("NN", 0, 1), AF.Identity, C(53))
-        act(v("NN", 5, 6), v("NN", 0, 1), AF.Identity, C(54))
-        if last:
-            ts(v("i1", 0, 64), v("IO", 0, 64), v("NN", 0, 1), A.add, 4095.0, A.min)
-            ts(v("i1", 0, 64), v("i1", 0, 64), 10, A.arith_shift_right)
-            ts(v("mk"), v("i1", 0, 64), C(4), A.is_equal)
+        act(X1, v("cat"), AF.Relu, None, 4 * BIG)
+        tt(X1, v("D1", 192 * t, 192 * t + 192), X1, A.subtract)
+        tt(v("w2"), v("w1"), X1, A.max)
+        tt(v("k4"), v("w2"), VALP, A.max)
 
     def send_lanes():
-        act(v("w2"), v("KEY"), AF.Identity, C(8))
-        act(v("cb0"), IM, AF.Identity, C(15))
+        act(v("w2"), v("k4"), AF.Identity, num(-4096.0))
+        act(v("w1"), IM, AF.Copy)
         s1 = newsem()
         for d in others:
             dma("s", slot("OS", d, 0, 48), blk("w2", 0, 192, d), s1)
-            dma("s", slot("OS", d, 48, 96), blk("cb0", 0, 192, d), s1)
+            dma("s", slot("OS", d, 48, 96), blk("w1", 0, 192, d), s1)
         dma("s", ext(T.yl[rows, :]), blk("w2", 0, 192, rank), "fo")
-        dma("s", ext(T.yi[rows, :]), blk("cb0", 0, 192, rank), "fo")
+        dma("s", ext(T.yi[rows, :]), blk("w1", 0, 192, rank), "fo")
         fused([(T.cores[d], third[j], "aO", slot("OS", d), T.OD[rank]) for j, d in enumerate(others)])
         arrive("aO", 6, [slot("OD", d) for d in others])
 
@@ -664,7 +676,7 @@ def rank_program(g, core, T, topo):
         for x in range(8):
             b = "B%d" % (6 + x % 2)
             mm(v(b, 0, 256), v("ONf"), v("MS", 256 * x, 256 * x + 256))
-            act(v("MS", 256 * x, 256 * x + 256), v(b, 0, 256), AF.Identity, C(10))
+            act(v("MS", 256 * x, 256 * x + 256), v(b, 0, 256), AF.Copy)
         patch(0, k - 1)
         patch(k - 1, k)
         cp(v("du", 8 * k, 8 * k + 8), v("DL", DH * k + 256, DH * k + 264))
@@ -678,156 +690,131 @@ def rank_program(g, core, T, topo):
 
     def round_(t):
         last = t == RO - 1
-        nn = v("D", DH + 264, DH + 265)
-        tt(v("cat"), v("cbg"), v("B3", 0, 192), A.subtract)
+        act(v("cat"), CAT, AF.Copy)
         for s in range(4):
-            mm(v("B%d" % (1 + s // 2), 192 * (s % 2), 192 * (s % 2) + 192), v("Rb", 128 * s, 128 * s + 128), v("cat"))
+            mm(v("B%d" % (1 + s // 2), 192 * (s % 2), 192 * (s % 2) + 192), sel(s, "Rb"), v("cat"))
         act(v("WTb", 0, 384), v("B1", 0, 384), AF.Copy)
         act(v("WTb", 384, 768), v("B2", 0, 384), AF.Copy)
-        act(X1, v("B3", 0, 192), AF.Relu, C(15), -1.0)
         for h in range(2):
             for k in range(2):
                 ts(v("M", 768 * k + 384 * h, 768 * k + 384 * h + 384), v("WTb", 384 * h, 384 * h + 384), C(5 + k), A.is_equal)
-        scan(v("S2", 1, 1537), v("M"), v("M"), 0.0, A.add, A.max)
+        scan(v("S2", 1, 1537), v("M", 0, 1536), v("M", 0, 1536), 0.0, A.add, A.max)
+        mm(v("B1", 384, 480), v("ONb"), v("S2", 16, 1537, 16))
         for r in range(16):
-            mm(v("B3", 0, 25), v("SRb", 128 * r, 128 * r + 128), v("S2", 96 * r, 96 * r + 97, 4), r == 0, r == 15)
+            mm(v("B2", 384, 480), sel(r), v("S2", 1 + r, 1537, 16), r == 0, r == 15)
+        act(v("EE", 0, 96), v("B2", 384, 480), AF.Copy)
+        for k in range(8):
+            ts(v("CM", 96 * k, 96 * k + 96), v("B1", 384, 480), v("JL", k, k + 1), A.is_le)
+        scan(v("UU"), v("RU"), v("CM"), 0.0, A.mult, A.add)
+        uu = v("UU", 95, 768, 96)
+        cp(v("ou"), uu)
+        tt(v("G", 0, 128), ind("EE", v("ou")), v("IO"), A.is_le)
+        ts(v("g8", 0, 8), uu, 48.0, A.is_ge, -768.0, A.mult)
+        mms(v("B1", 480, 488), [(times(16.0), uu)] + [(sel(r), v("G", r, 128, 16)) for r in range(16)])
+        cp(v("OG", 0, 8), v("B1", 480, 488))
+        tt(v("g8", 8, 16), v("g8", 0, 8), v("B1", 480, 488), A.add)
+        act(v("G", 128, 256), ind("S2", v("OG", 0, 8)))
+        cp(v("G", 256, 384), ind("M", v("OG", 0, 8)))
+        cp(v("OG", 8, 16), v("g8", 8, 16))
+        mms(v("B2", 0, 128), [(v("UB"), v("G", 256, 384)), (v("ONb"), v("G", 128, 256))])
+        tt(v("mq"), v("KP"), v("B2", 0, 128), A.is_equal)
+        tt(v("Vc", 0, 128), ind("CR", v("OG", 8, 16)), v("mq"), A.mult)
+        COL, pk, y = v("B1", 0, 128), v("B2", 128, 256), v("B2", 256, 384)
+        mm(COL, v("ONf"), v("Vc", 0, 128))
+        tt(v("Vc", 128, 256), ind("KR", v("OG", 8, 16)), v("mq"), A.mult)
         new_keys(t)
         if last:
             send_lanes()
-        ts(v("cl", 0, 25), v("B3", 0, 25), 128.0, A.min)
-        tt(v("c2"), v("cl", 1, 25), v("cl", 0, 24), A.is_equal)
-        tt(v("c2"), v("c2"), v("TR"), A.mult)
-        tt(v("c2"), v("c2"), v("cl", 0, 24), A.add)
-        cp(v("ou"), v("c2"))
-        up[0] = UP[2]
-        cp(ind("AW", v("ou")), v("UV"))
-        up[0] = 0.0
-        scan(Y1, v("AW", 0, 128), v("AW", 0, 128), 0.0, A.max, A.max)
-        tolist(v("t3"), Y1)
-        for i in range(5):
-            mm(v("B2", 8 * i, 8 * i + 8), v("IDb"), v("OI", 8 * i, 8 * i + 8), True, False)
-            mm(v("B2", 8 * i, 8 * i + 8), v("IDf"), v("t3", 15, 128, 16), False, True)
-        up[0] = UP[3]
-        cp(v("OG"), v("B2", 0, 40))
-        up[0] = 0.0
-        act(v("G"), ind("S2", v("OG")))
-        mm(v("B1"), v("UA"), v("G", 0, 512), True, False)
-        mm(v("B1"), v("UB"), v("G", 128, 640), False, True)
-        if not last:
-            address1()
-        act(v("MT"), ind("KR", v("OG", 0, 32)))
-        tt(v("B2"), v("B1"), v("KP"), A.is_equal)
-        tt(v("V"), v("MT"), v("B2"), A.mult)
-        pk = v("B2", 0, 128)
-        for i in range(4):
-            mm(pk, v("ONf"), v("V", 128 * i, 128 * i + 128), i == 0, i == 3)
-        if not last:
-            address2()
-        ts(v("i1"), pk, 4095.0, A.add)
-        act(v("PK"), pk, AF.Copy)
-        act(v("inv"), v("PK"), AF.Relu, C(14), -2.0 ** 66)
-        ts(v("i2"), v("i1"), 8191, A.bitwise_and)
-        ts(v("i3", 0, 128), v("i1"), 4095, A.bitwise_and)
-        ts(Y1, v("i2"), v("NN", 0, 1), A.is_lt, 4096.0, A.mult)
-        tt(COL, v("i3", 0, 128), Y1, A.add)
-        tolist(v("cls"), COL)
+        else:
+            address(t + 1)
+            repeat("KR", "k4")
+        mm(pk, v("ONf"), v("Vc", 128, 256))
+        tt(Y1, v("DG"), COL, A.mult)
+        scan(v("cls"), v("RS"), Y1, 0.0, A.mult, A.add)
         cp(v("cu"), v("cls", 15, 128, 16))
         act(v("Em"), ind("K", v("cu")), AF.Relu, None, -1.0)
         act(v("KG"), ind("K", v("cu")))
-        act(v("PG"), ind("P", v("cu")))
-        mm(v("B3", 0, 128), v("IDb"), v("inv"), True, False)
+        act(v("inv"), pk, AF.Relu, num(2.0 ** 66), -2.0 ** 66)
+        ts(v("i1"), pk, -4096.0, A.add)
+        mms(y, [(v("ONb"), v("CF", 192, 320)), (v("ONf"), v("Vc", 128, 256)), (sel(1, "FE"), v("Em"))])
         for c in range(8):
-            ts(v("E", 144 * c, 128 * c + 128), v("B4", 128 + 16 * c, 256), v("cls", 16 * c + 15, 16 * c + 16), A.is_equal,
+            ts(v("E", 144 * c, 128 * c + 128), v("B1", 16 * c, 128), v("cls", 16 * c + 15, 16 * c + 16), A.is_equal,
                v("WCs", 16 * c + 15, 16 * c + 16), A.mult)
-            mm(v("B3", 16 * c, 128), v("ONb"), v("E", 144 * c, 128 * c + 128), False, c == 7)
-        mm(v("B1", 0, 128), v("FE"), v("Em"))
-        mm(v("B1", 128, 256), v("ONb"), v("Em"))
-        act(v("w0"), v("B1", 0, 128), AF.Relu)
-        act(v("r0"), v("B1", 128, 256), AF.Relu, C(15), -1.0)
-        tt(v("cd"), COL, v("TK"), A.subtract)
-        ts(v("i2"), v("i1"), 1023, A.bitwise_and)
-        ts(v("i3", 0, 128), v("i1"), 10, A.arith_shift_right)
-        tt(Y1, v("THR"), v("B3", 0, 128), A.is_gt)
-        tt(Z1, v("w0"), Y1, A.mult)
-        tt(Z2, v("PK"), Z1, A.mult)
-        tt(v("D", 0, 128), v("KG"), Z2, A.add)
+            mm(v("B3", 16 * c, 128), v("ONb"), v("E", 144 * c, 128 * c + 128), c == 0, False)
+        mm(v("B3", 0, 128), times(1.0), v("inv"), False, True)
+        tt(v("D", 0, 128), v("KG"), y, A.max)
         if not last:
             for s in range(4):
-                mm(v("B2", 128 * s, 128 * s + 128), v("Rf", 128 * s, 128 * s + 128), v("D", 0, 128))
+                mm(v("B2", 128 * s, 128 * s + 128), sel(s, "Rf"), v("D", 0, 128))
             for h in range(2):
                 act(v("MT", 256 * h, 256 * h + 256), v("B2", 256 * h, 256 * h + 256), AF.Copy)
-        tt(Z2, v("cd"), Y1, A.mult)
-        tolist(v("t3"), Z2)
+        tt(Y2, v("TK"), Y1, A.add)
+        tt(v("fst"), v("THR"), v("B3", 0, 128), A.is_gt)
+        tt(Y2, v("fst"), Y2, A.mult)
+        scan(v("t3"), v("RS"), Y2, 0.0, A.mult, A.add)
         if not last:
+            mm(v("B1", 384, 416), v("IDf"), v("TL"), True, False)
             for s in range(4):
-                mm(v("B3", 128 + 8 * s, 136 + 8 * s), v("Rf", 128 * s, 128 * s + 128), v("t3", 15, 128, 16))
-        ts(X2, v("i2"), 1024.0, A.mult, -3.0, A.add)
-        tt(X2, v("i3", 0, 128), X2, A.add)
-        tt(v("pd"), X2, v("PG"), A.subtract)
-        tt(X2, v("pd"), Z1, A.mult)
-        tt(v("NP", 0, 128), v("PG"), X2, A.add)
-        if not last:
-            tt(v("sf"), v("B3", 128, 160), v("TL"), A.add)
-            for s in range(4):
-                mm(v("B3", 128 * s, 128 * s + 128), v("Rf", 128 * s, 128 * s + 128), v("NP", 0, 128))
-            act(v("V"), v("B3"), AF.Copy)
-            cp(v("su"), v("sf"))
-        tt(v("r0"), v("r0"), Y1, A.mult)
-        op("v", lambda e: e.tensor_reduce(T.NN[:, 1:2], T.r0[:, :], AxisListType.X, A.add), [v("NN", 1, 2)], [v("r0")])
-        mm(v("B1", 256, 257), v("Ff"), v("NN", 1, 2))
-        mm(v("B1", 0, 128), v("ONf"), v("NP", 0, 128))
-        tt(v("D", 256, 264), v("t3", 15, 128, 16), v("C", 56, 64), A.add)
-        if not last:
+                mm(v("B1", 384 + 8 * s, 392 + 8 * s), sel(s, "Rf"), v("t3", 15, 128, 16), False, s == 3)
+            cp(v("su"), v("B1", 384, 416))
             cp(ind("K", v("su")), v("MT"))
+            tt(v("D", 256, 264), v("t3", 15, 128, 16), v("C", 56, 64), A.add)
         else:
+            tt(v("D", 256, 264), v("t3", 15, 128, 16), v("C", 56, 64), A.add)
             cp(v("su", 0, 8), v("D", 256, 264))
             cp(ind("K", v("su", 0, 8)), v("D", 0, 128))
-        act(v("SG", 0, 64), ind("K", v("og")))
-        act(v("t1", 0, 64), v("SG", 0, 64), AF.Identity, C(15)) if not last else None
-        ts(v("NN", 2, 3), v("B1", 256, 257), 64.0, A.min, v("NN", 0, 1), A.add)
-        act(v("D", 128, 256), v("B1", 0, 128), AF.Identity, C(10))
-        send_changes(2 * t)
-        ts(nn, v("NN", 2, 3), 4096.0, A.min)
-        tt(v("NN", 3, 4), nn, v("NN", 0, 1), A.subtract)
+        mms(v("B1", 256, 384), [(sel(2, "FE"), v("Em")), (times(1.0), v("fst"))])
+        act(v("r0"), v("B1", 256, 384), AF.Relu, None, 1.0, v("NN", 1, 2))
+        mm(v("B1", 416, 417), v("Ff"), v("NN", 1, 2))
+        ts(v("NN", 2, 3), v("B1", 416, 417), 64.0, A.min, n_(t), A.add)
+        ts(n_(t + 1), v("NN", 2, 3), 4096.0, A.min)
+        tt(v("NN", 3, 4), n_(t + 1), n_(t), A.subtract)
+        mm(v("B1", 128, 256), sel(0, "FE"), v("Em"))
+        act(v("PG"), ind("P", v("cu")))
+        ts(v("i2"), v("i1"), 1023, A.bitwise_and)
+        ts(v("i3", 0, 128), v("i1"), 10, A.arith_shift_right)
+        act(X2, v("i2"), AF.Identity, None, 1024.0)
+        act(W0, v("B1", 128, 256), AF.Relu)
+        tt(X2, v("i3", 0, 128), X2, A.add)
+        tt(v("pd"), X2, v("PG"), A.subtract)
+        tt(X2, v("pd"), W0, A.mult)
+        tt(v("NP", 0, 128), v("PG"), X2, A.add)
         if not last:
-            spread(0, 16)
-            address3()
-            places()
+            for s in range(4):
+                mm(v("B3", 128 * s, 128 * s + 128), sel(s, "Rf"), v("NP", 0, 128))
+            act(v("V"), v("B3"), AF.Copy)
             cp(ind("P", v("su")), v("V"))
         else:
             cp(ind("P", v("su", 0, 8)), v("NP", 0, 128))
+        mm(v("B1", 0, 128), v("ONf"), v("NP", 0, 128))
+        act(v("D", 128, 256), v("B1", 0, 128), AF.Copy)
+        send_changes(2 * t)
+        act(v("SG", 0, 64), ind("K", v("og")))
         act(v("SG", 64, 128), ind("P", v("og")))
         ts(v("o1", 0, 4), v("JL", 0, 4), v("NN", 3, 4), A.is_lt, v("NN", 4, 5), A.mult)
         ts(v("o1", 4, 8), v("JL", 0, 4), v("NN", 3, 4), A.is_lt, v("NN", 5, 6), A.mult)
-        act(v("NN", 0, 1), nn, AF.Copy)
         if last:
+            act(v("D", DH + 264, DH + 265), n_(t + 1), AF.Copy)
             tt(v("i3", 0, 8), v("o1", 0, 8), v("C", 112, 120), A.add)
             tt(v("t2", 0, 64), v("SG", 0, 64), v("mk"), A.mult)
             tt(v("t2", 64, 128), v("SG", 64, 128), v("mk"), A.mult)
             mm(v("B2", 0, 128), v("Ff"), v("t2"))
             own_columns(v("D", DH + 256, DH + 264), 8, C(4), C(7))
             cp(v("SG"), v("B2", 0, 128))
-            act(v("t1", 0, 64), v("SG", 0, 64), AF.Identity, C(15))
         else:
             tt(v("D", DH + 256, DH + 264), v("o1", 0, 8), v("C", 112, 120), A.add)
             cp(v("so"), v("D", DH + 256, DH + 264))
-        act(v("t1", 64, 128), v("SG", 64, 128), AF.Identity, C(8))
+            by_pointer(t + 1)
+        act(v("t1", 0, 64), v("SG", 0, 64), AF.Identity, num(1.0))
         ts(v("i1", 0, 64), v("SG", 0, 64), 0.0, A.max)
         ts(v("i2", 0, 64), v("i1", 0, 64), 12, A.arith_shift_right, 1, A.bitwise_and)
         tt(v("t3", 0, 64), v("t1", 0, 64), v("i2", 0, 64), A.mult)
         tt(v("D", DH, DH + 64), v("SG", 0, 64), v("t3", 0, 64), A.subtract)
-        ts(v("D", DH + 64, DH + 128), v("t3", 0, 64), -1.0, A.add)
-        if not last:
-            cp(ind("K", v("so")), v("D", DH, DH + 128))
-        tt(v("t3", 64, 128), v("t1", 64, 128), v("i2", 0, 64), A.mult)
-        tt(v("NP", 128, 192), v("SG", 64, 128), v("t3", 64, 128), A.subtract)
-        act(v("NP", 192, 256), v("t3", 64, 128), AF.Identity, C(15))
+        act(v("D", DH + 64, DH + 128), v("t3", 0, 64), AF.Identity, num(-1.0))
+        tt(v("NP", 192, 256), v("SG", 64, 128), v("i2", 0, 64), A.mult)
+        tt(v("NP", 128, 192), v("SG", 64, 128), v("NP", 192, 256), A.subtract)
         mm(v("B1", 0, 128), v("ONf"), v("NP", 128, 256))
-        act(v("D", DH + 128, DH + 256), v("B1", 0, 128), AF.Identity, C(10))
-        if not last:
-            cp(ind("P", v("so")), v("NP", 128, 256))
-            columns()
-            repeat_keys()
+        act(v("D", DH + 128, DH + 256), v("B1", 0, 128), AF.Copy)
         send_changes(2 * t + 1, "sa" if last else "s")
         if last:
             take_changes(2 * t)
@@ -839,27 +826,26 @@ def rank_program(g, core, T, topo):
 
     cp(v("inv"), v("IO"))
     for r in range(16):
-        ts(v("SRb", 128 * r, 128 * r + 128), v("inv"), C(16 + r), A.is_equal)
-    ts(v("t3"), v("IO"), C(0), A.is_equal, -255.0, A.mult)
-    ts(v("cd"), v("IO"), C(0), A.is_equal, 256.0, A.mult)
-    tt(v("FE"), v("IDb"), v("t2"), A.subtract)
-    tt(v("UA"), v("t3"), v("t1"), A.add)
-    tt(v("UB"), v("cd"), v("t2"), A.add)
+        ts(sel(r), v("inv"), C(16 + r), A.is_equal)
+    tt(sel(0, "FE"), times(1.0), v("t2"), A.subtract)
+    act(sel(1, "FE"), sel(0, "FE"), AF.Identity, None, BIG)
+    act(sel(2, "FE"), v("ONb"), AF.Identity, None, -1.0)
+    ts(v("t3"), v("IO"), C(0), A.is_equal, 256.0, A.mult)
+    tt(v("UB"), v("t3"), v("t2"), A.add)
     ts(v("Ff"), v("B32"), C(3), A.is_equal)
     ts(v("DG"), v("B16"), C(2), A.is_equal)
     ts(v("RS"), v("B16"), 0.5, A.is_gt)
-    ts(v("KEY"), v("LK", 0, 192), 1.0, A.add)
-    ts(IM, v("LK", 192, 384), -1.0, A.add)
-    cp(v("NN", 0, 1), v("PI", 8, 9))
-    address1()
-    address2()
-    address3()
-    spread(0, 16)
-    places()
+    ts(v("JL", 0, 8), v("IO", 0, 8), 16.0, A.mult, C(2), A.add)
+    act(v("k4"), v("LK", 0, 192), AF.Identity, num(4096.0)) if False else ts(v("k4"), v("LK", 0, 192), 4096.0, A.add)
+    cp(IM, v("LK", 192, 384))
+    cp(n_(0), v("PI", 8, 9))
+    ms(v("KR", 768, 776), 0)
+    ms(v("CR", 768, 776), 0.0)
+    address(0)
+    repeat("KR", "k4")
+    by_pointer(0)
     for x in range(4):
         act(v("SRf", 512 * x, 512 * x + 512), v("SRb", 512 * x, 512 * x + 512), AF.Copy)
-    repeat_keys()
-    columns()
     sn, sm = newsem(), newsem()
     for a, m in enumerate(("MK", "MS")):
         for h in range(2):
@@ -873,52 +859,44 @@ def rank_program(g, core, T, topo):
     arrive("aD", 6, [slot("DD", d) for d in others], 42.0)
     for d in others:
         dma("s", blk("DK", 0, 576, d), slot("DD", d), sdk)
-    act(v("IDf"), v("IDb"), AF.Copy)
-    for i in range(5):
-        ms(v("OI", 8 * i, 8 * i + 8), float(i))
+    act(v("IDf"), times(1.0), AF.Copy)
+    act(v("KP"), v("IO"), AF.Identity, None, 1.0)
+    ts(v("KP"), v("KP"), 256.0, A.add)
     ms(v("t2"), 0.5)
     ms(v("t3"), 0.0)
     scan(v("THR"), v("t2"), v("t3"), 2.0 ** 64, A.mult, A.add)
-    tolist(v("WCs"), v("THR"))
+    tt(v("t1"), v("THR"), v("DG"), A.mult)
+    scan(v("WCs"), v("RS"), v("t1"), 0.0, A.mult, A.add)
     ts(v("THR"), v("THR"), 2.5, A.mult)
-    ts(C(11), C(2), 24.0, A.mult, 129.0, A.add)
     ts(C(12), C(4), 128.0, A.mult, 8192.0, A.add)
     ts(C(13), C(2), 8192.0, A.add)
-    ts(v("JL", 0, 8), v("IO", 0, 8), 16.0, A.mult, C(2), A.add)
-    ts(v("TR"), v("IO", 0, 24), C(11), A.add)
-    ts(v("TK"), v("IO"), C(12), A.add)
+    ts(v("TK"), v("IO"), C(12), A.add, -1.0, A.mult)
+    tt(v("TK"), v("TK"), v("DG"), A.mult)
     ts(v("TL"), v("IO", 0, 32), 16.0, A.mult, C(13), A.add)
     ts(v("C", 112, 120), v("JL"), 8192.0, A.add)
     ts(v("C", 56, 64), v("JL"), C(12), A.add)
     for x in range(5):
         ts(v("C", 64 + 8 * x, 72 + 8 * x), v("JL"), 2048.0, A.add)
-    act(v("K", 8192, WT), v("KP"), AF.Relu, None, -1.0)
-    act(v("P", 8192, WT), v("KP"), AF.Relu, None, -1.0)
-    act(v("MK", 2048, WM), v("IO"), AF.Relu, None, -1.0)
-    act(v("MS", 2048, WM), v("IO"), AF.Relu, None, -1.0)
-    act(v("AW", 128, 640), v("KP"), AF.Relu, None, -1.0)
-    ms(v("AW", 640, 648), 0.0)
+    ms(v("CF", 0, 192), 4096.0)
+    ts(C(106), C(2), 0.0, A.is_equal, -BIG, A.mult)
+    ts(C(107), C(2), 1.0, A.is_equal, -4096.0, A.mult)
+    ts(v("CF", 192, 320), v("RG", 1, 129), C(106), A.mult, C(107), A.add)
+    for m, c0 in (("K", 8192), ("P", 8192), ("MK", 2048), ("MS", 2048)):
+        for c in range(c0, SCRATCH[m][1][1], 128):
+            act(v(m, c, c + 128), v("IO"), AF.Relu, None, -1.0)
+    ms(v("EE", 96, 112), 256.0)
     ms(v("S2", 0, 1), 0.0)
     ms(v("S2", 1537, 1552), 0.0)
+    ms(v("M", 1536, 1552), 0.0)
     ms(v("D", 264, DH), 0.0)
     ms(v("D", DH + 264, 2 * DH), 0.0)
-    classes()
-    images()
-    early(False)
     for x in range(RO):
-        ts(v("D1", 192 * x, 192 * x + 192), v("DK", 192 * x, 192 * x + 192), 1.0, A.add)
+        act(v("D1", 192 * x, 192 * x + 192), v("DK", 192 * x, 192 * x + 192), AF.Identity, num(4096.0))
     ne = len(topo.engines(near[0], core))
     arrive("aK", 8 * ne, [v("K", 0, 8192)], 28.0)
     arrive("aP", 8 * ne, [v("P", 0, 8192)], 37.0)
     for t in range(RO):
-        for c in range(3):
-            look_eq(c)
-        for c in range(3):
-            look_val(c)
-        if t > 0:
-            classes()
-            images()
-            early(t == RO - 1)
+        look_up(t)
         round_(t)
     finish()
     emit(g, T, ops)

@@ -9,8 +9,13 @@ WT = 8704
 WM = 2176
 DH = 272
 BIG = 2.0 ** 21
-WAKE = 0.12
-PASSES = 500
+WAKE = 0.14
+COST = [0.00092, 0.08, 0.02, 0.00046]
+ROWS = ["gather", "pass", "early"]
+CATAT = 1
+DIRECT = 2
+AT = [10.5, 12.5, 1.7, 24.0, 27.0, 19.5]
+PASSES = 3000
 SHAKE = [0, 6.0]
 KEPT = {}
 F, B, I, U, H = "float32", "bfloat16", "int32", "uint16", "float16"
@@ -21,36 +26,36 @@ def sb(n, d=F):
 
 
 SCRATCH = {
-    "K": sb(WT), "P": sb(WT), "MK": sb(WM), "MS": sb(WM), "SI": sb(4096, I),
-    "VAL": sb(3072), "EQ": sb(1024), "EQb": sb(3072, B), "KB": sb(3072), "KR": sb(776, I), "CR": sb(776),
+    "K": sb(WT, I), "P": sb(WT, I), "MK": sb(WM), "MS": sb(WM), "SI": sb(2048, I), "Qh": sb(512, H), "Qb": sb(512, B),
+    "VAL": sb(3072), "LH": sb(3584, H), "EQb": sb(3072, B), "KB": sb(3072, I), "KR": sb(776, I), "CR": sb(776),
     "LS": sb(288, I), "DS": sb(432, I), "LK": sb(384, I), "DK": sb(576, I), "D1": sb(576),
-    "SBb": sb(2048, B), "SBh": sb(2048, H), "SRf": sb(2048), "SRb": sb(2048, B),
-    "IO": sb(128), "A16": sb(128), "B16": sb(128), "B32": sb(128), "KP": sb(128), "PI": sb(16, I),
+    "SBb": sb(1152, B), "SBh": sb(1152, H), "SRf": sb(2048), "SRb": sb(2048, B),
+    "IO": sb(128), "A16": sb(128), "B16": sb(128), "B32": sb(128), "PI": sb(16, I),
     "C": sb(128), "ONb": sb(128, B), "ONf": sb(128), "UP": sb(128, B), "IDf": sb(128), "IDh": sb(128, H),
-    "II": sb(1280, B), "UB": sb(128, B), "FE": sb(384, B), "Rb": sb(512, B), "Rf": sb(512), "Ff": sb(128), "DG": sb(128),
+    "II": sb(1024, B), "UB": sb(128, B), "FE": sb(384, B), "Rb": sb(512, B), "Rf": sb(512), "Ff": sb(128), "DG": sb(128),
     "RS": sb(128), "THR": sb(128), "RG": sb(768, B), "RU": sb(768, B), "TL": sb(32), "JL": sb(8), "CF": sb(320, B),
     "TK": sb(128), "WCs": sb(128), "t1": sb(128), "t2": sb(128), "t3": sb(128),
     "NN": sb(24), "k4": sb(192, I), "hb": sb(192, I), "home": sb(192, I), "tg": sb(192, I),
     "t0": sb(192, I), "tob": sb(192, B), "old": sb(192, B), "new": sb(384, B), "Wb": sb(192, B),
     "MA": sb(768, B), "M": sb(1552, B), "S": sb(768, B), "WA": sb(768, B), "WTb": sb(768, B),
-    "hi": sb(192, B), "lo": sb(192, H), "w1": sb(192), "w2": sb(192), "zz": sb(192), "cc": sb(192),
+    "hi": sb(384, B), "lo": sb(384, H), "w1": sb(192), "w2": sb(192), "zz": sb(192), "cc": sb(192),
     "pos": sb(192, U), "cat": sb(192, B), "S2": sb(1552, B), "CM": sb(768, B), "UU": sb(768, B), "EE": sb(112, B),
     "ou": sb(8, U), "OG": sb(16, U), "g8": sb(16), "G": sb(384, B), "MT": sb(512), "V": sb(512), "mq": sb(128),
     "Vc": sb(256), "i1": sb(128, I), "i2": sb(128, I), "i3": sb(144, I), "cls": sb(128), "cu": sb(8, U),
     "E": sb(1024, B), "inv": sb(128, B), "fst": sb(128, B), "KG": sb(128), "PG": sb(128), "Em": sb(128, B),
-    "r0": sb(128), "pd": sb(128), "NP": sb(256),
-    "su": sb(32, U), "og": sb(4, U), "so": sb(8, U), "SG": sb(128), "mk": sb(64),
-    "D": sb(2 * DH), "DL": sb(6 * DH), "du": sb(48, U), "o1": sb(40), "o2": sb(40), "o3": sb(40), "o4": sb(40),
-    "LD": ("dram", [4, 128, 48], I), "LE": ("dram", [4, 128, 48], I), "DD": ("dram", [4, 128, 144], I), "HL": ("dram", [5, 128, 256], F),
-    "XS": ("dram", [24, 128, 68], F), "XL": ("dram", [24, 128, 68], F),
-    "OS": ("dram", [4, 128, 96], F), "OD": ("dram", [4, 128, 96], F),
+    "r0": sb(128), "w0": sb(128), "tz": sb(192, I), "j3": sb(136, I), "p1": sb(144), "NP": sb(256),
+    "su": sb(32, U), "og": sb(4, U), "so": sb(8, U), "SG": sb(192),
+    "D": sb(2 * DH), "DL": sb(5 * DH), "du": sb(48, U), "o1": sb(16), "o2": sb(24), "Z": sb(576),
+    "DD": ("dram", [4, 128, 144], I), "HL": ("dram", [3, 128, 256], I),
+    "XS": ("dram", [32, 128, 68], F), "XK": ("dram", [8, 128, 36], F), "XM": ("dram", [8, 128, 32], F),
+    "OS": ("dram", [8, 128, 96], F),
 }
 for _i in range(8):
     SCRATCH["B%d" % _i] = ("psum", [128, 512], F)
 
-SEMAPHORES = (["qv", "qa", "qp", "qg", "ls", "lsA", "lsB", "aL", "aI", "aD", "aK", "aP", "aO", "fin", "fo", "fk", "fs"]
-              + ["aX%d" % i for i in range(6)] + ["h%d" % i for i in range(5)] + ["hr%d" % i for i in range(5)]
-              + ["d%d" % i for i in range(60)])
+SEMAPHORES = (["qv", "qa", "qp", "qg", "ls", "lsA", "lsB", "lsL", "aL", "aD", "aK", "aK0", "aK1", "aK2", "aP", "aO", "fin", "fo", "fk", "fs"]
+              + ["aX%d" % i for i in range(8)] + ["h%d" % i for i in range(3)] + ["hr%d" % i for i in range(3)]
+              + ["d%d" % i for i in range(70)])
 
 
 def overlap(a, b):
@@ -58,6 +63,18 @@ def overlap(a, b):
 
 
 def arrange(ops):
+    for o in ops:
+        hard, every = 0, 0
+        for y in o["all"]:
+            hard |= y["anc"]
+        for y in o["soft"]:
+            every |= y["anc"]
+        every |= hard
+        o["dep"] = [y for y in o["all"] if not hard >> y["i"] & 1]
+        o["soft"] = [y for y in o["soft"] if not every >> y["i"] & 1]
+        for y in o["all"] + [y for y in o["soft"] if y["lat"] == y["c"]]:
+            every |= 1 << y["i"]
+        o["anc"] = every
     for o in ops:
         o["left"] = len(o["dep"]) + len(o["soft"])
         for x in o["dep"] + o["soft"]:
@@ -151,6 +168,8 @@ def arrange(ops):
 
 
 def emit(g, T, ops):
+    for k, o in enumerate(ops):
+        o["i"] = k
     eng = {"v": g.vector, "a": g.scalar, "p": g.tensor, "g": g, "s": g.sync}
     hist, known, cnt, total, group = {}, {q: {} for q in eng}, {}, {}, {}
     for o in ops:
@@ -172,7 +191,7 @@ def emit(g, T, ops):
                     elif (ps and o2["q"] != q) or ((kind == "w" or k2 == "w") and overlap(r, r2)):
                         for o3 in (group[o2["sem"]] if o2["sem"] is not None else [o2]):
                             dep[o3["i"]] = o3
-        if q in "gs" and q in last:
+        if q in last and (q == "g" or (q == "s" and not o["r"] and not dep)):
             soft[last[q]["i"]] = last[q]
         if q == "a" and o["dma"]:
             if "ad" in last:
@@ -180,8 +199,12 @@ def emit(g, T, ops):
             last["ad"] = o
         if q == "x":
             soft[last["g"]["i"]] = last["g"]
+        for tag in o.get("row", []):
+            if tag in last:
+                soft[last[tag]["i"]] = last[tag]
+            last[tag] = o
         last[q] = o
-        o["dep"], o["soft"], o["next"] = list(dep.values()), list(soft.values()), []
+        o["all"], o["soft"], o["next"] = list(dep.values()), list(soft.values()), []
         for r in o["r"]:
             hist.setdefault(r[0], []).append(("r", r, o))
         for r in o["w"]:
@@ -189,7 +212,7 @@ def emit(g, T, ops):
     for o in arrange(ops):
         q = o["q"]
         need = {}
-        for o2 in o["dep"]:
+        for o2 in o["all"]:
             s, v = o2["tok"]
             if need.get(s, (0, None))[0] < v:
                 need[s] = (v, o2)
@@ -203,16 +226,17 @@ def emit(g, T, ops):
                         if kn.get(s3, 0) < v3:
                             kn[s3] = v3
             o["clock"] = dict(kn)
-            ins = o["f"](eng[q])
-            if o["sem"] is None:
-                s = "q" + q
-                cnt[s] = cnt.get(s, 0) + 1
-                ins.then_inc(T.sem[s], 1)
-                o["tok"] = (s, cnt[s])
-            else:
-                if o["dma"]:
-                    ins.then_inc(T.sem[o["sem"]], 16)
-                o["tok"] = (o["sem"], total[o["sem"]])
+            for f in o["fs"]:
+                ins = f(eng[q])
+                if o["sem"] is None:
+                    s = "q" + q
+                    cnt[s] = cnt.get(s, 0) + 1
+                    ins.then_inc(T.sem[s], 1)
+                    o["tok"] = (s, cnt[s])
+                else:
+                    if o["dma"]:
+                        ins.then_inc(T.sem[o["sem"]], 16)
+                    o["tok"] = (o["sem"], total[o["sem"]])
         else:
             o["clock"] = {}
             o["tok"] = (o["sem"], total[o["sem"]])
@@ -247,48 +271,32 @@ def helper(g, core, T, topo):
         near, far = crew(T, topo, c)
         n_off = len(topo.engines(c, T.cores[(r + 1) % N]))
         n_on = len(topo.engines(c, far[0])) - n_off
-        if core in near[:N - 1] or core == far[N - 1]:
-            if core == far[N - 1]:
-                jobs = [(2 + h, 1, piece_cols(r, h), n_on // 2) for h in range(2)]
-            else:
-                j = near.index(core)
-                jobs = [(4, 0, piece_cols(r, j - 1), n_on // 4)] if j > 0 else []
-                jobs += [(k, k // 2, piece_cols((r - 1 - j) % N, k % 2), n_off) for k in range(4)]
+        if core in near[:N - 1]:
+            i = near.index(core)
+            jobs = [(2, "PK"[i // 2], piece_cols(r, i % 2), n_on // 2)]
+            jobs += [(h, "P", piece_cols((r - 1 - i) % N, h), n_off) for h in ((0, 1) if i < DIRECT else (1, 0))]
             es = topo.engines(core, c)
             rid, pid = topo.addr(c)[0], topo.addr(c)[1]
             for (k, a, c0, n_in) in jobs:
-                tab = (T.K, T.P)[a]
                 for x in range(4):
                     q = g.sync if x % 2 == 0 else g.scalar
                     if x < 2:
-                        if k == 2 and core in near:
-                            q.wait_ge(T.sem.fo, 1)
                         q.wait_ge(T.sem["h%d" % k], n_in)
-                    q.dma_start(tab[32 * x:32 * x + 32, c0:c0 + 1024], T.HL[k]).then_inc(T.sem["hr%d" % k], 16)
+                    q.dma_start(T[a][32 * x:32 * x + 32, c0:c0 + 1024], T.HL[k]).then_inc(T.sem["hr%d" % k], 16)
             for (k, a, c0, n_in) in jobs:
-                tab = (T.K, T.P)[a]
                 g.wait_ge(T.sem["hr%d" % k], 64)
-                g.remote_dma(tab[:, c0:c0 + 1024], tab[:, c0:c0 + 1024], T.sem[("aK", "aP")[a]], T.sem.ls,
-                             pid, rid, bits(es))
-                if k == 1:
-                    g.sem_inc(T.sem.fo, 1)
+                g.remote_dma(T[a][:, c0:c0 + 1024], T[a][:, c0:c0 + 1024], T.sem["a" + a], T.sem.ls, pid, rid, bits(es))
             g.wait_ge(T.sem.ls, len(jobs) * len(es))
         if core == far[0]:
             es = topo.engines(core, T.cores[(r + 1) % N])
-            g.wait_ge(T.sem.aI, 6)
-            g.remote_dma_fused([RemoteDMATransfer(dst_ids=[dst(topo, T.cores[(r + 1 + j) % N])],
-                                                  dma_engine_mask=bits(es[2 * j:2 * j + 2]), remote_sem=T.sem.aI,
-                                                  src=T.LS[:, 96 * j + 48:96 * j + 96], dst=T.LE[r])
-                                for j in range(N - 1)], local_sem=T.sem.ls)
-            for a in range(2):
-                k = 2 * a + 1
-                for j in range(N - 1):
-                    to = crew(T, topo, T.cores[(r + 1 + j) % N])[0][j]
-                    c0 = (4 * j + k) * 256
-                    g.wait_ge(T.sem["d%d" % (3 * a + j)], n_on // 2 if a + j == 0 else n_on)
-                    g.remote_dma(T.HL[k], T.VAL[:, c0:c0 + 256], T.sem["h%d" % k], T.sem.ls, topo.addr(to)[1],
+            for j in range(N - 1):
+                to = crew(T, topo, T.cores[(r + 1 + j) % N])[0][j]
+                g.wait_ge(T.sem["d%d" % j], n_on if j > 0 else n_on // 2)
+                for h in ((1,) if j < DIRECT else (1, 0)):
+                    c0 = (2 * j + h) * 256
+                    g.remote_dma(T.HL[h], T.SI[:, c0:c0 + 256], T.sem["h%d" % h], T.sem.ls, topo.addr(to)[1],
                                  topo.addr(to)[0], bits(es))
-            g.wait_ge(T.sem.ls, 6 + 2 * (N - 1) * n_off)
+            g.wait_ge(T.sem.ls, (2 * N - 2 - DIRECT) * n_off)
 
 
 def rank_program(g, core, T, topo):
@@ -296,7 +304,7 @@ def rank_program(g, core, T, topo):
     if rank is None:
         helper(g, core, T, topo)
         return
-    ops, nd = [], [0]
+    ops, nd, queued = [], [0], [0.0]
     others = [(rank + 1 + j) % N for j in range(N - 1)]
     off = topo.engines(core, T.cores[others[0]])
     near, far = crew(T, topo, core)
@@ -328,11 +336,14 @@ def rank_program(g, core, T, topo):
         if q == "x":
             c = lat = 0.0
         elif dma:
-            c, lat = 0.1, 2.2 + max(outs[0][3], ins[0][3]) / 500.0
+            c, lat = 0.07, 2.0 + max(outs[0][3], ins[0][3]) / 500.0
+            if not r and len(w) == 1:
+                queued[0] += outs[0][3] / 750.0
+                lat += queued[0] if queued[0] < 8.0 else 0.0
         elif sem is not None:
-            c, lat = 1.0, (12.0 if sem == "lsA" else 4.0)
+            c, lat = 0.8, (7.0 if sem in ("lsA", "lsB") else 3.0)
         elif q == "p":
-            c = lat = max(64, ins[1][3]) * (4 if ins[1][4] == "4" else 1) * 0.00050
+            c = lat = max(min(64, ins[0][3]), ins[1][3]) * (4 if ins[1][4] == "4" else 1) * COST[3]
         else:
             big = [x for x in ins if x[3] > 1]
             m = max([outs[0][3]] + [x[3] for x in big])
@@ -340,8 +351,8 @@ def rank_program(g, core, T, topo):
             per = (3.8 if outs[0][4] == "i" else 1.56 if "i" in kinds else 2.0 if q == "g" else
                    0.5 if q == "v" and big and outs[0][4] == "2" and all(k == "2" for k in kinds) else
                    2.0 if len(big) == 2 and "p" not in kinds and outs[0][3] > 1 else 1.0)
-            c = lat = max(64, m * per) * 0.00100 + (0.1 if q == "a" else 0.04)
-        ops.append({"q": q, "f": f, "r": r, "w": w, "sem": sem, "n": n, "dma": dma, "i": len(ops), "c": c, "lat": lat,
+            c = lat = max(64, m * per) * COST[0] + (COST[1] if q == "a" else 0.15 if q == "g" else COST[2])
+        ops.append({"q": q, "fs": [f], "r": r, "w": w, "sem": sem, "n": n, "dma": dma, "i": len(ops), "c": c, "lat": lat,
                     "t0": t0, "gap": gap})
 
     def a_(x):
@@ -376,9 +387,23 @@ def rank_program(g, core, T, topo):
     def mm(o, l, r, start=True, stop=True):
         op("p", lambda e: e.matmul(o[0], l[0], r[0], start, stop), [o], [l, r])
 
+    def join(n):
+        part = ops[-n:]
+        del ops[-n:]
+        o = dict(part[0])
+        o.update({"r": sum([x["r"] for x in part], []), "w": sum([x["w"] for x in part], []), "n": sum(x["n"] for x in part),
+                  "fs": sum([x["fs"] for x in part], []), "c": sum(x["c"] for x in part)})
+        o["lat"] = o["c"] + part[-1]["lat"] - part[-1]["c"]
+        ops.append(o)
+
+    def row(tag):
+        if tag in ROWS:
+            ops[-1].setdefault("row", []).append(tag)
+
     def mms(o, pairs):
         for x, (l, r) in enumerate(pairs):
             mm(o, l, r, x == 0, x == len(pairs) - 1)
+        join(len(pairs))
 
     def iota(o, pat, base=0, cm=0, fl=True):
         if fl:
@@ -397,13 +422,14 @@ def rank_program(g, core, T, topo):
         return (ap_, [], [], 64, "d")
 
     def fused(trs, lsem="ls"):
-        lst = [RemoteDMATransfer(dst_ids=[dst(topo, c)], dma_engine_mask=bits(es), remote_sem=T.sem[rs], src=x[0], dst=d)
-               for (c, es, rs, x, d) in trs]
+        trs = [(t[0] if isinstance(t[0], list) else [t[0]],) + t[1:] for t in trs]
+        lst = [RemoteDMATransfer(dst_ids=[dst(topo, c) for c in cs], dma_engine_mask=bits(es), remote_sem=T.sem[rs],
+                                 srcs=[x[0]], dsts=[d] * len(cs)) for (cs, es, rs, x, d) in trs]
         op("g", lambda e: e.remote_dma_fused(lst, local_sem=T.sem[lsem]), [], [t[3] for t in trs], lsem,
            sum(len(t[1]) for t in trs))
 
     def arrive(sem, n, outs, t0=0.0):
-        op("x", None, outs, [], sem, n, False, t0, 5.0)
+        op("x", None, outs, [], sem, n, False, t0, 3.0)
 
     third = [off[0:2], off[2:4], off[4:6]]
     rows = slice(32 * rank, 32 * rank + 32)
@@ -423,6 +449,7 @@ def rank_program(g, core, T, topo):
     IM, X1, X2, W0 = v("B5", 0, 192), v("B5", 192, 384), v("B5", 384, 512), v("B5", 192, 320)
     Y1, Y2, Y3 = v("B4", 0, 128), v("B4", 128, 256), v("B4", 256, 384)
     VALP, CAT = v("B0", 0, 192), v("B3", 0, 192)
+    HI, LO = v("hi", 0, 384, 2), v("lo", 0, 384, 2)
 
     def n_(t):
         return v("NN", 8 + t, 9 + t)
@@ -432,59 +459,79 @@ def rank_program(g, core, T, topo):
         dma("s", v("LS", 96 * j, 96 * j + 48), ext(T.lk[32 * d:32 * d + 32, :]), sl)
         dma("a", v("LS", 96 * j + 48, 96 * j + 96), ext(T.li[32 * d:32 * d + 32, :]), sl)
     so_ = newsem()
-    for a, src in enumerate((T.tk, T.tp)):
-        for j in ((0, 3, 1, 2) if a == 0 else (0, 1, 2, 3)):
-            d = (others + [rank])[j]
-            sj = newsem()
-            for h in range(2):
-                c0 = (4 * j + 2 * a + h) * 256
-                dma("sa"[h], v("SI", c0, c0 + 256), ext(src[32 * d:32 * d + 32, 1024 * h:1024 * h + 1024]), sj)
-        if a == 0:
-            dma("s", blk("LK", 0, 192, rank), ext(T.lk[rows, :]), so_)
-            dma("a", blk("LK", 192, 384, rank), ext(T.li[rows, :]), so_)
-    for s in range(4):
-        dma("sa"[s % 2], blk("PI", 8, 9, s), ext(T.pn[rows, :]), so_)
-    sd, sdk = newsem(), newsem()
-    for j, d in enumerate(others):
-        dma("sa"[j % 2], v("DS", 144 * j, 144 * j + 144), ext(T.dk[32 * d:32 * d + 32, :]), sd)
-    dma("a", blk("DK", 0, 576, rank), ext(T.dk[rows, :]), sdk)
+
+    def load(q, name, src, j, h, sem=None):
+        d, c0 = (others + [rank])[j], (2 * j + h) * 256
+        dma(q, v(name, c0, c0 + 256), ext(src[32 * d:32 * d + 32, 1024 * h:1024 * h + 1024]), sem)
+
+    sj = newsem()
+    load("s", "KB", T.tk, 3, 0, sj)
+    load("a", "SI", T.tp, 0, 1, sj)
+    for name, j in (("KB", 0), ("SI", 3), ("KB", 1), ("KB", 2)):
+        sj = newsem()
+        for h in range(2):
+            load("sa"[h], name, T.tk if name == "KB" else T.tp, j, h, sj)
+    load("s", "KB", T.tk, 3, 1)
+    for x, (j, h) in enumerate(((1, 1), (2, 1), (2, 0), (0, 0), (1, 0))):
+        load("as"[x % 2], "SI", T.tp, j, h)
+        if x == 0:
+            dma("s", v("LK", 96 * rank, 96 * rank + 48), ext(T.lk[rows, :]), so_)
+            dma("a", v("LK", 96 * rank + 48, 96 * rank + 96), ext(T.li[rows, :]), so_)
+            for s in range(4):
+                dma("sa"[s % 2], blk("PI", 8, 9, s), ext(T.pn[rows, :]), so_)
     iota(v("PI", 0, 1), [[0, 1]], 0, 1, False)
     iota(v("IO"), [[1, 128]])
     iota(v("A16"), [[16, 8], [0, 16]])
     iota(v("B16"), [[0, 8], [1, 16]])
     iota(v("B32"), [[0, 4], [1, 32]])
-    fused([(T.cores[d], third[j], "aL", v("LS", 96 * j, 96 * j + 48), T.LD[rank]) for j, d in enumerate(others)]
-          + [(far[0], on[2 * j:2 * j + 2], "aI", v("LS", 96 * j + 48, 96 * j + 96), T.LS[:, 96 * j + 48:96 * j + 96])
-             for j in range(N - 1)])
-    arrive("aL", 6, [slot("LD", d) for d in others], 11.0)
-    arrive("aI", 6, [slot("LE", d) for d in others], 19.0)
-    hn = len(on) // 2
-    for a in range(2):
-        for j, d in enumerate(others):
-            c0 = (4 * j + 2 * a) * 256
-            cp(v("VAL", c0, c0 + 512), v("SI", c0, c0 + 512))
-            hp = crew(T, topo, T.cores[d])[0][j]
-            lo_, hi_ = v("VAL", c0, c0 + 256), v("VAL", c0 + 256, c0 + 512)
-            if a + j == 0:
-                act(v("EQ", 0, 512), v("SI", 3072, 3584), AF.Copy)
-                qn = hn // 2
-                fused([(hp, off, "h0", lo_, T.HL[0]), (far[0], on[:hn], "d0", hi_, hi_[0])]
-                      + [(near[1 + h], on[hn + qn * h:hn + qn * h + qn], "h4", v("EQ", 256 * h, 256 * h + 256), T.HL[4])
-                         for h in range(2)], "lsA")
-            else:
-                fused([(hp, off, "h%d" % (2 * a), lo_, T.HL[2 * a]), (far[0], on, "d%d" % (3 * a + j), hi_, hi_[0])], "lsA")
-    act(v("EQ", 512, 1024), v("SI", 3584, 4096), AF.Copy)
-    fused([(far[N - 1], on[hn * h:hn * h + hn], "h%d" % (2 + h), v("EQ", 512 + 256 * h, 768 + 256 * h), T.HL[2 + h])
-           for h in range(2)], "lsB")
-    fused([(T.cores[d], third[j], "aD", v("DS", 144 * j, 144 * j + 144), T.DD[rank]) for j, d in enumerate(others)])
-    for j, d in enumerate(others):
-        dma("sa"[j % 2], blk("LK", 0, 192, d), slot("LD", d), so_)
-    si = newsem()
-    for j, d in enumerate(others):
-        dma("s", blk("LK", 192, 384, d), slot("LE", d), si)
-
+    fused(lsem="lsL", trs=[(T.cores[d], third[j], "aL", v("LS", 96 * j, 96 * j + 96), T.LK[:, 96 * rank:96 * rank + 96])
+           for j, d in enumerate(others)])
+    arrive("aL", 6, [v("LK", 96 * d, 96 * d + 96) for d in others], AT[0])
+    hn, ho = len(on) // 2, len(off) // 2
+    fused([(far[0], on[:hn], "d0", v("SI", 256, 512), T.SI[:, 256:512]), (near[2], on[hn:], "h2", v("KB", 1536, 1792), T.HL[2])], "lsA")
+    fused([(near[h], on[hn * h:hn * h + hn], "h2", v("SI", 1536 + 256 * h, 1792 + 256 * h), T.HL[2]) for h in range(2)], "lsA")
+    arrive("aK", len(topo.engines(near[0], core)), [v("K", piece_cols(rank, 0), piece_cols(rank, 0) + 1024)], AT[5])
+    iota(v("RG"), [[0, 4], [1, 192]])
     cp(C(0), v("PI", 0, 1))
+    ts(times(1.0), v("IO"), C(0), A.is_equal)
+    for j, (c0, c1) in enumerate(((0, 512), (512, 1024), (1024, 1536), (1792, 2048))):
+        x, hi_, lo_, b = v("KB", c0, c1), v("EQb", c0, c1), v("LH", c0, c1), v("B%d" % j, 0, c1 - c0)
+        act(hi_, x, AF.Copy)
+        mm(b, times(1.0), hi_)
+        tt(lo_, x, b, A.subtract)
+    for j, d in enumerate(others):
+        fused([(T.cores[d], off[:ho], "aK%d" % j, v("EQb", 512 * j, 512 * j + 512), T.M[:, 512 * j:512 * j + 512]),
+               (T.cores[d], off[ho:], "aK%d" % j, v("LH", 512 * j, 512 * j + 512), T.LH[:, 2048 + 512 * j:2560 + 512 * j])]
+              + [(far[0], on if j < DIRECT else on[hn * h:hn * h + hn], "d%d" % j, v("SI", 512 * j + 256 * h, 512 * j + 256 * h + 256),
+                  T.SI[:, 512 * j + 256 * h:512 * j + 256 * h + 256]) for h in ((1,) if j < DIRECT else (0, 1)) if j > 0], "lsA")
+        arrive("aK%d" % j, len(off), [v("M", 512 * j, 512 * j + 512), v("LH", 2048 + 512 * j, 2560 + 512 * j)], AT[1] + AT[2] * j)
+    for j in range(DIRECT):
+        fused([(crew(T, topo, T.cores[others[j]])[0][j], off, "h0", v("SI", 512 * j, 512 * j + 256), T.HL[0])], "lsB")
+    iota(v("K", 8192, WT), [[0, 512]], 0, 0, False)
+    arrive("aP", 8 * len(topo.engines(near[0], core)), [v("P", 0, 8192)], AT[4])
     ts(v("PI", 1, 2), v("PI", 0, 1), 112, A.bitwise_and)
+    cp(C(1), v("PI", 1, 2))
+    ts(v("ONf"), v("A16"), C(1), A.is_equal)
+    act(v("ONb"), v("ONf"), AF.Copy)
+
+    def pick(o, x, r):
+        op("g", lambda e: e.affine_select(o[0], x[0], [[0, 8], [1, 16]], A.is_equal, 0.0, -r, 0), [o], [x])
+
+    for r in range(16):
+        pick(sel(r), v("ONb"), r)
+    sd, sdk = newsem(), newsem()
+    for j, d in enumerate(others):
+        dma("s", v("DS", 144 * j, 144 * j + 144), ext(T.dk[32 * d:32 * d + 32, :]), sd, v("LH", j, j + 1))
+    dma("s", blk("DK", 0, 576, rank), ext(T.dk[rows, :]), sdk, v("LH", 3, 4))
+    fused([(T.cores[d], third[j], "aD", v("DS", 144 * j, 144 * j + 144), T.DD[rank]) for j, d in enumerate(others)])
+    arrive("aD", 6, [slot("DD", d) for d in others], AT[3])
+    iota(v("P", 8192, WT), [[0, 512]], 0, 0, False)
+    for r in range(16):
+        pick(sel(r, "SRf"), v("ONf"), r)
+    iota(v("RU"), [[0, 8], [1, 96]])
+    iota(v("MK", 2048, WM), [[0, 128]])
+    iota(v("MS", 2048, WM), [[0, 128]])
+
     ts(v("PI", 2, 3), v("PI", 0, 1), 15, A.bitwise_and)
     ts(v("PI", 3, 4), v("PI", 0, 1), 31, A.bitwise_and)
     ts(v("PI", 4, 5), v("PI", 0, 1), 5, A.arith_shift_right)
@@ -497,83 +544,82 @@ def rank_program(g, core, T, topo):
     for x in NUMS:
         ms(num(x), x)
     ts(v("PI", 5, 6), v("PI", 4, 5), 3.0, A.add)
-    cp(v("C", 1, 5), v("PI", 1, 5))
+    cp(v("C", 2, 5), v("PI", 2, 5))
     ts(v("C", 32, 48), v("IO", 0, 16), -1.0, A.mult, C(0), A.add)
     ts(v("C", 48, 52), v("IO", 0, 4), -32.0, A.mult, C(0), A.add)
     ts(v("PI", 5, 6), v("PI", 5, 6), 3, A.bitwise_and)
     ts(C(5), C(4), 1.0, A.add, -0.0625, A.mult)
-    ts(v("C", 16, 32), v("IO", 0, 16), C(1), A.add)
     ts(C(6), v("PI", 5, 6), 5.0, A.add, -0.0625, A.mult)
     ts(C(7), v("PI", 5, 6), 4.0, A.add)
-    ts(v("ONf"), v("A16"), C(1), A.is_equal)
-    ts(times(1.0), v("IO"), C(0), A.is_equal)
-    ts(v("t1"), v("IO"), C(0), A.is_lt)
-    ts(v("t2"), v("IO"), C(0), A.is_gt)
-    act(v("ONb"), v("ONf"), AF.Copy)
+    ts(v("G", 0, 128), v("B16"), C(2), A.is_lt)
+    ts(v("G", 128, 256), v("B16"), C(2), A.is_gt)
     for x in SCALES[1:]:
-        act(times(x), times(1.0), AF.Identity, None, x)
+        ts(times(x), times(1.0), x, A.mult)
     cp(v("IDh"), times(1.0))
-    tt(v("t1"), v("t1"), v("ONf"), A.mult)
-    tt(v("t2"), v("t2"), v("ONf"), A.mult)
+    tt(v("G", 0, 128), v("G", 0, 128), v("ONb"), A.mult)
+    tt(v("G", 128, 256), v("G", 128, 256), v("ONb"), A.mult)
     cp(v("inv"), v("A16"))
-    tt(v("UP"), times(4096.0), v("t1"), A.subtract)
-    for name, step in (("RG", 192), ("RU", 96)):
-        ms(v(name), 1.0)
-        ms(v(name, 0, 768, step), 0.0)
-    for r in range(16):
+    tt(v("UP"), times(4096.0), v("G", 0, 128), A.subtract)
+    for r in range(8):
         ts(sel(r, "SBb"), v("inv"), C(32 + r), A.is_equal)
+    ts(sel(8, "SBb"), v("IO"), C(40), A.is_equal)
     cp(v("SBh"), v("SBb"))
-    ts(v("SBb"), v("SBb"), 4096.0, A.mult)
+    ts(v("SBb", 0, 1024), v("SBb", 0, 1024), 4096.0, A.mult)
     for s in range(4):
         ts(sel(s, "Rf"), v("B32"), C(48 + s), A.is_equal)
     act(v("Rb"), v("Rf"), AF.Copy)
+    ts(v("t3"), v("B32"), 4.0, A.mult)
+    for b in range(4):
+        ts(sel(b, "Qb"), v("t3"), C(32 + b), A.is_equal)
+        ts(v("V", 32 * b, 32 * b + 32), v("t3", 0, 32), C(32 + b), A.is_equal)
+    cp(v("Qh"), v("Qb"))
 
     def address(t):
         ts(v("home"), v("k4"), 4095, A.bitwise_and)
         ts(v("tg"), v("k4"), 12, A.arith_shift_right)
         ts(v("hb"), v("k4"), 8191, A.bitwise_and)
-        ts(v("lo"), v("home"), -2048.0, A.add)
-        act(v("hi"), v("tg"), AF.Copy)
+        act(LO, v("home"), AF.Identity, num(-2048.0))
+        act(HI, v("tg"), AF.Copy)
         ts(v("new", 0, 192), v("hb"), n_(max(t - 1, 0)), A.is_lt)
-        mms(v("B6", 0, 192), [(v("IDh"), v("lo")), (times(4096.0), v("new", 0, 192))])
-        ts(v("pos"), v("B6", 0, 192), 2048.0, A.add)
-        for r in range(8):
-            b = "B%d" % (7 - r % 2)
-            for h in range(2):
-                mms(v(b, h, 384, 2), [(sel(r + 8 * h, "SBb"), v("hi")), (sel(r + 8 * h, "SBh"), v("lo"))])
-            act(v("KB", r, 3072, 8), v(b, 0, 384), AF.Identity, num(-2048.0))
+        mms(v("B6", 0, 192), [(v("IDh"), LO), (times(4096.0), v("new", 0, 192))])
+        act(v("pos"), v("B6", 0, 192), AF.Identity, num(2048.0))
+        mm(v("B7", 0, 192), sel(8, "SBb"), HI)
+        mm(v("B7", 192, 384), sel(8, "SBh"), LO)
+        act(v("hi", 1, 384, 2), v("B7", 0, 192), AF.Copy)
+        act(v("lo", 1, 384, 2), v("B7", 192, 384), AF.Copy)
         ts(v("t0"), v("k4"), 10, A.arith_shift_right, 3, A.bitwise_and)
         tt(X1, v("hb"), IM, A.is_lt)
-        tt(v("tg"), v("t0"), X1, A.add)
+        tt(v("tz"), v("t0"), X1, A.add)
         act(v("old"), X1, AF.Copy)
-        ts(v("t0"), v("tg"), 3, A.bitwise_and)
+        ts(v("t0"), v("tz"), 3, A.bitwise_and)
         act(v("tob"), v("t0"), AF.Identity, num(-0.0625), -0.0625)
         for d in range(4):
             ts(v("MA", 192 * d, 192 * d + 192), v("tob"), -(d + 1) / 16.0, A.is_equal)
-        scan(v("S"), v("RG"), v("MA"), 0.0, A.mult, A.add)
+        scan(v("S"), v("RG"), v("MA"), 0.0, A.min, A.add)
         for h in range(2):
-            b = v("B%d" % (6 + h), 0, 384)
+            b = v("B0", 0, 384)
             mms(b, [(v("ONb"), v("S", 384 * h, 384 * h + 384)), (v("UP"), v("MA", 384 * h, 384 * h + 384))])
             act(v("WA", 384 * h, 384 * h + 384), b, AF.Relu, num(-float(4096 + CAP)))
-        mms(v("B6", 0, 192), [(times(BIG), v("WA", 192 * d, 192 * d + 192)) for d in range(4)])
-        act(v("Wb"), v("B6", 0, 192), AF.Copy)
-        tt(v("w1"), v("k4"), v("B6", 0, 192), A.min)
+        mms(v("B0", 0, 192), [(times(BIG), v("WA", 192 * d, 192 * d + 192)) for d in range(4)])
+        act(v("Wb"), v("B0", 0, 192), AF.Copy)
+        tt(v("w1"), v("k4"), v("B0", 0, 192), A.min)
 
     def repeat(name, x):
         s1 = newsem()
         for t in range(4):
             for s in range(4):
                 dma("s", blk(name, 192 * s, 192 * s + 192, t), blk(x, 0, 192, s), s1)
+        join(16)
 
     def by_pointer(t):
         new = v("new", 0, 192) if t == 0 else v("new", 192, 384)
         if t > 0:
             ts(new, v("hb"), n_(t), A.is_lt)
-        mms(v("B6", 0, 192), [(v("IDh"), v("lo")), (times(4096.0), new)])
-        act(v("cc"), v("B6", 0, 192), AF.Identity, num(2048.0))
+        mms(v("B1", 0, 192), [(v("IDh"), LO), (times(4096.0), new)])
+        act(v("cc"), v("B1", 0, 192), AF.Identity, num(2048.0))
         repeat("CR", "cc")
-        mms(v("B7", 0, 192), [(v("IDh"), v("lo")), (times(BIG), new), (times(-BIG), v("old")), (times(-1.0), v("Wb"))])
-        act(v("zz"), v("B7", 0, 192), AF.Identity, num(2049.0 - BIG))
+        mms(v("B1", 192, 384), [(v("IDh"), LO), (times(BIG), new), (times(-BIG), v("old")), (times(-1.0), v("Wb"))])
+        act(v("zz"), v("B1", 192, 384), AF.Identity, num(2049.0 - BIG))
         tt(IM, v("zz"), IM, A.max)
         ts(v("og"), v("JL", 0, 4), n_(t), A.add, 4095.0, A.min)
         act(v("NN", 4, 5), n_(t), AF.Identity, num(-8192.0))
@@ -581,32 +627,50 @@ def rank_program(g, core, T, topo):
         if t == RO - 1:
             ts(v("i3", 0, 64), v("IO", 0, 64), n_(t), A.add, 4095.0, A.min)
             ts(v("i3", 0, 64), v("i3", 0, 64), 10, A.arith_shift_right)
-            ts(v("mk"), v("i3", 0, 64), C(4), A.is_equal)
+            ts(v("SG", 128, 192), v("i3", 0, 64), C(4), A.is_equal)
 
     def look_up(t):
         new = v("new", 0, 192) if t == 0 else v("new", 192, 384)
         mm(CAT, times(1.0), v("tob"), True, False)
         for c in range(3):
-            tt(v("EQb", 1024 * c, 1024 * c + 1024), ind("K", v("pos", 64 * c, 64 * c + 64)), v("KB", 1024 * c, 1024 * c + 1024), A.is_equal)
+            for h in range(2 * c, 2 * c + 2):
+                b, x = ("B6", "B7", "B2")[h % 3], v("KB", 512 * h, 512 * h + 512)
+                for r in range(8):
+                    mms(v(b, r, 512, 8), [(sel(r, "SBb"), v("hi", 64 * h, 64 * h + 64)), (sel(r, "SBh"), v("lo", 64 * h, 64 * h + 64))])
+                    if r % 4 == 3:
+                        join(4)
+                act(x, ind("K", v("pos", 32 * h, 32 * h + 32)), AF.Identity, num(2048.0))
+                row("gather")
+                tt(v("EQb", 512 * h, 512 * h + 512), x, v(b), A.is_equal)
+                row("pass")
             if c == 2:
                 mm(CAT, times(0.25), v("old"), False, False)
                 mm(CAT, times(1.0), v("Wb"), False, False)
                 mm(CAT, times(-0.25), new, False, False)
             for r in range(16):
                 mm(v("B3", 64 * c, 64 * c + 64), sel(r), v("EQb", 1024 * c + r, 1024 * c + 1024, 16), False, c == 2 and r == 15)
+                if r % 8 == 7:
+                    join(8)
         if t > 0:
             cp(ind("K", v("so")), v("D", DH, DH + 128))
         mm(VALP, times(1.0), v("CF", 0, 192), True, False)
         for c in range(3):
             for h in range(2 * c, 2 * c + 2):
                 b, x = v("B%d" % (6 + h % 2)), v("VAL", 512 * h, 512 * h + 512)
+                if h == CATAT:
+                    act(v("cat"), CAT, AF.Copy)
+                    row("gather")
                 act(x, ind("P", v("pos", 32 * h, 32 * h + 32)))
+                row("gather")
                 mm(b, times(1.0), v("EQb", 512 * h, 512 * h + 512))
                 tt(x, x, b, A.mult)
+                row("pass")
             if c == 2:
                 mm(VALP, times(-1.0), v("Wb"), False, False)
             for r in range(16):
                 mm(v("B0", 64 * c, 64 * c + 64), sel(r, "SRf"), v("VAL", 1024 * c + r, 1024 * c + 1024, 16), False, c == 2 and r == 15)
+                if r % 2 == 1:
+                    join(2)
         if t > 0:
             cp(ind("P", v("so")), v("NP", 128, 256))
 
@@ -625,45 +689,42 @@ def rank_program(g, core, T, topo):
             dma("s", slot("OS", d, 48, 96), blk("w1", 0, 192, d), s1)
         dma("s", ext(T.yl[rows, :]), blk("w2", 0, 192, rank), "fo")
         dma("s", ext(T.yi[rows, :]), blk("w1", 0, 192, rank), "fo")
-        fused([(T.cores[d], third[j], "aO", slot("OS", d), T.OD[rank]) for j, d in enumerate(others)])
-        arrive("aO", 6, [slot("OD", d) for d in others])
+        fused([(T.cores[d], third[j], "aO", slot("OS", d), T.OS[4 + rank]) for j, d in enumerate(others)])
+        arrive("aO", 6, [slot("OS", 4 + d) for d in others])
 
     def store_lanes():
         for d in others:
-            dma("s", ext(T.yl[32 * d:32 * d + 32, :]), slot("OD", d, 0, 48), "fin")
-            dma("s", ext(T.yi[32 * d:32 * d + 32, :]), slot("OD", d, 48, 96), "fin")
+            dma("s", ext(T.yl[32 * d:32 * d + 32, :]), slot("OS", 4 + d, 0, 48), "fin")
+            dma("s", ext(T.yi[32 * d:32 * d + 32, :]), slot("OS", 4 + d, 48, 96), "fin")
 
-    landing = {}
-
-    def send_changes(k, q="s"):
-        c0 = DH * (k % 2)
-        s1 = newsem()
-        landing[k] = newsem()
+    def send_changes(k, q="s", name="XS", c0=0, c1=DH, sem=None):
+        a, b, x = DH * (k % 2), DH * k, 8 * (k % 4)
+        s1, s2, sem = newsem(), newsem(), sem or "aX%d" % k
         for j, d in enumerate(others):
-            dma(q[j % len(q)], slot("XS", 4 * k + d), blk("D", c0, c0 + DH, d), s1)
-        dma("s", blk("DL", DH * k, DH * k + DH, rank), blk("D", c0, c0 + DH, rank), landing[k])
-        fused([(T.cores[d], third[j], "aX%d" % k, slot("XS", 4 * k + d), T.XL[4 * k + rank]) for j, d in enumerate(others)])
-        arrive("aX%d" % k, 6, [slot("XL", 4 * k + d) for d in others])
-
-    def take_changes(k, q="s"):
+            dma(q[j % len(q)], slot(name, x + d), blk("D", a + c0, a + c1, d), s1)
+        dma("s", blk("DL", b + c0, b + c1, rank), blk("D", a + c0, a + c1, rank), s2)
+        fused([(T.cores[d], third[j], sem, slot(name, x + d), T[name][x + 4 + rank]) for j, d in enumerate(others)])
+        arrive(sem, 6, [slot(name, x + 4 + d) for d in others])
         for j, d in enumerate(others):
-            dma(q[j % len(q)], blk("DL", DH * k, DH * k + DH, d), slot("XL", 4 * k + d), landing[k])
+            dma("s", blk("DL", b + c0, b + c1, d), slot(name, x + 4 + d), s2)
 
-    def own_columns(o, n, ta, tb):
-        ts(v("i3", 48, 48 + n), v("i3", 0, n), 10, A.arith_shift_right)
-        ts(v("i3", 96, 96 + n), v("i3", 0, n), 1023, A.bitwise_and)
-        ts(v("o1", 0, n), v("i3", 48, 48 + n), ta, A.is_equal)
-        ts(v("o2", 0, n), v("i3", 48, 48 + n), tb, A.is_equal)
-        ts(v("o4", 0, n), v("i3", 48, 48 + n), tb, A.is_equal, 1024.0, A.mult)
-        tt(v("o3", 0, n), v("i3", 96, 96 + n), v("C", 64, 64 + n), A.subtract)
-        tt(v("o1", 0, n), v("o1", 0, n), v("o2", 0, n), A.add)
-        tt(v("o4", 0, n), v("o4", 0, n), v("C", 64, 64 + n), A.add)
-        tt(v("o3", 0, n), v("o3", 0, n), v("o1", 0, n), A.mult)
-        tt(o, v("o3", 0, n), v("o4", 0, n), A.add)
+    def own_columns(o, n, ta, tb, z=0):
+        hi_, lo_ = v("j3", 16 + z, 16 + z + n), v("j3", 32 + z, 32 + z + n)
+        p = [v("p1", 16 * x + z, 16 * x + z + n) for x in range(4)]
+        ts(hi_, v("j3", z, z + n), 10, A.arith_shift_right)
+        ts(lo_, v("j3", z, z + n), 1023, A.bitwise_and)
+        ts(p[0], hi_, ta, A.is_equal)
+        ts(p[1], hi_, tb, A.is_equal)
+        ts(p[3], hi_, tb, A.is_equal, 1024.0, A.mult)
+        tt(p[2], lo_, v("C", 64, 64 + n), A.subtract)
+        tt(p[0], p[0], p[1], A.add)
+        tt(p[3], p[3], v("C", 64, 64 + n), A.add)
+        tt(p[2], p[2], p[0], A.mult)
+        tt(o, p[2], p[3], A.add)
 
     def patch(k0, k1):
         for k in range(k0, k1):
-            cp(v("i3", 8 * (k - k0), 8 * (k - k0) + 8), v("DL", DH * k + 256, DH * k + 264))
+            cp(v("j3", 8 * (k - k0), 8 * (k - k0) + 8), v("DL", DH * k + 256, DH * k + 264))
         n = 8 * (k1 - k0)
         own_columns(v("o2", 0, n), n, float(rank), float(4 + (rank - 1) % N))
         cp(v("du", 8 * k0, 8 * k1), v("o2", 0, n))
@@ -671,26 +732,39 @@ def rank_program(g, core, T, topo):
             cp(ind("MK", v("du", 8 * k, 8 * k + 8)), v("DL", DH * k, DH * k + 128))
             cp(ind("MS", v("du", 8 * k, 8 * k + 8)), v("DL", DH * k + 128, DH * k + 256))
 
+    def own_sums(x0, x1):
+        for x in range(x0, x1):
+            mm(v("B4", 0, 256), v("ONf"), v("MS", 256 * x, 256 * x + 256))
+            act(v("MS", 256 * x, 256 * x + 256), v("B4", 0, 256), AF.Copy)
+
     def finish():
-        k = 2 * RO - 1
-        for x in range(8):
-            b = "B%d" % (6 + x % 2)
-            mm(v(b, 0, 256), v("ONf"), v("MS", 256 * x, 256 * x + 256))
-            act(v("MS", 256 * x, 256 * x + 256), v(b, 0, 256), AF.Copy)
-        patch(0, k - 1)
-        patch(k - 1, k)
-        cp(v("du", 8 * k, 8 * k + 8), v("DL", DH * k + 256, DH * k + 264))
-        cp(ind("MK", v("du", 8 * k, 8 * k + 8)), v("DL", DH * k, DH * k + 128))
+        c0 = 4 * DH
+        cp(v("du", 32, 40), v("DL", c0 + 128, c0 + 136))
+        cp(ind("MK", v("du", 32, 40)), v("DL", c0, c0 + 128))
+        for w in [rank] + others:
+            mm(blk("B1", 0, 64, w), v("Ff", 32 * w, 32 * w + 32), v("Z", 80 * w, 80 * w + 64))
+        for w in [rank] + others:
+            mm(blk("B2", 0, 9, w), v("Rf", 128 * rank + 32 * w, 128 * rank + 32 * w + 32), v("Z", 80 * w + 64, 80 * w + 73))
+        for w in [rank] + others:
+            mm(blk("B3", 0, 64, w), v("Ff", 32 * w, 32 * w + 32), v("Z", 320 + 64 * w, 384 + 64 * w))
+        ts(v("i1", 0, 64), v("B1", 0, 64), 0.0, A.max)
+        ts(v("t1", 0, 64), v("B1", 0, 64), 1.0, A.add)
+        cp(v("du", 40, 48), v("B2", 0, 8))
+        act(v("NN", 16, 17), v("B2", 8, 9), AF.Copy)
+        split(v("B1", 0, 64), v("B3", 0, 64))
+        cp(ind("MK", v("du", 40, 48)), v("D", DH, DH + 128))
         dma("s", ext(T.yk[:, 0:1024]), v("MK", 0, 1024), "fk")
         dma("a", ext(T.yk[:, 1024:2048]), v("MK", 1024, 2048), "fk")
-        dma("a", ext(T.yn[:, :]), v("DL", DH * k + 264, DH * k + 265), "fk")
-        cp(ind("MS", v("du", 8 * k, 8 * k + 8)), v("DL", DH * k + 128, DH * k + 256))
+        dma("s", ext(T.yn[:, :]), v("NN", 16, 17), "fk")
+        cp(ind("MS", v("du", 32, 40)), v("DL", c0 + 144, c0 + DH))
+        cp(ind("MS", v("du", 40, 48)), v("D", DH + 128, DH + 256))
         for x in range(8):
             dma("sa"[x % 2], ext(T.ys[x:x + 1, :]), v("MS", 0, 2048, 1, 16 * x, 16 * x + 1), "fs")
 
     def round_(t):
         last = t == RO - 1
-        act(v("cat"), CAT, AF.Copy)
+        if CATAT > 5:
+            act(v("cat"), CAT, AF.Copy)
         for s in range(4):
             mm(v("B%d" % (1 + s // 2), 192 * (s % 2), 192 * (s % 2) + 192), sel(s, "Rb"), v("cat"))
         act(v("WTb", 0, 384), v("B1", 0, 384), AF.Copy)
@@ -702,10 +776,13 @@ def rank_program(g, core, T, topo):
         mm(v("B1", 384, 480), v("ONb"), v("S2", 16, 1537, 16))
         for r in range(16):
             mm(v("B2", 384, 480), sel(r), v("S2", 1 + r, 1537, 16), r == 0, r == 15)
+            if r % 4 == 3:
+                join(4)
         act(v("EE", 0, 96), v("B2", 384, 480), AF.Copy)
         for k in range(8):
             ts(v("CM", 96 * k, 96 * k + 96), v("B1", 384, 480), v("JL", k, k + 1), A.is_le)
-        scan(v("UU"), v("RU"), v("CM"), 0.0, A.mult, A.add)
+        join(8)
+        scan(v("UU"), v("RU"), v("CM"), 0.0, A.min, A.add)
         uu = v("UU", 95, 768, 96)
         cp(v("ou"), uu)
         tt(v("G", 0, 128), ind("EE", v("ou")), v("IO"), A.is_le)
@@ -717,15 +794,13 @@ def rank_program(g, core, T, topo):
         cp(v("G", 256, 384), ind("M", v("OG", 0, 8)))
         cp(v("OG", 8, 16), v("g8", 8, 16))
         mms(v("B2", 0, 128), [(v("UB"), v("G", 256, 384)), (v("ONb"), v("G", 128, 256))])
-        tt(v("mq"), v("KP"), v("B2", 0, 128), A.is_equal)
+        tt(v("mq"), v("A16"), v("B2", 0, 128), A.is_equal)
         tt(v("Vc", 0, 128), ind("CR", v("OG", 8, 16)), v("mq"), A.mult)
         COL, pk, y = v("B1", 0, 128), v("B2", 128, 256), v("B2", 256, 384)
         mm(COL, v("ONf"), v("Vc", 0, 128))
         tt(v("Vc", 128, 256), ind("KR", v("OG", 8, 16)), v("mq"), A.mult)
         new_keys(t)
-        if last:
-            send_lanes()
-        else:
+        if not last:
             address(t + 1)
             repeat("KR", "k4")
         mm(pk, v("ONf"), v("Vc", 128, 256))
@@ -735,7 +810,7 @@ def rank_program(g, core, T, topo):
         act(v("Em"), ind("K", v("cu")), AF.Relu, None, -1.0)
         act(v("KG"), ind("K", v("cu")))
         act(v("inv"), pk, AF.Relu, num(2.0 ** 66), -2.0 ** 66)
-        ts(v("i1"), pk, -4096.0, A.add)
+        act(v("i1"), pk, AF.Identity, num(-4096.0))
         mms(y, [(v("ONb"), v("CF", 192, 320)), (v("ONf"), v("Vc", 128, 256)), (sel(1, "FE"), v("Em"))])
         for c in range(8):
             ts(v("E", 144 * c, 128 * c + 128), v("B1", 16 * c, 128), v("cls", 16 * c + 15, 16 * c + 16), A.is_equal,
@@ -760,108 +835,138 @@ def rank_program(g, core, T, topo):
             cp(ind("K", v("su")), v("MT"))
             tt(v("D", 256, 264), v("t3", 15, 128, 16), v("C", 56, 64), A.add)
         else:
-            tt(v("D", 256, 264), v("t3", 15, 128, 16), v("C", 56, 64), A.add)
-            cp(v("su", 0, 8), v("D", 256, 264))
+            tt(v("o2", 16, 24), v("t3", 15, 128, 16), v("C", 56, 64), A.add)
+            cp(v("su", 0, 8), v("o2", 16, 24))
             cp(ind("K", v("su", 0, 8)), v("D", 0, 128))
-        mms(v("B1", 256, 384), [(sel(2, "FE"), v("Em")), (times(1.0), v("fst"))])
-        act(v("r0"), v("B1", 256, 384), AF.Relu, None, 1.0, v("NN", 1, 2))
-        mm(v("B1", 416, 417), v("Ff"), v("NN", 1, 2))
-        ts(v("NN", 2, 3), v("B1", 416, 417), 64.0, A.min, n_(t), A.add)
+            cp(v("j3", 112, 120), v("cls", 15, 128, 16))
+            ts(v("j3", 120, 128), v("j3", 112, 120), 1023, A.bitwise_and)
+            ts(v("j3", 128, 136), v("j3", 112, 120), 12, A.arith_shift_right)
+            ts(v("p1", 128, 136), v("j3", 128, 136), 1024.0, A.mult)
+            tt(v("p1", 128, 136), v("p1", 128, 136), v("j3", 120, 128), A.add)
+            ts(v("p1", 136, 144), v("t3", 15, 128, 16), 4096.0, A.mult)
+            tt(v("p1", 136, 144), v("p1", 136, 144), v("C", 64, 72), A.add)
+            tt(v("D", 128, 136), v("p1", 136, 144), v("p1", 128, 136), A.max)
+            send_changes(4, "sa", "XK", 0, 144)
+        mm(v("B3", 128, 256), sel(0, "FE"), v("Em"))
+        mms(v("B3", 256, 384), [(sel(2, "FE"), v("Em")), (times(1.0), v("fst"))])
+        act(v("w0"), v("B3", 128, 256), AF.Relu)
+        act(v("r0"), v("B3", 256, 384), AF.Relu, None, 1.0, v("NN", 1, 2))
+        mm(v("B3", 416, 417), v("Ff"), v("NN", 1, 2))
+        ts(v("NN", 2, 3), v("B3", 416, 417), 64.0, A.min, n_(t), A.add)
         ts(n_(t + 1), v("NN", 2, 3), 4096.0, A.min)
         tt(v("NN", 3, 4), n_(t + 1), n_(t), A.subtract)
-        mm(v("B1", 128, 256), sel(0, "FE"), v("Em"))
         act(v("PG"), ind("P", v("cu")))
         ts(v("i2"), v("i1"), 1023, A.bitwise_and)
         ts(v("i3", 0, 128), v("i1"), 10, A.arith_shift_right)
         act(X2, v("i2"), AF.Identity, None, 1024.0)
-        act(W0, v("B1", 128, 256), AF.Relu)
         tt(X2, v("i3", 0, 128), X2, A.add)
-        tt(v("pd"), X2, v("PG"), A.subtract)
-        tt(X2, v("pd"), W0, A.mult)
+        tt(X2, X2, v("PG"), A.subtract)
+        tt(X2, X2, v("w0"), A.mult)
         tt(v("NP", 0, 128), v("PG"), X2, A.add)
         if not last:
             for s in range(4):
-                mm(v("B3", 128 * s, 128 * s + 128), sel(s, "Rf"), v("NP", 0, 128))
-            act(v("V"), v("B3"), AF.Copy)
+                mm(v("B1", 128 * s, 128 * s + 128), sel(s, "Rf"), v("NP", 0, 128))
+            act(v("V"), v("B1"), AF.Copy)
+            if "early" in ROWS:
+                row("gather")
             cp(ind("P", v("su")), v("V"))
+            if "early" in ROWS:
+                row("pass")
         else:
             cp(ind("P", v("su", 0, 8)), v("NP", 0, 128))
-        mm(v("B1", 0, 128), v("ONf"), v("NP", 0, 128))
-        act(v("D", 128, 256), v("B1", 0, 128), AF.Copy)
-        send_changes(2 * t)
-        act(v("SG", 0, 64), ind("K", v("og")))
-        act(v("SG", 64, 128), ind("P", v("og")))
+        mm(v("B4", 256, 384), v("ONf"), v("NP", 0, 128))
         ts(v("o1", 0, 4), v("JL", 0, 4), v("NN", 3, 4), A.is_lt, v("NN", 4, 5), A.mult)
         ts(v("o1", 4, 8), v("JL", 0, 4), v("NN", 3, 4), A.is_lt, v("NN", 5, 6), A.mult)
         if last:
-            act(v("D", DH + 264, DH + 265), n_(t + 1), AF.Copy)
-            tt(v("i3", 0, 8), v("o1", 0, 8), v("C", 112, 120), A.add)
-            tt(v("t2", 0, 64), v("SG", 0, 64), v("mk"), A.mult)
-            tt(v("t2", 64, 128), v("SG", 64, 128), v("mk"), A.mult)
-            mm(v("B2", 0, 128), v("Ff"), v("t2"))
-            own_columns(v("D", DH + 256, DH + 264), 8, C(4), C(7))
-            cp(v("SG"), v("B2", 0, 128))
-        else:
-            tt(v("D", DH + 256, DH + 264), v("o1", 0, 8), v("C", 112, 120), A.add)
-            cp(v("so"), v("D", DH + 256, DH + 264))
-            by_pointer(t + 1)
+            act(v("D", 144, DH), v("B4", 256, 384), AF.Copy)
+            z, zp = 80 * rank, 320 + 64 * rank
+            act(v("Z", z + 72, z + 73), n_(t + 1), AF.Copy)
+            tt(v("j3", 64, 72), v("o1", 0, 8), v("C", 112, 120), A.add)
+            own_columns(v("Z", z + 64, z + 72), 8, C(4), C(7), 64)
+            tt(v("Z", z, z + 64), ind("K", v("og")), v("SG", 128, 192), A.mult)
+            tt(v("Z", zp, zp + 64), ind("P", v("og")), v("SG", 128, 192), A.mult)
+            for c0, w, sem in ((0, 80, "aX5"), (320, 64, "aX6")):
+                x = v("Z", c0 + w * rank, c0 + w * rank + w)
+                fused([([T.cores[d] for d in others], off, sem, x, x[0])])
+                arrive(sem, len(others) * len(off), [v("Z", c0 + w * d, c0 + w * d + w) for d in others])
+            send_changes(4, "sa", "XM", 144, DH, "aX7")
+            send_lanes()
+            store_lanes()
+            return
+        act(v("D", 128, 256), v("B4", 256, 384), AF.Copy)
+        send_changes(2 * t)
+        act(v("SG", 0, 64), ind("K", v("og")))
+        act(v("SG", 64, 128), ind("P", v("og")))
+        tt(v("D", DH + 256, DH + 264), v("o1", 0, 8), v("C", 112, 120), A.add)
+        cp(v("so"), v("D", DH + 256, DH + 264))
+        by_pointer(t + 1)
         act(v("t1", 0, 64), v("SG", 0, 64), AF.Identity, num(1.0))
         ts(v("i1", 0, 64), v("SG", 0, 64), 0.0, A.max)
+        split(v("SG", 0, 64), v("SG", 64, 128))
+        send_changes(2 * t + 1)
+
+    def split(k, p):
         ts(v("i2", 0, 64), v("i1", 0, 64), 12, A.arith_shift_right, 1, A.bitwise_and)
         tt(v("t3", 0, 64), v("t1", 0, 64), v("i2", 0, 64), A.mult)
-        tt(v("D", DH, DH + 64), v("SG", 0, 64), v("t3", 0, 64), A.subtract)
+        tt(v("D", DH, DH + 64), k, v("t3", 0, 64), A.subtract)
         act(v("D", DH + 64, DH + 128), v("t3", 0, 64), AF.Identity, num(-1.0))
-        tt(v("NP", 192, 256), v("SG", 64, 128), v("i2", 0, 64), A.mult)
-        tt(v("NP", 128, 192), v("SG", 64, 128), v("NP", 192, 256), A.subtract)
-        mm(v("B1", 0, 128), v("ONf"), v("NP", 128, 256))
-        act(v("D", DH + 128, DH + 256), v("B1", 0, 128), AF.Copy)
-        send_changes(2 * t + 1, "sa" if last else "s")
-        if last:
-            take_changes(2 * t)
-            store_lanes()
-            take_changes(2 * t + 1, "sa")
-        else:
-            take_changes(2 * t)
-            take_changes(2 * t + 1)
+        tt(v("NP", 192, 256), p, v("i2", 0, 64), A.mult)
+        tt(v("NP", 128, 192), p, v("NP", 192, 256), A.subtract)
+        mm(v("B4", 384, 512), v("ONf"), v("NP", 128, 256))
+        act(v("D", DH + 128, DH + 256), v("B4", 384, 512), AF.Copy)
 
-    cp(v("inv"), v("IO"))
-    for r in range(16):
-        ts(sel(r), v("inv"), C(16 + r), A.is_equal)
-    tt(sel(0, "FE"), times(1.0), v("t2"), A.subtract)
-    act(sel(1, "FE"), sel(0, "FE"), AF.Identity, None, BIG)
-    act(sel(2, "FE"), v("ONb"), AF.Identity, None, -1.0)
-    ts(v("t3"), v("IO"), C(0), A.is_equal, 256.0, A.mult)
-    tt(v("UB"), v("t3"), v("t2"), A.add)
+    tt(sel(0, "FE"), times(1.0), v("G", 128, 256), A.subtract)
+    ts(sel(1, "FE"), sel(0, "FE"), BIG, A.mult)
+    ts(sel(2, "FE"), v("ONb"), -1.0, A.mult)
+    ts(v("G", 256, 384), times(1.0), 256.0, A.mult)
+    tt(v("UB"), v("G", 256, 384), v("G", 128, 256), A.add)
     ts(v("Ff"), v("B32"), C(3), A.is_equal)
     ts(v("DG"), v("B16"), C(2), A.is_equal)
     ts(v("RS"), v("B16"), 0.5, A.is_gt)
     ts(v("JL", 0, 8), v("IO", 0, 8), 16.0, A.mult, C(2), A.add)
-    act(v("k4"), v("LK", 0, 192), AF.Identity, num(4096.0)) if False else ts(v("k4"), v("LK", 0, 192), 4096.0, A.add)
-    cp(IM, v("LK", 192, 384))
+    act(v("MT", 0, 384), v("LK"), AF.Copy)
+    for a in range(2):
+        for s in range(4):
+            for b in range(4):
+                mm(v("B%d" % (7 - a), 48 * b, 48 * b + 48, 1, 32 * s, 32 * s + 32), v("V", 32 * b, 32 * b + 32),
+                   v("MT", 96 * s + 48 * a, 96 * s + 48 * a + 48))
+            join(4)
+    ts(v("k4"), v("B7", 0, 192), 4096.0, A.add)
+    cp(IM, v("B6", 0, 192))
     cp(n_(0), v("PI", 8, 9))
     ms(v("KR", 768, 776), 0)
     ms(v("CR", 768, 776), 0.0)
     address(0)
     repeat("KR", "k4")
+    x = 0
+    for j in (3, 0, 1, 2):
+        src = (rank - 1 - j) % N
+        for h in ((1,) if j == 3 else (0, 1)):
+            c0 = 512 * j + 256 * h
+            if j == 3:
+                hi_, lo_ = v("EQb", c0, c0 + 256), v("LH", c0, c0 + 256)
+            else:
+                hi_, lo_ = v("M", c0, c0 + 256), v("LH", 2048 + c0, 2304 + c0)
+            for y in range(2):
+                b = "B%d" % (1 + x % 4)
+                for z in range(2):
+                    mms(v(b, 256 * z, 256 * z + 256), [(sel(2 * y + z, "Qb"), hi_), (sel(2 * y + z, "Qh"), lo_)])
+                to = v("K", piece_cols(src, h) + 512 * y, piece_cols(src, h) + 512 * y + 512)
+                if x % 2 == 0:
+                    act(to, v(b), AF.Copy)
+                else:
+                    cp(to, v(b))
+                x += 1
     by_pointer(0)
-    for x in range(4):
-        act(v("SRf", 512 * x, 512 * x + 512), v("SRb", 512 * x, 512 * x + 512), AF.Copy)
-    sn, sm = newsem(), newsem()
-    for a, m in enumerate(("MK", "MS")):
-        for h in range(2):
-            c0 = 512 * a + 256 * h
-            dma("s", blk(m, 1024 * h, 1024 * h + 1024, rank), v("EQ", c0, c0 + 256), sn)
-    for a, m in enumerate(("MS", "MK")):
-        for j, d in enumerate(others):
-            for h in range(2):
-                c0 = (4 * j + 2 * (1 - a) + h) * 256
-                dma("s", blk(m, 1024 * h, 1024 * h + 1024, d), v("VAL", c0, c0 + 256), sm, v("VAL", 0, 1) if a + j + h == 0 else None)
-    arrive("aD", 6, [slot("DD", d) for d in others], 42.0)
+    for m, src in (("MS", T.tp), ("MK", T.tk)):
+        dma("s", v("SI"), ext(src[:, :]))
+        for x in range(4):
+            act(v(m, 512 * x, 512 * x + 512), v("SI", 512 * x, 512 * x + 512), AF.Copy)
+    own_sums(0, 4)
     for d in others:
         dma("s", blk("DK", 0, 576, d), slot("DD", d), sdk)
     act(v("IDf"), times(1.0), AF.Copy)
-    act(v("KP"), v("IO"), AF.Identity, None, 1.0)
-    ts(v("KP"), v("KP"), 256.0, A.add)
+    ts(v("A16"), v("IO"), 256.0, A.add)
     ms(v("t2"), 0.5)
     ms(v("t3"), 0.0)
     scan(v("THR"), v("t2"), v("t3"), 2.0 ** 64, A.mult, A.add)
@@ -880,23 +985,24 @@ def rank_program(g, core, T, topo):
     ms(v("CF", 0, 192), 4096.0)
     ts(C(106), C(2), 0.0, A.is_equal, -BIG, A.mult)
     ts(C(107), C(2), 1.0, A.is_equal, -4096.0, A.mult)
-    ts(v("CF", 192, 320), v("RG", 1, 129), C(106), A.mult, C(107), A.add)
-    for m, c0 in (("K", 8192), ("P", 8192), ("MK", 2048), ("MS", 2048)):
-        for c in range(c0, SCRATCH[m][1][1], 128):
-            act(v(m, c, c + 128), v("IO"), AF.Relu, None, -1.0)
+    tt(C(106), C(106), C(107), A.add)
+    act(v("CF", 192, 320), v("IO"), AF.Identity, C(106), 0.0)
     ms(v("EE", 96, 112), 256.0)
     ms(v("S2", 0, 1), 0.0)
     ms(v("S2", 1537, 1552), 0.0)
     ms(v("M", 1536, 1552), 0.0)
+    ms(v("Z", 80 * rank + 72, 80 * rank + 80), 0.0)
     ms(v("D", 264, DH), 0.0)
     ms(v("D", DH + 264, 2 * DH), 0.0)
     for x in range(RO):
         act(v("D1", 192 * x, 192 * x + 192), v("DK", 192 * x, 192 * x + 192), AF.Identity, num(4096.0))
-    ne = len(topo.engines(near[0], core))
-    arrive("aK", 8 * ne, [v("K", 0, 8192)], 28.0)
-    arrive("aP", 8 * ne, [v("P", 0, 8192)], 37.0)
     for t in range(RO):
         look_up(t)
+        if t == RO - 1:
+            patch(0, 2)
+            patch(2, 4)
         round_(t)
+        if t == 0:
+            own_sums(4, 8)
     finish()
     emit(g, T, ops)

import numpy as np
from concourse.bass import DstId, RemoteDMATransfer
from concourse.mybir import dt, AluOpType, AxisListType, ActivationFunctionType

A = AluOpType
AF = ActivationFunctionType
N, J, CAP, RO = 4, 3072, 896, 3
WT = 8704
WM = 2176
DH = 272
BIG = 2.0 ** 21
WAKE = 0.14
COST = [0.00092, 0.08, 0.02, 0.00046]
ROWS = ["gather", "pass", "early"]
CATAT = 1
DIRECT = 2
AT = [10.5, 12.5, 1.7, 24.0, 27.0, 19.5]
PASSES = 3000
SHAKE = [0, 6.0]
KEPT = {}
F, B, I, U, H = "float32", "bfloat16", "int32", "uint16", "float16"


def sb(n, d=F):
    return ("sbuf", [128, n], d)


SCRATCH = {
    "K": sb(WT, I), "P": sb(WT, I), "MK": sb(WM), "MS": sb(WM), "SI": sb(2048, I), "Qh": sb(512, H), "Qb": sb(512, B),
    "VAL": sb(3072), "LH": sb(3584, H), "EQb": sb(3072, B), "KB": sb(3072, I), "KR": sb(776, I), "CR": sb(776),
    "LS": sb(288, I), "DS": sb(432, I), "LK": sb(384, I), "DK": sb(576, I), "D1": sb(576),
    "SBb": sb(1152, B), "SBh": sb(1152, H), "SRf": sb(2048), "SRb": sb(2048, B),
    "IO": sb(128), "A16": sb(128), "B16": sb(128), "B32": sb(128), "PI": sb(16, I),
    "C": sb(128), "ONb": sb(128, B), "ONf": sb(128), "UP": sb(128, B), "IDf": sb(128), "IDh": sb(128, H),
    "II": sb(1024, B), "UB": sb(128, B), "FE": sb(384, B), "Rb": sb(512, B), "Rf": sb(512), "Ff": sb(128), "DG": sb(128),
    "RS": sb(128), "THR": sb(128), "RG": sb(768, B), "RU": sb(768, B), "TL": sb(32), "JL": sb(8), "CF": sb(320, B),
    "TK": sb(128), "WCs": sb(128), "t1": sb(128), "t2": sb(128), "t3": sb(128),
    "NN": sb(24), "k4": sb(192, I), "hb": sb(192, I), "home": sb(192, I), "tg": sb(192, I),
    "t0": sb(192, I), "tob": sb(192, B), "old": sb(192, B), "new": sb(384, B), "Wb": sb(192, B),
    "MA": sb(768, B), "M": sb(1552, B), "S": sb(768, B), "WA": sb(768, B), "WTb": sb(768, B),
    "hi": sb(384, B), "lo": sb(384, H), "w1": sb(192), "w2": sb(192), "zz": sb(192), "cc": sb(192),
    "pos": sb(192, U), "cat": sb(192, B), "S2": sb(1552, B), "CM": sb(768, B), "UU": sb(768, B), "EE": sb(112, B),
    "ou": sb(8, U), "OG": sb(16, U), "g8": sb(16), "G": sb(384, B), "MT": sb(512), "V": sb(512), "mq": sb(128),
    "Vc": sb(256), "i1": sb(128, I), "i2": sb(128, I), "i3": sb(144, I), "cls": sb(128), "cu": sb(8, U),
    "E": sb(1024, B), "inv": sb(128, B), "fst": sb(128, B), "KG": sb(128), "PG": sb(128), "Em": sb(128, B),
    "r0": sb(128), "w0": sb(128), "tz": sb(192, I), "j3": sb(136, I), "p1": sb(144), "NP": sb(256),
    "su": sb(32, U), "og": sb(4, U), "so": sb(8, U), "SG": sb(192),
    "D": sb(2 * DH), "DL": sb(5 * DH), "du": sb(48, U), "o1": sb(16), "o2": sb(24), "Z": sb(576),
    "DD": ("dram", [4, 128, 144], I), "HL": ("dram", [3, 128, 256], I),
    "XS": ("dram", [32, 128, 68], F), "XK": ("dram", [8, 128, 36], F), "XM": ("dram", [8, 128, 32], F),
    "OS": ("dram", [8, 128, 96], F),
}
for _i in range(8):
    SCRATCH["B%d" % _i] = ("psum", [128, 512], F)

SEMAPHORES = (["qv", "qa", "qp", "qg", "ls", "lsA", "lsB", "lsL", "aL", "aD", "aK", "aK0", "aK1", "aK2", "aP", "aO", "fin", "fo", "fk", "fs"]
              + ["aX%d" % i for i in range(8)] + ["h%d" % i for i in range(3)] + ["hr%d" % i for i in range(3)]
              + ["d%d" % i for i in range(70)])


def overlap(a, b):
    return a[0] == b[0] and a[1] < b[2] and b[1] < a[2] and a[3] < b[4] and b[3] < a[4]


def arrange(ops):
    for o in ops:
        hard, every = 0, 0
        for y in o["all"]:
            hard |= y["anc"]
        for y in o["soft"]:
            every |= y["anc"]
        every |= hard
        o["dep"] = [y for y in o["all"] if not hard >> y["i"] & 1]
        o["soft"] = [y for y in o["soft"] if not every >> y["i"] & 1]
        for y in o["all"] + [y for y in o["soft"] if y["lat"] == y["c"]]:
            every |= 1 << y["i"]
        o["anc"] = every
    for o in ops:
        o["left"] = len(o["dep"]) + len(o["soft"])
        for x in o["dep"] + o["soft"]:
            x["next"].append(o)
    o_ = [o for o in ops if o["left"] == 0]
    top, left = [], {o["i"]: o["left"] for o in ops}
    while o_:
        o = o_.pop()
        top.append(o)
        for x in o["next"]:
            left[x["i"]] -= 1
            if left[x["i"]] == 0:
                o_.append(x)
    for o in reversed(top):
        o["pr"] = o["lat"] + WAKE + max([x["pr"] for x in o["next"]] + [0.0])
    free = {q: 0.0 for q in "vapgsx"}
    ready, out = [o for o in ops if o["left"] == 0], []
    for o in ready:
        o["at"] = o["t0"]
    while ready:
        first = min(ready, key=lambda o: max(o["at"], free[o["q"]]))
        q = first["q"]
        now = max(first["at"], free[q])
        cand = [o for o in ready if o["q"] == q]
        best = max([o for o in cand if o["at"] <= now + 0.02], key=lambda o: o["pr"])
        for o in cand:
            if o["pr"] > best["pr"] + best["c"] and o["at"] < now + 0.5 * best["c"] and q != "x":
                best = o
        ready.remove(best)
        st = max(best["at"], free[q])
        if q != "x":
            free[q] = st + best["c"]
        best["st"], best["end"] = st, st + best["lat"]
        out.append(best)
        for x in best["next"]:
            x["left"] -= 1
            if x["left"] == 0:
                x["at"] = max([x["t0"]] + [y["end"] + WAKE for y in x["dep"]] + [y["st"] + y["c"] + x["gap"] for y in x["soft"]])
                ready.append(x)
    for o in ops:
        o["dn"], o["sn"] = [], []
    for o in ops:
        for y in o["dep"]:
            y["dn"].append(o)
        for y in o["soft"]:
            y["sn"].append(o)

    def place(line, at, c):
        k, hi = 0, len(line)
        while k < hi:
            m = (k + hi) // 2
            if line[m][1] <= at:
                k = m + 1
            else:
                hi = m
        while k < len(line) and line[k][0] < at + c - 1e-9:
            at = max(at, line[k][1])
            k += 1
        line.insert(k, (at, at + c))
        return at

    best, span = [o["st"] for o in ops], max(o["end"] for o in ops)
    rng = np.random.default_rng(SHAKE[0])
    for n_ in range(0 if len(ops) in KEPT else PASSES):
        if n_ % 2 == 0:
            mid, wid, amp = rng.random() * span, 4.0 + 16.0 * rng.random(), SHAKE[1] * rng.random()
            key = {o["i"]: s + (amp * rng.random() if abs(s - mid) < wid else 0.0) for o, s in zip(ops, best)}
            for o in top:
                key[o["i"]] = max([key[o["i"]]] + [key[y["i"]] + 1e-6 for y in o["dep"] + o["soft"]])
            lines = {q: [] for q in free}
            for o in sorted(ops, key=lambda o: key[o["i"]]):
                at = max([o["t0"]] + [y["end"] + WAKE for y in o["dep"]] + [y["st"] + y["c"] + o["gap"] for y in o["soft"]])
                o["st"] = at if o["q"] == "x" else place(lines[o["q"]], at, o["c"])
                o["end"] = o["st"] + o["lat"]
        lines = {q: [] for q in free}
        for o in sorted(ops, key=lambda o: (-o["st"] - o["c"], -o["st"])):
            at = max([o["lat"] - o["c"]] + [x["rs"] + x["c"] + o["lat"] - o["c"] + WAKE for x in o["dn"]]
                     + [x["rs"] + x["c"] + x["gap"] for x in o["sn"]])
            o["rs"] = at if o["q"] == "x" else place(lines[o["q"]], at, o["c"])
        lines = {q: [] for q in free}
        for o in sorted(ops, key=lambda o: (-o["rs"] - o["c"], -o["rs"])):
            at = max([o["t0"]] + [y["end"] + WAKE for y in o["dep"]] + [y["st"] + y["c"] + o["gap"] for y in o["soft"]])
            o["st"] = at if o["q"] == "x" else place(lines[o["q"]], at, o["c"])
            o["end"] = o["st"] + o["lat"]
        if max(o["end"] for o in ops) <= span:
            best, span = [o["st"] for o in ops], max(o["end"] for o in ops)
    best = KEPT.setdefault(len(ops), best)
    for o, s in zip(ops, best):
        o["st"], o["end"] = s, s + o["lat"]
    return sorted(ops, key=lambda o: o["st"])


def emit(g, T, ops):
    for k, o in enumerate(ops):
        o["i"] = k
    eng = {"v": g.vector, "a": g.scalar, "p": g.tensor, "g": g, "s": g.sync}
    hist, known, cnt, total, group = {}, {q: {} for q in eng}, {}, {}, {}
    for o in ops:
        if o["sem"] is not None:
            total[o["sem"]] = total.get(o["sem"], 0) + o["n"]
            group.setdefault(o["sem"], []).append(o)
    last = {}
    for o in ops:
        q = o["q"]
        dep, soft = {}, {}
        for kind, regs in (("r", o["r"]), ("w", o["w"])):
            for r in regs:
                ps = r[0][0] == "B" and len(r[0]) == 2
                for (k2, r2, o2) in hist.get(r[0], []):
                    if o2["q"] == "p" and q == "p" and ps:
                        soft[o2["i"]] = o2
                    elif o2["sem"] is not None and o2["sem"] == o["sem"]:
                        continue
                    elif (ps and o2["q"] != q) or ((kind == "w" or k2 == "w") and overlap(r, r2)):
                        for o3 in (group[o2["sem"]] if o2["sem"] is not None else [o2]):
                            dep[o3["i"]] = o3
        if q in last and (q == "g" or (q == "s" and not o["r"] and not dep)):
            soft[last[q]["i"]] = last[q]
        if q == "a" and o["dma"]:
            if "ad" in last:
                soft[last["ad"]["i"]] = last["ad"]
            last["ad"] = o
        if q == "x":
            soft[last["g"]["i"]] = last["g"]
        for tag in o.get("row", []):
            if tag in last:
                soft[last[tag]["i"]] = last[tag]
            last[tag] = o
        last[q] = o
        o["all"], o["soft"], o["next"] = list(dep.values()), list(soft.values()), []
        for r in o["r"]:
            hist.setdefault(r[0], []).append(("r", r, o))
        for r in o["w"]:
            hist.setdefault(r[0], []).append(("w", r, o))
    for o in arrange(ops):
        q = o["q"]
        need = {}
        for o2 in o["all"]:
            s, v = o2["tok"]
            if need.get(s, (0, None))[0] < v:
                need[s] = (v, o2)
        if q != "x":
            kn = known[q]
            for s, (v, o2) in sorted(need.items(), key=lambda e: -e[1][1]["end"]):
                if kn.get(s, 0) < v:
                    eng[q].wait_ge(T.sem[s], v)
                    kn[s] = v
                    for s3, v3 in o2["clock"].items():
                        if kn.get(s3, 0) < v3:
                            kn[s3] = v3
            o["clock"] = dict(kn)
            for f in o["fs"]:
                ins = f(eng[q])
                if o["sem"] is None:
                    s = "q" + q
                    cnt[s] = cnt.get(s, 0) + 1
                    ins.then_inc(T.sem[s], 1)
                    o["tok"] = (s, cnt[s])
                else:
                    if o["dma"]:
                        ins.then_inc(T.sem[o["sem"]], 16)
                    o["tok"] = (o["sem"], total[o["sem"]])
        else:
            o["clock"] = {}
            o["tok"] = (o["sem"], total[o["sem"]])
    for s, v in list(cnt.items()) + list(total.items()):
        if known["s"].get(s, 0) < v:
            g.sync.wait_ge(T.sem[s], v)


def bits(es):
    m = 0
    for e in es:
        m |= 1 << e
    return m


def dst(topo, c):
    a = topo.addr(c)
    return DstId(rid=a[0], pnc=a[1])


def crew(T, topo, c):
    rest = [x for x in topo.cores_of(c) if x not in T.cores]
    return [x for x in rest if topo.die(x) == topo.die(c)], [x for x in rest if topo.die(x) != topo.die(c)]


def piece_cols(t, h):
    return 1024 * t if h == 0 else 4096 + 1024 * ((t - 1) % N)


def helper(g, core, T, topo):
    for r, c in enumerate(T.cores):
        near, far = crew(T, topo, c)
        n_off = len(topo.engines(c, T.cores[(r + 1) % N]))
        n_on = len(topo.engines(c, far[0])) - n_off
        if core in near[:N - 1]:
            i = near.index(core)
            jobs = [(2, "PK"[i // 2], piece_cols(r, i % 2), n_on // 2)]
            jobs += [(h, "P", piece_cols((r - 1 - i) % N, h), n_off) for h in ((0, 1) if i < DIRECT else (1, 0))]
            es = topo.engines(core, c)
            rid, pid = topo.addr(c)[0], topo.addr(c)[1]
            for (k, a, c0, n_in) in jobs:
                for x in range(4):
                    q = g.sync if x % 2 == 0 else g.scalar
                    if x < 2:
                        q.wait_ge(T.sem["h%d" % k], n_in)
                    q.dma_start(T[a][32 * x:32 * x + 32, c0:c0 + 1024], T.HL[k]).then_inc(T.sem["hr%d" % k], 16)
            for (k, a, c0, n_in) in jobs:
                g.wait_ge(T.sem["hr%d" % k], 64)
                g.remote_dma(T[a][:, c0:c0 + 1024], T[a][:, c0:c0 + 1024], T.sem["a" + a], T.sem.ls, pid, rid, bits(es))
            g.wait_ge(T.sem.ls, len(jobs) * len(es))
        if core == far[0]:
            es = topo.engines(core, T.cores[(r + 1) % N])
            for j in range(N - 1):
                to = crew(T, topo, T.cores[(r + 1 + j) % N])[0][j]
                g.wait_ge(T.sem["d%d" % j], n_on if j > 0 else n_on // 2)
                for h in ((1,) if j < DIRECT else (1, 0)):
                    c0 = (2 * j + h) * 256
                    g.remote_dma(T.HL[h], T.SI[:, c0:c0 + 256], T.sem["h%d" % h], T.sem.ls, topo.addr(to)[1],
                                 topo.addr(to)[0], bits(es))
            g.wait_ge(T.sem.ls, (2 * N - 2 - DIRECT) * n_off)


def rank_program(g, core, T, topo):
    rank = T.rank_of(core)
    if rank is None:
        helper(g, core, T, topo)
        return
    ops, nd, queued = [], [0], [0.0]
    others = [(rank + 1 + j) % N for j in range(N - 1)]
    off = topo.engines(core, T.cores[others[0]])
    near, far = crew(T, topo, core)
    on = [e for e in topo.engines(core, far[0]) if e not in off]

    def v(name, c0=0, c1=None, st=1, p0=0, p1=128):
        c1 = SCRATCH[name][1][1] if c1 is None else c1
        return (T[name][p0:p1, c0:c1:st] if st > 1 else T[name][p0:p1, c0:c1], [(name, p0, p1, c0, c1)], [],
                (c1 - c0 + st - 1) // st, "p" if SCRATCH[name][0] == "psum" else "2" if SCRATCH[name][2] in (B, H, U) else "4")

    def blk(name, c0, c1, d):
        return v(name, c0, c1, 1, 32 * d, 32 * d + 32)

    def slot(name, k, c0=None, c1=None):
        return (T[name][k] if c0 is None else T[name][k, :, c0:c1], [(name, k, k + 1, c0 or 0, c1 or 9999)], [], 64, "d")

    def ind(name, o):
        w = v(name)
        return (w[0].indirect(o[0]), w[1], o[1], 16 * o[3], "i")

    def op(q, f, outs, ins, sem=None, n=0, dma=False, t0=0.0, gap=0.0):
        r, w = [], []
        ins = [x for x in ins if isinstance(x, tuple)]
        for x in ins:
            r += x[1] + x[2]
        for x in outs:
            w += x[1]
            r += x[2]
        if q == "x":
            c = lat = 0.0
        elif dma:
            c, lat = 0.07, 2.0 + max(outs[0][3], ins[0][3]) / 500.0
            if not r and len(w) == 1:
                queued[0] += outs[0][3] / 750.0
                lat += queued[0] if queued[0] < 8.0 else 0.0
        elif sem is not None:
            c, lat = 0.8, (7.0 if sem in ("lsA", "lsB") else 3.0)
        elif q == "p":
            c = lat = max(min(64, ins[0][3]), ins[1][3]) * (4 if ins[1][4] == "4" else 1) * COST[3]
        else:
            big = [x for x in ins if x[3] > 1]
            m = max([outs[0][3]] + [x[3] for x in big])
            kinds = [x[4] for x in big]
            per = (3.8 if outs[0][4] == "i" else 1.56 if "i" in kinds else 2.0 if q == "g" else
                   0.5 if q == "v" and big and outs[0][4] == "2" and all(k == "2" for k in kinds) else
                   2.0 if len(big) == 2 and "p" not in kinds and outs[0][3] > 1 else 1.0)
            c = lat = max(64, m * per) * COST[0] + (COST[1] if q == "a" else 0.15 if q == "g" else COST[2])
        ops.append({"q": q, "fs": [f], "r": r, "w": w, "sem": sem, "n": n, "dma": dma, "i": len(ops), "c": c, "lat": lat,
                    "t0": t0, "gap": gap})

    def a_(x):
        return x[0] if isinstance(x, tuple) else x

    def ts(o, x, s1, op0, s2=None, op1=None):
        if op1 is None:
            op("v", lambda e: e.tensor_scalar(o[0], x[0], a_(s1), None, op0), [o], [x, s1])
        else:
            op("v", lambda e: e.tensor_scalar(o[0], x[0], a_(s1), a_(s2), op0, op1), [o], [x, s1, s2])

    def tt(o, x, y, op0):
        op("v", lambda e: e.tensor_tensor(o[0], x[0], y[0], op0), [o], [x, y])

    def cp(o, x):
        op("v", lambda e: e.tensor_copy(o[0], x[0]), [o], [x])

    def scan(o, x, y, init, op0, op1):
        op("v", lambda e: e.tensor_tensor_scan(o[0], x[0], y[0], init, op0, op1), [o], [x, y])

    def ms(o, c):
        op("v", lambda e: e.memset(o[0], c), [o], [])

    def act(o, x, func=AF.Identity, bias=None, scale=1.0, acc=None):
        if acc is not None:
            op("a", lambda e: e.activation(o[0], x[0], func, scale=scale, accum_out=acc[0]), [o, acc], [x])
        elif bias is None:
            op("a", lambda e: e.activation(o[0], x[0], func, scale=scale), [o], [x])
        else:
            op("a", lambda e: e.activation(o[0], x[0], func, bias=bias[0], scale=scale), [o], [x, bias])

    def mm(o, l, r, start=True, stop=True):
        op("p", lambda e: e.matmul(o[0], l[0], r[0], start, stop), [o], [l, r])

    def join(n):
        part = ops[-n:]
        del ops[-n:]
        o = dict(part[0])
        o.update({"r": sum([x["r"] for x in part], []), "w": sum([x["w"] for x in part], []), "n": sum(x["n"] for x in part),
                  "fs": sum([x["fs"] for x in part], []), "c": sum(x["c"] for x in part)})
        o["lat"] = o["c"] + part[-1]["lat"] - part[-1]["c"]
        ops.append(o)

    def row(tag):
        if tag in ROWS:
            ops[-1].setdefault("row", []).append(tag)

    def mms(o, pairs):
        for x, (l, r) in enumerate(pairs):
            mm(o, l, r, x == 0, x == len(pairs) - 1)
        join(len(pairs))

    def iota(o, pat, base=0, cm=0, fl=True):
        if fl:
            op("g", lambda e: e.iota(o[0], pat, base, cm, allow_small_or_imprecise_dtypes=True), [o], [])
        else:
            op("g", lambda e: e.iota(o[0], pat, base, cm), [o], [])

    def newsem():
        nd[0] += 1
        return "d%d" % (nd[0] - 1)

    def dma(q, o, x, sem=None, after=None):
        op(q, lambda e: e.dma_start(o[0], x[0]), [o] + ([after] if after else []), [x], sem or newsem(), 16, True)

    def ext(ap_):
        return (ap_, [], [], 64, "d")

    def fused(trs, lsem="ls"):
        trs = [(t[0] if isinstance(t[0], list) else [t[0]],) + t[1:] for t in trs]
        lst = [RemoteDMATransfer(dst_ids=[dst(topo, c) for c in cs], dma_engine_mask=bits(es), remote_sem=T.sem[rs],
                                 srcs=[x[0]], dsts=[d] * len(cs)) for (cs, es, rs, x, d) in trs]
        op("g", lambda e: e.remote_dma_fused(lst, local_sem=T.sem[lsem]), [], [t[3] for t in trs], lsem,
           sum(len(t[1]) for t in trs))

    def arrive(sem, n, outs, t0=0.0):
        op("x", None, outs, [], sem, n, False, t0, 3.0)

    third = [off[0:2], off[2:4], off[4:6]]
    rows = slice(32 * rank, 32 * rank + 32)

    def C(k):
        return v("C", k, k + 1)

    SCALES = [1.0, 0.25, -0.25, 4096.0, BIG, -BIG, -1.0, 16.0]

    def times(x):
        k = SCALES.index(x)
        return v("II", 128 * k, 128 * k + 128)

    def sel(r, name="SRb"):
        return v(name, 128 * r, 128 * r + 128)

    IM, X1, X2, W0 = v("B5", 0, 192), v("B5", 192, 384), v("B5", 384, 512), v("B5", 192, 320)
    Y1, Y2, Y3 = v("B4", 0, 128), v("B4", 128, 256), v("B4", 256, 384)
    VALP, CAT = v("B0", 0, 192), v("B3", 0, 192)
    HI, LO = v("hi", 0, 384, 2), v("lo", 0, 384, 2)

    def n_(t):
        return v("NN", 8 + t, 9 + t)

    sl = newsem()
    for j, d in enumerate(others):
        dma("s", v("LS", 96 * j, 96 * j + 48), ext(T.lk[32 * d:32 * d + 32, :]), sl)
        dma("a", v("LS", 96 * j + 48, 96 * j + 96), ext(T.li[32 * d:32 * d + 32, :]), sl)
    so_ = newsem()

    def load(q, name, src, j, h, sem=None):
        d, c0 = (others + [rank])[j], (2 * j + h) * 256
        dma(q, v(name, c0, c0 + 256), ext(src[32 * d:32 * d + 32, 1024 * h:1024 * h + 1024]), sem)

    sj = newsem()
    load("s", "KB", T.tk, 3, 0, sj)
    load("a", "SI", T.tp, 0, 1, sj)
    for name, j in (("KB", 0), ("SI", 3), ("KB", 1), ("KB", 2)):
        sj = newsem()
        for h in range(2):
            load("sa"[h], name, T.tk if name == "KB" else T.tp, j, h, sj)
    load("s", "KB", T.tk, 3, 1)
    for x, (j, h) in enumerate(((1, 1), (2, 1), (2, 0), (0, 0), (1, 0))):
        load("as"[x % 2], "SI", T.tp, j, h)
        if x == 0:
            dma("s", v("LK", 96 * rank, 96 * rank + 48), ext(T.lk[rows, :]), so_)
            dma("a", v("LK", 96 * rank + 48, 96 * rank + 96), ext(T.li[rows, :]), so_)
            for s in range(4):
                dma("sa"[s % 2], blk("PI", 8, 9, s), ext(T.pn[rows, :]), so_)
    iota(v("PI", 0, 1), [[0, 1]], 0, 1, False)
    iota(v("IO"), [[1, 128]])
    iota(v("A16"), [[16, 8], [0, 16]])
    iota(v("B16"), [[0, 8], [1, 16]])
    iota(v("B32"), [[0, 4], [1, 32]])
    fused(lsem="lsL", trs=[(T.cores[d], third[j], "aL", v("LS", 96 * j, 96 * j + 96), T.LK[:, 96 * rank:96 * rank + 96])
           for j, d in enumerate(others)])
    arrive("aL", 6, [v("LK", 96 * d, 96 * d + 96) for d in others], AT[0])
    hn, ho = len(on) // 2, len(off) // 2
    fused([(far[0], on[:hn], "d0", v("SI", 256, 512), T.SI[:, 256:512]), (near[2], on[hn:], "h2", v("KB", 1536, 1792), T.HL[2])], "lsA")
    fused([(near[h], on[hn * h:hn * h + hn], "h2", v("SI", 1536 + 256 * h, 1792 + 256 * h), T.HL[2]) for h in range(2)], "lsA")
    arrive("aK", len(topo.engines(near[0], core)), [v("K", piece_cols(rank, 0), piece_cols(rank, 0) + 1024)], AT[5])
    iota(v("RG"), [[0, 4], [1, 192]])
    cp(C(0), v("PI", 0, 1))
    ts(times(1.0), v("IO"), C(0), A.is_equal)
    for j, (c0, c1) in enumerate(((0, 512), (512, 1024), (1024, 1536), (1792, 2048))):
        x, hi_, lo_, b = v("KB", c0, c1), v("EQb", c0, c1), v("LH", c0, c1), v("B%d" % j, 0, c1 - c0)
        act(hi_, x, AF.Copy)
        mm(b, times(1.0), hi_)
        tt(lo_, x, b, A.subtract)
    for j, d in enumerate(others):
        fused([(T.cores[d], off[:ho], "aK%d" % j, v("EQb", 512 * j, 512 * j + 512), T.M[:, 512 * j:512 * j + 512]),
               (T.cores[d], off[ho:], "aK%d" % j, v("LH", 512 * j, 512 * j + 512), T.LH[:, 2048 + 512 * j:2560 + 512 * j])]
              + [(far[0], on if j < DIRECT else on[hn * h:hn * h + hn], "d%d" % j, v("SI", 512 * j + 256 * h, 512 * j + 256 * h + 256),
                  T.SI[:, 512 * j + 256 * h:512 * j + 256 * h + 256]) for h in ((1,) if j < DIRECT else (0, 1)) if j > 0], "lsA")
        arrive("aK%d" % j, len(off), [v("M", 512 * j, 512 * j + 512), v("LH", 2048 + 512 * j, 2560 + 512 * j)], AT[1] + AT[2] * j)
    for j in range(DIRECT):
        fused([(crew(T, topo, T.cores[others[j]])[0][j], off, "h0", v("SI", 512 * j, 512 * j + 256), T.HL[0])], "lsB")
    iota(v("K", 8192, WT), [[0, 512]], 0, 0, False)
    arrive("aP", 8 * len(topo.engines(near[0], core)), [v("P", 0, 8192)], AT[4])
    ts(v("PI", 1, 2), v("PI", 0, 1), 112, A.bitwise_and)
    cp(C(1), v("PI", 1, 2))
    ts(v("ONf"), v("A16"), C(1), A.is_equal)
    act(v("ONb"), v("ONf"), AF.Copy)

    def pick(o, x, r):
        op("g", lambda e: e.affine_select(o[0], x[0], [[0, 8], [1, 16]], A.is_equal, 0.0, -r, 0), [o], [x])

    for r in range(16):
        pick(sel(r), v("ONb"), r)
    sd, sdk = newsem(), newsem()
    for j, d in enumerate(others):
        dma("s", v("DS", 144 * j, 144 * j + 144), ext(T.dk[32 * d:32 * d + 32, :]), sd, v("LH", j, j + 1))
    dma("s", blk("DK", 0, 576, rank), ext(T.dk[rows, :]), sdk, v("LH", 3, 4))
    fused([(T.cores[d], third[j], "aD", v("DS", 144 * j, 144 * j + 144), T.DD[rank]) for j, d in enumerate(others)])
    arrive("aD", 6, [slot("DD", d) for d in others], AT[3])
    iota(v("P", 8192, WT), [[0, 512]], 0, 0, False)
    for r in range(16):
        pick(sel(r, "SRf"), v("ONf"), r)
    iota(v("RU"), [[0, 8], [1, 96]])
    iota(v("MK", 2048, WM), [[0, 128]])
    iota(v("MS", 2048, WM), [[0, 128]])

    ts(v("PI", 2, 3), v("PI", 0, 1), 15, A.bitwise_and)
    ts(v("PI", 3, 4), v("PI", 0, 1), 31, A.bitwise_and)
    ts(v("PI", 4, 5), v("PI", 0, 1), 5, A.arith_shift_right)
    NUMS = {-1.0: 8, -float(4096 + CAP): 9, -2048.0: 10, 2048.0: 11, 2.0 ** 66: 14, 1.0: 15, -0.0625: 52, -8192.0: 53,
            -4160.0: 54, 2049.0 - BIG: 55, -4096.0: 104, 4096.0: 105}

    def num(x):
        return C(NUMS[x])

    for x in NUMS:
        ms(num(x), x)
    ts(v("PI", 5, 6), v("PI", 4, 5), 3.0, A.add)
    cp(v("C", 2, 5), v("PI", 2, 5))
    ts(v("C", 32, 48), v("IO", 0, 16), -1.0, A.mult, C(0), A.add)
    ts(v("C", 48, 52), v("IO", 0, 4), -32.0, A.mult, C(0), A.add)
    ts(v("PI", 5, 6), v("PI", 5, 6), 3, A.bitwise_and)
    ts(C(5), C(4), 1.0, A.add, -0.0625, A.mult)
    ts(C(6), v("PI", 5, 6), 5.0, A.add, -0.0625, A.mult)
    ts(C(7), v("PI", 5, 6), 4.0, A.add)
    ts(v("G", 0, 128), v("B16"), C(2), A.is_lt)
    ts(v("G", 128, 256), v("B16"), C(2), A.is_gt)
    for x in SCALES[1:]:
        ts(times(x), times(1.0), x, A.mult)
    cp(v("IDh"), times(1.0))
    tt(v("G", 0, 128), v("G", 0, 128), v("ONb"), A.mult)
    tt(v("G", 128, 256), v("G", 128, 256), v("ONb"), A.mult)
    cp(v("inv"), v("A16"))
    tt(v("UP"), times(4096.0), v("G", 0, 128), A.subtract)
    for r in range(8):
        ts(sel(r, "SBb"), v("inv"), C(32 + r), A.is_equal)
    ts(sel(8, "SBb"), v("IO"), C(40), A.is_equal)
    cp(v("SBh"), v("SBb"))
    ts(v("SBb", 0, 1024), v("SBb", 0, 1024), 4096.0, A.mult)
    for s in range(4):
        ts(sel(s, "Rf"), v("B32"), C(48 + s), A.is_equal)
    act(v("Rb"), v("Rf"), AF.Copy)
    ts(v("t3"), v("B32"), 4.0, A.mult)
    for b in range(4):
        ts(sel(b, "Qb"), v("t3"), C(32 + b), A.is_equal)
        ts(v("V", 32 * b, 32 * b + 32), v("t3", 0, 32), C(32 + b), A.is_equal)
    cp(v("Qh"), v("Qb"))

    def address(t):
        ts(v("home"), v("k4"), 4095, A.bitwise_and)
        ts(v("tg"), v("k4"), 12, A.arith_shift_right)
        ts(v("hb"), v("k4"), 8191, A.bitwise_and)
        act(LO, v("home"), AF.Identity, num(-2048.0))
        act(HI, v("tg"), AF.Copy)
        ts(v("new", 0, 192), v("hb"), n_(max(t - 1, 0)), A.is_lt)
        mms(v("B6", 0, 192), [(v("IDh"), LO), (times(4096.0), v("new", 0, 192))])
        act(v("pos"), v("B6", 0, 192), AF.Identity, num(2048.0))
        mm(v("B7", 0, 192), sel(8, "SBb"), HI)
        mm(v("B7", 192, 384), sel(8, "SBh"), LO)
        act(v("hi", 1, 384, 2), v("B7", 0, 192), AF.Copy)
        act(v("lo", 1, 384, 2), v("B7", 192, 384), AF.Copy)
        ts(v("t0"), v("k4"), 10, A.arith_shift_right, 3, A.bitwise_and)
        tt(X1, v("hb"), IM, A.is_lt)
        tt(v("tz"), v("t0"), X1, A.add)
        act(v("old"), X1, AF.Copy)
        ts(v("t0"), v("tz"), 3, A.bitwise_and)
        act(v("tob"), v("t0"), AF.Identity, num(-0.0625), -0.0625)
        for d in range(4):
            ts(v("MA", 192 * d, 192 * d + 192), v("tob"), -(d + 1) / 16.0, A.is_equal)
        scan(v("S"), v("RG"), v("MA"), 0.0, A.min, A.add)
        for h in range(2):
            b = v("B0", 0, 384)
            mms(b, [(v("ONb"), v("S", 384 * h, 384 * h + 384)), (v("UP"), v("MA", 384 * h, 384 * h + 384))])
            act(v("WA", 384 * h, 384 * h + 384), b, AF.Relu, num(-float(4096 + CAP)))
        mms(v("B0", 0, 192), [(times(BIG), v("WA", 192 * d, 192 * d + 192)) for d in range(4)])
        act(v("Wb"), v("B0", 0, 192), AF.Copy)
        tt(v("w1"), v("k4"), v("B0", 0, 192), A.min)

    def repeat(name, x):
        s1 = newsem()
        for t in range(4):
            for s in range(4):
                dma("s", blk(name, 192 * s, 192 * s + 192, t), blk(x, 0, 192, s), s1)
        join(16)

    def by_pointer(t):
        new = v("new", 0, 192) if t == 0 else v("new", 192, 384)
        if t > 0:
            ts(new, v("hb"), n_(t), A.is_lt)
        mms(v("B1", 0, 192), [(v("IDh"), LO), (times(4096.0), new)])
        act(v("cc"), v("B1", 0, 192), AF.Identity, num(2048.0))
        repeat("CR", "cc")
        mms(v("B1", 192, 384), [(v("IDh"), LO), (times(BIG), new), (times(-BIG), v("old")), (times(-1.0), v("Wb"))])
        act(v("zz"), v("B1", 192, 384), AF.Identity, num(2049.0 - BIG))
        tt(IM, v("zz"), IM, A.max)
        ts(v("og"), v("JL", 0, 4), n_(t), A.add, 4095.0, A.min)
        act(v("NN", 4, 5), n_(t), AF.Identity, num(-8192.0))
        act(v("NN", 5, 6), n_(t), AF.Identity, num(-4160.0))
        if t == RO - 1:
            ts(v("i3", 0, 64), v("IO", 0, 64), n_(t), A.add, 4095.0, A.min)
            ts(v("i3", 0, 64), v("i3", 0, 64), 10, A.arith_shift_right)
            ts(v("SG", 128, 192), v("i3", 0, 64), C(4), A.is_equal)

    def look_up(t):
        new = v("new", 0, 192) if t == 0 else v("new", 192, 384)
        mm(CAT, times(1.0), v("tob"), True, False)
        for c in range(3):
            for h in range(2 * c, 2 * c + 2):
                b, x = ("B6", "B7", "B2")[h % 3], v("KB", 512 * h, 512 * h + 512)
                for r in range(8):
                    mms(v(b, r, 512, 8), [(sel(r, "SBb"), v("hi", 64 * h, 64 * h + 64)), (sel(r, "SBh"), v("lo", 64 * h, 64 * h + 64))])
                    if r % 4 == 3:
                        join(4)
                act(x, ind("K", v("pos", 32 * h, 32 * h + 32)), AF.Identity, num(2048.0))
                row("gather")
                tt(v("EQb", 512 * h, 512 * h + 512), x, v(b), A.is_equal)
                row("pass")
            if c == 2:
                mm(CAT, times(0.25), v("old"), False, False)
                mm(CAT, times(1.0), v("Wb"), False, False)
                mm(CAT, times(-0.25), new, False, False)
            for r in range(16):
                mm(v("B3", 64 * c, 64 * c + 64), sel(r), v("EQb", 1024 * c + r, 1024 * c + 1024, 16), False, c == 2 and r == 15)
                if r % 8 == 7:
                    join(8)
        if t > 0:
            cp(ind("K", v("so")), v("D", DH, DH + 128))
        mm(VALP, times(1.0), v("CF", 0, 192), True, False)
        for c in range(3):
            for h in range(2 * c, 2 * c + 2):
                b, x = v("B%d" % (6 + h % 2)), v("VAL", 512 * h, 512 * h + 512)
                if h == CATAT:
                    act(v("cat"), CAT, AF.Copy)
                    row("gather")
                act(x, ind("P", v("pos", 32 * h, 32 * h + 32)))
                row("gather")
                mm(b, times(1.0), v("EQb", 512 * h, 512 * h + 512))
                tt(x, x, b, A.mult)
                row("pass")
            if c == 2:
                mm(VALP, times(-1.0), v("Wb"), False, False)
            for r in range(16):
                mm(v("B0", 64 * c, 64 * c + 64), sel(r, "SRf"), v("VAL", 1024 * c + r, 1024 * c + 1024, 16), False, c == 2 and r == 15)
                if r % 2 == 1:
                    join(2)
        if t > 0:
            cp(ind("P", v("so")), v("NP", 128, 256))

    def new_keys(t):
        act(X1, v("cat"), AF.Relu, None, 4 * BIG)
        tt(X1, v("D1", 192 * t, 192 * t + 192), X1, A.subtract)
        tt(v("w2"), v("w1"), X1, A.max)
        tt(v("k4"), v("w2"), VALP, A.max)

    def send_lanes():
        act(v("w2"), v("k4"), AF.Identity, num(-4096.0))
        act(v("w1"), IM, AF.Copy)
        s1 = newsem()
        for d in others:
            dma("s", slot("OS", d, 0, 48), blk("w2", 0, 192, d), s1)
            dma("s", slot("OS", d, 48, 96), blk("w1", 0, 192, d), s1)
        dma("s", ext(T.yl[rows, :]), blk("w2", 0, 192, rank), "fo")
        dma("s", ext(T.yi[rows, :]), blk("w1", 0, 192, rank), "fo")
        fused([(T.cores[d], third[j], "aO", slot("OS", d), T.OS[4 + rank]) for j, d in enumerate(others)])
        arrive("aO", 6, [slot("OS", 4 + d) for d in others])

    def store_lanes():
        for d in others:
            dma("s", ext(T.yl[32 * d:32 * d + 32, :]), slot("OS", 4 + d, 0, 48), "fin")
            dma("s", ext(T.yi[32 * d:32 * d + 32, :]), slot("OS", 4 + d, 48, 96), "fin")

    def send_changes(k, q="s", name="XS", c0=0, c1=DH, sem=None):
        a, b, x = DH * (k % 2), DH * k, 8 * (k % 4)
        s1, s2, sem = newsem(), newsem(), sem or "aX%d" % k
        for j, d in enumerate(others):
            dma(q[j % len(q)], slot(name, x + d), blk("D", a + c0, a + c1, d), s1)
        dma("s", blk("DL", b + c0, b + c1, rank), blk("D", a + c0, a + c1, rank), s2)
        fused([(T.cores[d], third[j], sem, slot(name, x + d), T[name][x + 4 + rank]) for j, d in enumerate(others)])
        arrive(sem, 6, [slot(name, x + 4 + d) for d in others])
        for j, d in enumerate(others):
            dma("s", blk("DL", b + c0, b + c1, d), slot(name, x + 4 + d), s2)

    def own_columns(o, n, ta, tb, z=0):
        hi_, lo_ = v("j3", 16 + z, 16 + z + n), v("j3", 32 + z, 32 + z + n)
        p = [v("p1", 16 * x + z, 16 * x + z + n) for x in range(4)]
        ts(hi_, v("j3", z, z + n), 10, A.arith_shift_right)
        ts(lo_, v("j3", z, z + n), 1023, A.bitwise_and)
        ts(p[0], hi_, ta, A.is_equal)
        ts(p[1], hi_, tb, A.is_equal)
        ts(p[3], hi_, tb, A.is_equal, 1024.0, A.mult)
        tt(p[2], lo_, v("C", 64, 64 + n), A.subtract)
        tt(p[0], p[0], p[1], A.add)
        tt(p[3], p[3], v("C", 64, 64 + n), A.add)
        tt(p[2], p[2], p[0], A.mult)
        tt(o, p[2], p[3], A.add)

    def patch(k0, k1):
        for k in range(k0, k1):
            cp(v("j3", 8 * (k - k0), 8 * (k - k0) + 8), v("DL", DH * k + 256, DH * k + 264))
        n = 8 * (k1 - k0)
        own_columns(v("o2", 0, n), n, float(rank), float(4 + (rank - 1) % N))
        cp(v("du", 8 * k0, 8 * k1), v("o2", 0, n))
        for k in range(k0, k1):
            cp(ind("MK", v("du", 8 * k, 8 * k + 8)), v("DL", DH * k, DH * k + 128))
            cp(ind("MS", v("du", 8 * k, 8 * k + 8)), v("DL", DH * k + 128, DH * k + 256))

    def own_sums(x0, x1):
        for x in range(x0, x1):
            mm(v("B4", 0, 256), v("ONf"), v("MS", 256 * x, 256 * x + 256))
            act(v("MS", 256 * x, 256 * x + 256), v("B4", 0, 256), AF.Copy)

    def finish():
        c0 = 4 * DH
        cp(v("du", 32, 40), v("DL", c0 + 128, c0 + 136))
        cp(ind("MK", v("du", 32, 40)), v("DL", c0, c0 + 128))
        for w in [rank] + others:
            mm(blk("B1", 0, 64, w), v("Ff", 32 * w, 32 * w + 32), v("Z", 80 * w, 80 * w + 64))
        for w in [rank] + others:
            mm(blk("B2", 0, 9, w), v("Rf", 128 * rank + 32 * w, 128 * rank + 32 * w + 32), v("Z", 80 * w + 64, 80 * w + 73))
        for w in [rank] + others:
            mm(blk("B3", 0, 64, w), v("Ff", 32 * w, 32 * w + 32), v("Z", 320 + 64 * w, 384 + 64 * w))
        ts(v("i1", 0, 64), v("B1", 0, 64), 0.0, A.max)
        ts(v("t1", 0, 64), v("B1", 0, 64), 1.0, A.add)
        cp(v("du", 40, 48), v("B2", 0, 8))
        act(v("NN", 16, 17), v("B2", 8, 9), AF.Copy)
        split(v("B1", 0, 64), v("B3", 0, 64))
        cp(ind("MK", v("du", 40, 48)), v("D", DH, DH + 128))
        dma("s", ext(T.yk[:, 0:1024]), v("MK", 0, 1024), "fk")
        dma("a", ext(T.yk[:, 1024:2048]), v("MK", 1024, 2048), "fk")
        dma("s", ext(T.yn[:, :]), v("NN", 16, 17), "fk")
        cp(ind("MS", v("du", 32, 40)), v("DL", c0 + 144, c0 + DH))
        cp(ind("MS", v("du", 40, 48)), v("D", DH + 128, DH + 256))
        for x in range(8):
            dma("sa"[x % 2], ext(T.ys[x:x + 1, :]), v("MS", 0, 2048, 1, 16 * x, 16 * x + 1), "fs")

    def round_(t):
        last = t == RO - 1
        if CATAT > 5:
            act(v("cat"), CAT, AF.Copy)
        for s in range(4):
            mm(v("B%d" % (1 + s // 2), 192 * (s % 2), 192 * (s % 2) + 192), sel(s, "Rb"), v("cat"))
        act(v("WTb", 0, 384), v("B1", 0, 384), AF.Copy)
        act(v("WTb", 384, 768), v("B2", 0, 384), AF.Copy)
        for h in range(2):
            for k in range(2):
                ts(v("M", 768 * k + 384 * h, 768 * k + 384 * h + 384), v("WTb", 384 * h, 384 * h + 384), C(5 + k), A.is_equal)
        scan(v("S2", 1, 1537), v("M", 0, 1536), v("M", 0, 1536), 0.0, A.add, A.max)
        mm(v("B1", 384, 480), v("ONb"), v("S2", 16, 1537, 16))
        for r in range(16):
            mm(v("B2", 384, 480), sel(r), v("S2", 1 + r, 1537, 16), r == 0, r == 15)
            if r % 4 == 3:
                join(4)
        act(v("EE", 0, 96), v("B2", 384, 480), AF.Copy)
        for k in range(8):
            ts(v("CM", 96 * k, 96 * k + 96), v("B1", 384, 480), v("JL", k, k + 1), A.is_le)
        join(8)
        scan(v("UU"), v("RU"), v("CM"), 0.0, A.min, A.add)
        uu = v("UU", 95, 768, 96)
        cp(v("ou"), uu)
        tt(v("G", 0, 128), ind("EE", v("ou")), v("IO"), A.is_le)
        ts(v("g8", 0, 8), uu, 48.0, A.is_ge, -768.0, A.mult)
        mms(v("B1", 480, 488), [(times(16.0), uu)] + [(sel(r), v("G", r, 128, 16)) for r in range(16)])
        cp(v("OG", 0, 8), v("B1", 480, 488))
        tt(v("g8", 8, 16), v("g8", 0, 8), v("B1", 480, 488), A.add)
        act(v("G", 128, 256), ind("S2", v("OG", 0, 8)))
        cp(v("G", 256, 384), ind("M", v("OG", 0, 8)))
        cp(v("OG", 8, 16), v("g8", 8, 16))
        mms(v("B2", 0, 128), [(v("UB"), v("G", 256, 384)), (v("ONb"), v("G", 128, 256))])
        tt(v("mq"), v("A16"), v("B2", 0, 128), A.is_equal)
        tt(v("Vc", 0, 128), ind("CR", v("OG", 8, 16)), v("mq"), A.mult)
        COL, pk, y = v("B1", 0, 128), v("B2", 128, 256), v("B2", 256, 384)
        mm(COL, v("ONf"), v("Vc", 0, 128))
        tt(v("Vc", 128, 256), ind("KR", v("OG", 8, 16)), v("mq"), A.mult)
        new_keys(t)
        if not last:
            address(t + 1)
            repeat("KR", "k4")
        mm(pk, v("ONf"), v("Vc", 128, 256))
        tt(Y1, v("DG"), COL, A.mult)
        scan(v("cls"), v("RS"), Y1, 0.0, A.mult, A.add)
        cp(v("cu"), v("cls", 15, 128, 16))
        act(v("Em"), ind("K", v("cu")), AF.Relu, None, -1.0)
        act(v("KG"), ind("K", v("cu")))
        act(v("inv"), pk, AF.Relu, num(2.0 ** 66), -2.0 ** 66)
        act(v("i1"), pk, AF.Identity, num(-4096.0))
        mms(y, [(v("ONb"), v("CF", 192, 320)), (v("ONf"), v("Vc", 128, 256)), (sel(1, "FE"), v("Em"))])
        for c in range(8):
            ts(v("E", 144 * c, 128 * c + 128), v("B1", 16 * c, 128), v("cls", 16 * c + 15, 16 * c + 16), A.is_equal,
               v("WCs", 16 * c + 15, 16 * c + 16), A.mult)
            mm(v("B3", 16 * c, 128), v("ONb"), v("E", 144 * c, 128 * c + 128), c == 0, False)
        mm(v("B3", 0, 128), times(1.0), v("inv"), False, True)
        tt(v("D", 0, 128), v("KG"), y, A.max)
        if not last:
            for s in range(4):
                mm(v("B2", 128 * s, 128 * s + 128), sel(s, "Rf"), v("D", 0, 128))
            for h in range(2):
                act(v("MT", 256 * h, 256 * h + 256), v("B2", 256 * h, 256 * h + 256), AF.Copy)
        tt(Y2, v("TK"), Y1, A.add)
        tt(v("fst"), v("THR"), v("B3", 0, 128), A.is_gt)
        tt(Y2, v("fst"), Y2, A.mult)
        scan(v("t3"), v("RS"), Y2, 0.0, A.mult, A.add)
        if not last:
            mm(v("B1", 384, 416), v("IDf"), v("TL"), True, False)
            for s in range(4):
                mm(v("B1", 384 + 8 * s, 392 + 8 * s), sel(s, "Rf"), v("t3", 15, 128, 16), False, s == 3)
            cp(v("su"), v("B1", 384, 416))
            cp(ind("K", v("su")), v("MT"))
            tt(v("D", 256, 264), v("t3", 15, 128, 16), v("C", 56, 64), A.add)
        else:
            tt(v("o2", 16, 24), v("t3", 15, 128, 16), v("C", 56, 64), A.add)
            cp(v("su", 0, 8), v("o2", 16, 24))
            cp(ind("K", v("su", 0, 8)), v("D", 0, 128))
            cp(v("j3", 112, 120), v("cls", 15, 128, 16))
            ts(v("j3", 120, 128), v("j3", 112, 120), 1023, A.bitwise_and)
            ts(v("j3", 128, 136), v("j3", 112, 120), 12, A.arith_shift_right)
            ts(v("p1", 128, 136), v("j3", 128, 136), 1024.0, A.mult)
            tt(v("p1", 128, 136), v("p1", 128, 136), v("j3", 120, 128), A.add)
            ts(v("p1", 136, 144), v("t3", 15, 128, 16), 4096.0, A.mult)
            tt(v("p1", 136, 144), v("p1", 136, 144), v("C", 64, 72), A.add)
            tt(v("D", 128, 136), v("p1", 136, 144), v("p1", 128, 136), A.max)
            send_changes(4, "sa", "XK", 0, 144)
        mm(v("B3", 128, 256), sel(0, "FE"), v("Em"))
        mms(v("B3", 256, 384), [(sel(2, "FE"), v("Em")), (times(1.0), v("fst"))])
        act(v("w0"), v("B3", 128, 256), AF.Relu)
        act(v("r0"), v("B3", 256, 384), AF.Relu, None, 1.0, v("NN", 1, 2))
        mm(v("B3", 416, 417), v("Ff"), v("NN", 1, 2))
        ts(v("NN", 2, 3), v("B3", 416, 417), 64.0, A.min, n_(t), A.add)
        ts(n_(t + 1), v("NN", 2, 3), 4096.0, A.min)
        tt(v("NN", 3, 4), n_(t + 1), n_(t), A.subtract)
        act(v("PG"), ind("P", v("cu")))
        ts(v("i2"), v("i1"), 1023, A.bitwise_and)
        ts(v("i3", 0, 128), v("i1"), 10, A.arith_shift_right)
        act(X2, v("i2"), AF.Identity, None, 1024.0)
        tt(X2, v("i3", 0, 128), X2, A.add)
        tt(X2, X2, v("PG"), A.subtract)
        tt(X2, X2, v("w0"), A.mult)
        tt(v("NP", 0, 128), v("PG"), X2, A.add)
        if not last:
            for s in range(4):
                mm(v("B1", 128 * s, 128 * s + 128), sel(s, "Rf"), v("NP", 0, 128))
            act(v("V"), v("B1"), AF.Copy)
            if "early" in ROWS:
                row("gather")
            cp(ind("P", v("su")), v("V"))
            if "early" in ROWS:
                row("pass")
        else:
            cp(ind("P", v("su", 0, 8)), v("NP", 0, 128))
        mm(v("B4", 256, 384), v("ONf"), v("NP", 0, 128))
        ts(v("o1", 0, 4), v("JL", 0, 4), v("NN", 3, 4), A.is_lt, v("NN", 4, 5), A.mult)
        ts(v("o1", 4, 8), v("JL", 0, 4), v("NN", 3, 4), A.is_lt, v("NN", 5, 6), A.mult)
        if last:
            act(v("D", 144, DH), v("B4", 256, 384), AF.Copy)
            z, zp = 80 * rank, 320 + 64 * rank
            act(v("Z", z + 72, z + 73), n_(t + 1), AF.Copy)
            tt(v("j3", 64, 72), v("o1", 0, 8), v("C", 112, 120), A.add)
            own_columns(v("Z", z + 64, z + 72), 8, C(4), C(7), 64)
            tt(v("Z", z, z + 64), ind("K", v("og")), v("SG", 128, 192), A.mult)
            tt(v("Z", zp, zp + 64), ind("P", v("og")), v("SG", 128, 192), A.mult)
            for c0, w, sem in ((0, 80, "aX5"), (320, 64, "aX6")):
                x = v("Z", c0 + w * rank, c0 + w * rank + w)
                fused([([T.cores[d] for d in others], off, sem, x, x[0])])
                arrive(sem, len(others) * len(off), [v("Z", c0 + w * d, c0 + w * d + w) for d in others])
            send_changes(4, "sa", "XM", 144, DH, "aX7")
            send_lanes()
            store_lanes()
            return
        act(v("D", 128, 256), v("B4", 256, 384), AF.Copy)
        send_changes(2 * t)
        act(v("SG", 0, 64), ind("K", v("og")))
        act(v("SG", 64, 128), ind("P", v("og")))
        tt(v("D", DH + 256, DH + 264), v("o1", 0, 8), v("C", 112, 120), A.add)
        cp(v("so"), v("D", DH + 256, DH + 264))
        by_pointer(t + 1)
        act(v("t1", 0, 64), v("SG", 0, 64), AF.Identity, num(1.0))
        ts(v("i1", 0, 64), v("SG", 0, 64), 0.0, A.max)
        split(v("SG", 0, 64), v("SG", 64, 128))
        send_changes(2 * t + 1)

    def split(k, p):
        ts(v("i2", 0, 64), v("i1", 0, 64), 12, A.arith_shift_right, 1, A.bitwise_and)
        tt(v("t3", 0, 64), v("t1", 0, 64), v("i2", 0, 64), A.mult)
        tt(v("D", DH, DH + 64), k, v("t3", 0, 64), A.subtract)
        act(v("D", DH + 64, DH + 128), v("t3", 0, 64), AF.Identity, num(-1.0))
        tt(v("NP", 192, 256), p, v("i2", 0, 64), A.mult)
        tt(v("NP", 128, 192), p, v("NP", 192, 256), A.subtract)
        mm(v("B4", 384, 512), v("ONf"), v("NP", 128, 256))
        act(v("D", DH + 128, DH + 256), v("B4", 384, 512), AF.Copy)

    tt(sel(0, "FE"), times(1.0), v("G", 128, 256), A.subtract)
    ts(sel(1, "FE"), sel(0, "FE"), BIG, A.mult)
    ts(sel(2, "FE"), v("ONb"), -1.0, A.mult)
    ts(v("G", 256, 384), times(1.0), 256.0, A.mult)
    tt(v("UB"), v("G", 256, 384), v("G", 128, 256), A.add)
    ts(v("Ff"), v("B32"), C(3), A.is_equal)
    ts(v("DG"), v("B16"), C(2), A.is_equal)
    ts(v("RS"), v("B16"), 0.5, A.is_gt)
    ts(v("JL", 0, 8), v("IO", 0, 8), 16.0, A.mult, C(2), A.add)
    act(v("MT", 0, 384), v("LK"), AF.Copy)
    for a in range(2):
        for s in range(4):
            for b in range(4):
                mm(v("B%d" % (7 - a), 48 * b, 48 * b + 48, 1, 32 * s, 32 * s + 32), v("V", 32 * b, 32 * b + 32),
                   v("MT", 96 * s + 48 * a, 96 * s + 48 * a + 48))
            join(4)
    ts(v("k4"), v("B7", 0, 192), 4096.0, A.add)
    cp(IM, v("B6", 0, 192))
    cp(n_(0), v("PI", 8, 9))
    ms(v("KR", 768, 776), 0)
    ms(v("CR", 768, 776), 0.0)
    address(0)
    repeat("KR", "k4")
    x = 0
    for j in (3, 0, 1, 2):
        src = (rank - 1 - j) % N
        for h in ((1,) if j == 3 else (0, 1)):
            c0 = 512 * j + 256 * h
            if j == 3:
                hi_, lo_ = v("EQb", c0, c0 + 256), v("LH", c0, c0 + 256)
            else:
                hi_, lo_ = v("M", c0, c0 + 256), v("LH", 2048 + c0, 2304 + c0)
            for y in range(2):
                b = "B%d" % (1 + x % 4)
                for z in range(2):
                    mms(v(b, 256 * z, 256 * z + 256), [(sel(2 * y + z, "Qb"), hi_), (sel(2 * y + z, "Qh"), lo_)])
                to = v("K", piece_cols(src, h) + 512 * y, piece_cols(src, h) + 512 * y + 512)
                if x % 2 == 0:
                    act(to, v(b), AF.Copy)
                else:
                    cp(to, v(b))
                x += 1
    by_pointer(0)
    for m, src in (("MS", T.tp), ("MK", T.tk)):
        dma("s", v("SI"), ext(src[:, :]))
        for x in range(4):
            act(v(m, 512 * x, 512 * x + 512), v("SI", 512 * x, 512 * x + 512), AF.Copy)
    own_sums(0, 4)
    for d in others:
        dma("s", blk("DK", 0, 576, d), slot("DD", d), sdk)
    act(v("IDf"), times(1.0), AF.Copy)
    ts(v("A16"), v("IO"), 256.0, A.add)
    ms(v("t2"), 0.5)
    ms(v("t3"), 0.0)
    scan(v("THR"), v("t2"), v("t3"), 2.0 ** 64, A.mult, A.add)
    tt(v("t1"), v("THR"), v("DG"), A.mult)
    scan(v("WCs"), v("RS"), v("t1"), 0.0, A.mult, A.add)
    ts(v("THR"), v("THR"), 2.5, A.mult)
    ts(C(12), C(4), 128.0, A.mult, 8192.0, A.add)
    ts(C(13), C(2), 8192.0, A.add)
    ts(v("TK"), v("IO"), C(12), A.add, -1.0, A.mult)
    tt(v("TK"), v("TK"), v("DG"), A.mult)
    ts(v("TL"), v("IO", 0, 32), 16.0, A.mult, C(13), A.add)
    ts(v("C", 112, 120), v("JL"), 8192.0, A.add)
    ts(v("C", 56, 64), v("JL"), C(12), A.add)
    for x in range(5):
        ts(v("C", 64 + 8 * x, 72 + 8 * x), v("JL"), 2048.0, A.add)
    ms(v("CF", 0, 192), 4096.0)
    ts(C(106), C(2), 0.0, A.is_equal, -BIG, A.mult)
    ts(C(107), C(2), 1.0, A.is_equal, -4096.0, A.mult)
    tt(C(106), C(106), C(107), A.add)
    act(v("CF", 192, 320), v("IO"), AF.Identity, C(106), 0.0)
    ms(v("EE", 96, 112), 256.0)
    ms(v("S2", 0, 1), 0.0)
    ms(v("S2", 1537, 1552), 0.0)
    ms(v("M", 1536, 1552), 0.0)
    ms(v("Z", 80 * rank + 72, 80 * rank + 80), 0.0)
    ms(v("D", 264, DH), 0.0)
    ms(v("D", DH + 264, 2 * DH), 0.0)
    for x in range(RO):
        act(v("D1", 192 * x, 192 * x + 192), v("DK", 192 * x, 192 * x + 192), AF.Identity, num(4096.0))
    for t in range(RO):
        look_up(t)
        if t == RO - 1:
            patch(0, 2)
            patch(2, 4)
        round_(t)
        if t == 0:
            own_sums(4, 8)
    finish()
    emit(g, T, ops)
